import numpy as np, ml_dtypes
CORES = [5,29,101,125,133,157,229,253]
N = 8
import mx_ref
BF = ml_dtypes.bfloat16
def entries(a):
    return np.ascontiguousarray(a.T).reshape(-1)
def table(e):
    return np.ascontiguousarray(np.reshape(e, (-1, 16)).T).astype(np.int32)
def gcols(t, e):
    v = np.concatenate([t.reshape(8, 16, -1, 4), np.zeros((8, 16, 1, 4), BF)], axis=2)
    return np.ascontiguousarray(np.stack([v[g][:, e[g]] for g in range(8)])).reshape(128, -1)
def gpick(z, e):
    return np.concatenate([z[16 * g:16 * g + 16][:, e[g]] for g in range(8)])
def tile(rs):
    return np.stack(rs, axis=2).reshape(128, -1).astype(BF)
def pick(q, e):
    c = np.concatenate([q[0].reshape(128, -1, 4), np.zeros((128, 1, 4), np.uint8)], axis=1); s = np.concatenate([q[1], np.ones((16, 1), np.uint8)], axis=1)
    return (np.ascontiguousarray(c[:, e].reshape(128, -1)), np.ascontiguousarray(s[:, e]))
def join(*qs):
    return (np.concatenate([q[0] for q in qs], axis=1), np.concatenate([q[1] for q in qs], axis=1))
def put(q, e, v):
    c, s = q[0].reshape(128, -1, 4).copy(), q[1].copy(); c[:, e] = v[0].reshape(128, -1, 4); s[:, e] = v[1]
    return (c.reshape(128, -1), s)
def pk(c, s):
    return (np.ascontiguousarray(c), mx_ref.live(s))
def emit(q):
    return q[0], q[1]
def packed(v, rng):
    q = [mx_ref.quantize(np.ascontiguousarray(v[r])) for r in range(N)]
    return np.stack([a for a, b in q]), np.stack([mx_ref.plane(b, rng) for a, b in q])
def values_of_codes():
    e, c = np.zeros((128, 128, 4), np.float32), np.zeros((128, 2, 4), np.uint8)
    e[np.arange(128), np.arange(128), 0] = 1
    c[:127, :, 0] = np.arange(256).reshape(2, 128).T[:127]
    return mx_ref.matmul(mx_ref.quantize(e.reshape(128, 512).astype(BF)), (c.reshape(128, 8), np.full((16, 2), 127, np.uint8))).T.reshape(-1).astype(np.float64)
CODE_VALUE, SCALE_VALUE = values_of_codes(), 2.0 ** (np.arange(256) - 127.0)
def decode(q):
    return (CODE_VALUE[q[0]].reshape(16, 8, -1, 4) * SCALE_VALUE[q[1]][:, None, :, None] + 0.0).reshape(128, -1).astype(np.float32)
def f(rng, *shape):
    return mx_ref.flush((rng.standard_normal(shape, dtype=np.float32) * np.exp2(rng.integers(-2, 3, shape[:-1] + (1,)))).astype(BF))
def wide(rng, *shape, cols=0):
    v = rng.standard_normal(shape, dtype=np.float32) * np.exp2(rng.integers(-12, 13, shape)).astype(np.float32)
    if cols: v *= np.repeat(np.exp2(rng.integers(-cols, cols + 1, shape[:-2] + (1, shape[-1] // 4))) * (rng.random(shape[:-2] + (1, shape[-1] // 4)) > 0.0625), 4, axis=-1).astype(np.float32)
    return mx_ref.flush(v.astype(BF))
C, H, R = 448, 224, 3
WIDTH = [1, 2, 7, 14, 28, 56, 112, 224]
def big(v):
    v = v.astype(np.float32)
    v[np.abs(v) < np.float32(2.0 ** -16)] = 0
    return v.astype(BF)
def numbers_of(rng):
    return {"x": big(f(rng, N, 128, 4 * C)), "u": np.array(f(rng, N, 128, 512)), "v": np.array(f(rng, N, 128, 512))}
def bases(rng):
    return np.stack([table(rng.permutation(C)) for r in range(N)])
def layers(rng):
    return big(f(rng, N, 128, 2048)).reshape(N, 8, 16, 4, 8, 16, 4)
def weights(rng, w):
    c, s = packed(np.ascontiguousarray(w).reshape(N, 128, 2048), rng)
    return {"wc": c, "ws": s}
def setup_inputs(rng):
    return {**numbers_of(rng), "p": bases(rng), **weights(rng, layers(rng))}
def setup_inputs_ties(rng):
    d = numbers_of(rng)
    p = bases(rng)
    o = rng.permutation(N)
    x = d["x"].astype(np.float32).reshape(N, 8, 16, C, 4)
    n = (N, 8, 8, C, 4)
    x[:, :, 8:] = (1.125 + 0.25 * rng.integers(0, 4, n)) * np.exp2(-1.0 * rng.integers(8, 15, n)) * rng.choice([-1.0, 1.0], n)
    x[:, :, 8, :, 0] = 1.96875
    x[:, :, :8] = 0
    u = d["u"].reshape(N, 128, 128, 4)
    u[:, :, ::16] = 0
    for r in range(N):
        if o[r] % 2 == 1: x[r, :, 0, :, 0] = rng.integers(0, 4, (8, C))
        else: x[r, :, 0, :, 0] = rng.integers(0, 7, (1, C)) + rng.integers(0, 2, (8, C))
        for h in range(0, 128, 16): u[r, h, h, 0] = 0.0 if o[r] == 0 else -1.0 if o[r] == 1 else 1.0
        if o[r] == 0:
            x[r, 7, 0, :, 0] = 0
            x[r, 7, 0, p[r, 0, 0], 0] = 1
            u[r, 112, 112, 0] = 1.0
    w = layers(rng)
    w[:, :, :, :, :, :8] = 0
    return {"x": x.reshape(N, 128, 4 * C).astype(BF), "u": u.reshape(N, 128, 512), "v": d["v"], "p": p, **weights(rng, w)}
def setup_inputs_near(rng):
    d = numbers_of(rng)
    x = d["x"].astype(np.float32).reshape(N, 8, 16, C, 4)
    u = d["u"].reshape(N, 128, 128, 4)
    o = rng.permutation(N) % 4
    x[:, :, 0] = 0
    x[:, :, 8:] = 0
    u[:, :, ::16] = 0
    for r in range(N):
        k = 1.0 if o[r] == 0 else 2.0 ** -30
        if o[r] < 3:
            s = rng.integers(0, 252, (1, C)) + rng.integers(0, 4, (8, C))
            for i in range(2): x[r, :, 8 + i] = ((s[:, :, None] >> (4 * i + np.arange(4))) & 1) * np.exp2(4 * i + np.arange(4) - 23.0)
            if o[r] < 2:
                x[r, :, 0, :, 0] = rng.choice([-1.0, 1.0], C)
                x[r, :, 11, :, 0] = 2.0 ** -10
            for g in rng.permutation(8)[:4]: x[r, g, 0, rng.integers(C), 0] = 2.0 ** 29 * rng.choice([-1.0, 1.0])
        else:
            for i in (10, 12): x[r, :, i, :, 0] = (1.0 + 0.125 * rng.integers(0, 2, (8, C))) * 2.0 ** -30
        for h in range(0, 128, 16):
            if o[r] < 3:
                u[r, h, h, 0] = k
                u[r, h + 8:h + 10, h] = k
                u[r, h + 11, h, 0] = k
            else:
                a = rng.choice([-1.0, 1.0])
                u[r, h + 10, h, 0] = 1.125 * k * a
                u[r, h + 12, h, 0] = -k * a
    w = layers(rng)
    for i in (0, 8, 9, 10, 11, 12, 13, 14, 15):
        w[:, :, i] = 0
        w[:, :, :, :, :, i] = 0
    return {"x": x.reshape(N, 128, 4 * C).astype(BF), "u": u.reshape(N, 128, 512), "v": d["v"], "p": bases(rng), **weights(rng, w)}
def setup_inputs_huge(rng):
    d = numbers_of(rng)
    o = rng.permutation(N)
    x = 0.6 + 0.06 * rng.random((N, 8, 16, C, 4)) + 0.03 * rng.random((N, 1, 1, C, 1))
    a = 1.0 - 0.1 * rng.random((N, 128, 8, 4))
    for r in range(N):
        if o[r] < N // 2: a[r] *= -1.0
        else:
            x[r] *= rng.choice([-1.0, 1.0], (1, 1, C, 1))
            a[r] *= rng.choice([-1.0, 1.0], (1, 8, 1))
    u = d["u"].reshape(N, 128, 128, 4)
    u[:, :, ::16] = (2.0 ** 30 * a).astype(np.float32).astype(BF)
    w = np.zeros((N, 128, 4, 128, 4), np.float32)
    i = np.arange(128)
    for b in range(4): w[:, i, b, i, b] = -4
    return {"x": (2.0 ** 30 * x).astype(np.float32).reshape(N, 128, 4 * C).astype(BF), "u": u.reshape(N, 128, 512), "v": d["v"], "p": bases(rng), **weights(rng, w.astype(BF))}
def setup_inputs_ends(rng):
    v = np.array(f(rng, N, 128, 512))
    o = rng.permutation(N) % 4
    x, u = np.zeros((N, 128, C, 4), np.float32), np.zeros((N, 128, 128, 4), np.float32)
    w, e = np.zeros((N, 128, 4, 128, 4), np.float32), []
    i = np.arange(128)
    for r in range(N):
        c = rng.choice([-1.0, 1.0], (1, C, 1))
        a = rng.choice([-1.0, 1.0], (1, 128, 1))
        if o[r] == 0:
            x[r] = 2.0 ** 30
            x[r, 64:] *= rng.choice([0.5, 1.0], (64, C, 4))
            x[r, 64:, ::4] = 2.0 ** 30
            u[r] = -2.0 ** 30
            u[r, 64:, :64] = 0
        elif o[r] == 1:
            x[r] = 2.0 ** 30 * c
            u[r] = 2.0 ** 30 * a
        elif o[r] == 2:
            x[r] = 2.0 ** -29 * rng.choice([-1.0, 1.0], (128, C, 4))
            u[r] = 2.0 ** -30 * rng.choice([-1.0, 1.0], (128, 128, 4))
        else:
            x[r] = 2.0 ** -29 * c
            u[r] = 2.0 ** -30 * a
        if o[r] > 1:
            for b in range(4): w[r, i, b, i, b] = 2.0 ** -20
        e.append(table(np.arange(C) if o[r] % 2 == 0 else C - 1 - np.arange(C)))
    v = (np.where(v < 0, -1.0, 1.0) * np.where(rng.permutation(N) % 2, 2.0 ** -30, 2.0 ** 30)[:, None, None]).astype(np.float32).astype(BF)
    return {"x": x.reshape(N, 128, 4 * C).astype(BF), "u": u.reshape(N, 128, 512).astype(BF), "v": v, "p": np.stack(e), **weights(rng, w.astype(BF))}
def setup_inputs_spread(rng):
    d = setup_inputs(rng)
    d["x"] = big(wide(rng, N, 128, 4 * C, cols=6))
    return d
def check_inputs(d):
    bad = []
    for k in ("x", "u", "v"):
        a = np.abs(d[k].astype(np.float32))
        if not (np.isfinite(a).all() and ((a == 0) | (a >= 2.0 ** -30) & (a <= 2.0 ** 30)).all()): bad.append("a value of " + k)
    none, least, most = [emit(mx_ref.quantize(np.full((128, 16), k, np.float32).astype(BF)))[1][0, 0] for k in (0.0, 2.0 ** -30, 2.0 ** 30)]
    for r in range(N):
        if not np.array_equal(np.sort(d["p"][r].reshape(-1)), np.arange(C)): bad.append("p: not every column once")
        if ((d["wc"][r] == 0x7F) | (d["wc"][r] == 0xFF)).any(): bad.append("wc: a code that is no number")
        s = mx_ref.live(d["ws"][r])
        if ((s != none) & ((s < least) | (s > most))).any(): bad.append("ws: a scale out of range")
    return bad
def reference(x, u, v, p, wc, ws):
    qu = [mx_ref.quantize(u[r]) for r in range(N)]
    lay = [pk(wc[r], ws[r]) for r in range(N)]
    now = [x[r] for r in range(N)]
    base = [entries(p[r]) for r in range(N)]
    order = np.zeros((N, 8, C), np.int64)
    for t in range(R):
        own, sent = [], []
        for r in range(N):
            q = mx_ref.quantize(now[r])
            own.append(decode(q))
            s = mx_ref.matmul(qu[r], q)[::16] + np.float32(0.0)
            o = base[r]
            for g in range(8):
                key = np.maximum.accumulate(s[g][o].reshape(-1, WIDTH[g]), axis=1).reshape(-1, 2 * WIDTH[g])
                o = np.take_along_axis(o.reshape(-1, 2 * WIDTH[g]), np.argsort(key, axis=1, kind="stable"), axis=1).reshape(-1)
                order[r, g] = o
            base[r] = o
            a = own[r].astype(BF)
            z = (gcols(a, order[r, :, :H]).astype(np.float32) + gcols(a, order[r, :, H:]).astype(np.float32)) * np.float32(0.5)
            sent.append(mx_ref.quantize(z.astype(BF)))
        for r in range(N):
            q = sent[(r - 1) % N]
            place = np.argsort(order[r], axis=1) % H
            now[r] = tile([gpick(mx_ref.matmul(pick(lay[r], np.arange(128 * b, 128 * b + 128)), q), place) * np.float32(0.03125) + own[r][:, b::4] for b in range(4)])
    y, od = np.zeros((N, 128, C), np.float32), np.zeros((N, 8, C), np.float32)
    oc, osc = np.zeros((N, 128, 4 * C), np.uint8), np.zeros((N, 16, C), np.uint8)
    for r in range(N):
        q = mx_ref.quantize(now[r])
        y[r] = mx_ref.matmul(mx_ref.quantize(v[r]), q)
        od[r] = order[r]
        oc[r], osc[r] = emit(q)
    return {"y": y, "od": od, "oc": oc, "osc": osc}

@@ -1,0 +1,620 @@
+from concourse.bass import DstId, RemoteDMATransfer
+from concourse.mybir import dt, AluOpType, ActivationFunctionType
+
+OP = AluOpType
+AF = ActivationFunctionType
+ROUNDS, C, HALF = 3, 448, 224
+BIG = 1e29
+TW = 536
+
+SCRATCH = {}
+
+
+def _sb(name, n, ty="float32"):
+    SCRATCH[name] = ("sbuf", [128, n], ty)
+
+
+def _mx(c, s, n):
+    _sb(c, n, "float8_e4m3fn_x4")
+    _sb(s, n, "uint8")
+
+
+for _n, _w in (("xt", 1792), ("xn", 1792), ("ut", 512), ("vt", 512), ("one", 576), ("qtr", 576), ("eb", 516), ("cb", 576), ("cl", 2048),
+               ("G", TW), ("WQ", TW), ("W1", TW), ("W2", TW), ("FB", 896), ("HB", 1792), ("ZT", 896), ("gm", 8)):
+    _sb(_n, _w, "bfloat16")
+for _n, _w in (("MR", 384), ("MT", 384), ("KF", 28), ("KL", 8), ("BQ", 672), ("BF", 2 * C), ("CUR", 128), ("CURF", 512), ("KEY", 128),
+               ("KEYF", 512), ("TQ", 128), ("TF", 128), ("MC", 128), ("MC2", 128), ("MCF", 512), ("MCG", 512), ("TMP", 1024),
+               ("DR", 1664), ("XL", 8), ("YL", 8), ("XK", 8), ("DK", 8), ("XF", 28), ("YF", 28), ("CK", 28), ("CT", 28), ("SIG", 480),
+               ("TT", 896), ("CA", 28), ("CB", 28), ("CD", 28), ("KT", 28), ("IOT", C), ("COL", 3 * C), ("OD", 480), ("GZ", 896),
+               ("PB", 896), ("RG", 2 * C), ("yb", C)):
+    _sb(_n, _w)
+for _n, _w in (("pi", 28), ("ii", 92), ("ML", 8), ("MF", 28)):
+    _sb(_n, _w, "int32")
+for _n, _w in (("LL", 8), ("LF", 28), ("RL", 28), ("RM", 28), ("R2", 28), ("ZL", 28), ("PL", 28), ("CW", 28), ("IC", 28), ("UL", 72)):
+    _sb(_n, _w, "uint16")
+_mx("qu", "su", 128)
+_mx("qB", "sB", 1024)
+_mx("qv", "pv", 128)
+_mx("wq", "wp", 512)
+_mx("qcb", "scb", 144)
+_mx("qcl", "scl", 512)
+_mx("qe", "se", 512)
+_mx("ga", "gas", 132)
+_mx("gb", "gbs", 132)
+_mx("wa", "was", 132)
+_mx("wb", "wbs", 132)
+for _t in range(ROUNDS + 1):
+    _mx("qx%d" % _t, "sx%d" % _t, C)
+    _mx("qp%d" % _t, "sp%d" % _t, C)
+for _t in range(ROUNDS):
+    _mx("zc%d" % _t, "zs%d" % _t, HALF)
+    _mx("lc%d" % _t, "ls%d" % _t, HALF)
+    _mx("hc%d" % _t, "hs%d" % _t, HALF // 2)
+SCRATCH["ps"] = ("psum", [128, 4096], "float32")
+
+SEMAPHORES = (["sv", "st", "ss", "sg", "snd", "dx", "dp", "du", "dw", "dv", "dy", "dc", "dd", "dq"]
+              + ["%s%d" % (_a, _t) for _a in ("rc", "rs", "lz") for _t in range(ROUNDS)])
+
+
+def _relays(topo, src, dst):
+    ok = [c for c in topo.cores_of(src) if c != src and topo.may_write(c, dst)]
+    near = [c for c in ok if topo.die(c) == topo.die(src)]
+    far = [c for c in ok if topo.die(c) != topo.die(src)]
+    return [near[0], far[0]]
+
+
+def _bits(engines):
+    m = 0
+    for e in engines:
+        m |= 1 << e
+    return m
+
+
+def _relay_program(g, core, T, topo):
+    n = len(T.cores)
+    for r in range(n):
+        dst = T.cores[(r + 1) % n]
+        rel = _relays(topo, T.cores[r], dst)
+        if core not in rel:
+            continue
+        h = rel.index(core)
+        a, b = h * HALF // 2, (h + 1) * HALF // 2
+        rid, pid = topo.addr(dst, core)
+        m = topo.mask(core, dst)
+        k = len(topo.engines(core, dst))
+        half = len(topo.engines(T.cores[r], core)) // 2
+        for t in range(ROUNDS):
+            g.wait_ge(T.sem["rc%d" % t], half)
+            g.remote_dma(T["lc%d" % t][:, a:b].bitcast(dt.uint8), T["hc%d" % t][:, :].bitcast(dt.uint8), T.sem["lz%d" % t], T.sem.snd, pid, rid, m)
+            g.wait_ge(T.sem["rs%d" % t], half)
+            g.remote_dma(T["ls%d" % t][:, a:b], T["hs%d" % t][:, :], T.sem["lz%d" % t], T.sem.snd, pid, rid, m)
+        g.wait_ge(T.sem.snd, 2 * k * ROUNDS)
+
+
+def rank_program(g, core, T, topo):
+    rank = T.rank_of(core)
+    if rank is None:
+        _relay_program(g, core, T, topo)
+        return
+    Q = {"v": g.vector, "t": g.tensor, "s": g.scalar, "g": g, "y": g.sync}
+    ESEM = {"v": "sv", "t": "st", "s": "ss", "g": "sg"}
+    count = {"sv": 0, "st": 0, "ss": 0, "sg": 0}
+    seen = {}
+    hist = {}
+
+    def A(name, c0, c1, st=1, p0=0, p1=128):
+        t = T[name]
+        if st == 1:
+            ap = t[:, c0:c1] if (p0, p1) == (0, 128) else t[p0:p1, c0:c1]
+        else:
+            ap = t[:, c0:c1:st] if (p0, p1) == (0, 128) else t[p0:p1, c0:c1:st]
+        return (ap, [(name, p0, p1, c0, c1, st)])
+
+    def ps(bank, c0, c1, st=1, p0=0, p1=128):
+        x = A("ps", 512 * bank + c0, 512 * bank + c1, st, p0, p1)
+        return (x[0], [("ps%d" % bank, 0, 128, 0, 512, 1)])
+
+    def ind(win, off):
+        return (win[0].indirect(off[0]), win[1] + off[1])
+
+    def bc(x):
+        return (x[0].bitcast(dt.uint8), x[1])
+
+    def u32(x):
+        return (x[0].bitcast(dt.uint32), x[1])
+
+    def wait(q, sem, val):
+        if seen.get((q, sem), 0) < val:
+            Q[q].wait_ge(T.sem[sem], val)
+            seen[(q, sem)] = val
+
+    def hazards(q, reads, writes):
+        need = {}
+        for regs, w in ((reads, False), (writes, True)):
+            for (n, p0, p1, c0, c1, st) in regs:
+                bank = n[:2] == "ps"
+                for (eq, sem, val, ew, a0, a1, b0, b1, bs) in hist.get(n, ()):
+                    if a0 >= p1 or p0 >= a1 or b0 >= c1 or c0 >= b1:
+                        continue
+                    if st == bs and (c0 - b0) % st:
+                        continue
+                    if bank and eq == q and (q == "t" or not ew):
+                        continue
+                    if not bank and not w and not ew:
+                        continue
+                    need[sem] = max(need.get(sem, 0), val)
+        for sem in need:
+            wait(q, sem, need[sem])
+
+    def note(q, sem, val, reads, writes):
+        for regs, w in ((reads, False), (writes, True)):
+            for (n, p0, p1, c0, c1, st) in regs:
+                h = hist.setdefault(n, [])
+                if w:
+                    h[:] = [e for e in h if not (p0 <= e[4] and e[5] <= p1 and c0 <= e[6] and e[7] <= c1 and e[0] == q
+                                                 and (st == 1 or (st == e[8] and (c0 - e[6]) % st == 0)))]
+                h[:] = [e for e in h if not (e[0] == q and e[1] == sem and e[3] == w and e[4:] == (p0, p1, c0, c1, st))]
+                h.append((q, sem, val, w, p0, p1, c0, c1, st))
+
+    def do(q, call, outs, ins):
+        reads = [r for x in ins for r in x[1]]
+        writes = [r for x in outs for r in x[1]]
+        hazards(q, reads, writes)
+        sem = ESEM[q]
+        count[sem] += 1
+        call().then_inc(T.sem[sem], 1)
+        note(q, sem, count[sem], reads, writes)
+
+    def dmas(q, pairs, sem):
+        for out, in_ in pairs:
+            hazards(q, in_[1], out[1])
+        for out, in_ in pairs:
+            Q[q].dma_start(out[0], in_[0]).then_inc(T.sem[sem], 16)
+        count[sem] = count.get(sem, 0) + 16 * len(pairs)
+        for out, in_ in pairs:
+            note("d" + sem, sem, count[sem], in_[1], out[1])
+
+    def tt(out, a, b, op):
+        do("v", lambda: g.vector.tensor_tensor(out[0], a[0], b[0], op), [out], [a, b])
+
+    def ts(out, a, s1, op0, s2=None, op1=None):
+        ins = [a] + [x for x in (s1, s2) if isinstance(x, tuple)]
+        v1 = s1[0] if isinstance(s1, tuple) else s1
+        v2 = s2[0] if isinstance(s2, tuple) else s2
+        if op1 is None:
+            do("v", lambda: g.vector.tensor_scalar(out[0], a[0], v1, None, op0), [out], ins)
+        else:
+            do("v", lambda: g.vector.tensor_scalar(out[0], a[0], v1, v2, op0, op1), [out], ins)
+
+    def cp(out, a):
+        do("v", lambda: g.vector.tensor_copy(out[0], a[0]), [out], [a])
+
+    def act(out, a, scale=1.0):
+        if isinstance(scale, tuple):
+            do("s", lambda: g.scalar.activation(out[0], a[0], AF.Copy, scale=scale[0]), [out], [a, scale])
+        elif scale == 1.0:
+            do("s", lambda: g.scalar.activation(out[0], a[0], AF.Copy), [out], [a])
+        else:
+            do("s", lambda: g.scalar.activation(out[0], a[0], AF.Copy, scale=scale), [out], [a])
+
+    def pick(qo, so, o, qi, si, w, off):
+        act(A(so, *o), ind(A(si, 0, w), off))
+        src = A(qi, 0, w)
+        do("v", lambda: g.vector.tensor_copy(u32(A(qo, *o))[0], u32(src)[0].indirect(off[0])), [A(qo, *o)], [src, off])
+
+    def scatter(win, off, vals):
+        do("v", lambda: g.vector.tensor_copy(win[0].indirect(off[0]), vals[0]), [win], [vals, off])
+
+    def scan(out, d0, d1):
+        do("v", lambda: g.vector.tensor_tensor_scan(out[0], d0[0], d1[0], -BIG, OP.min, OP.max), [out], [d0, d1])
+
+    def tr(out, a):
+        do("v", lambda: g.vector.transpose(out[0], a[0]), [out], [a])
+
+    def fill(x, val):
+        do("v", lambda: g.vector.memset(x[0], val), [x], [])
+
+    def quant(c, s, a):
+        do("v", lambda: g.vector.quantize_mx(c[0], s[0], a[0]), [c, s], [a])
+
+    def mm(out, w, ws, x, xs, start=True, stop=True):
+        do("t", lambda: g.tensor.matmul_mx(out[0], w[0], ws[0], x[0], xs[0], start, stop), [out], [w, ws, x, xs])
+
+    def aff(out, in_, pattern, op, val, base, cm):
+        do("g", lambda: g.affine_select(out[0], in_[0], pattern, op, val, base, cm), [out], [in_])
+
+    def iota(out, pattern, base, cm):
+        do("g", lambda: g.iota(out[0], pattern, base, cm, allow_small_or_imprecise_dtypes=True), [out], [])
+
+    def ext(ap):
+        return (ap, [])
+
+    dmas("s", [(A("pi", 0, 28, 1, 16 * h, 16 * h + 16), ext(T.p[:, :])) for h in range(0, 8)], "dp")
+    dmas("y", [(A("xt", 0, 1792), ext(T.x[:, :]))], "dx")
+    dmas("y", [(A("ut", 0, 512), ext(T.u[:, :]))], "du")
+    dmas("y", [(bc(A("wq", 0, 512)), ext(T.wc[:, :])), (A("wp", 0, 512), ext(T.ws[:, :]))], "dw")
+    dmas("y", [(A("vt", 0, 512), ext(T.v[:, :]))], "dv")
+
+    fill(A("qtr", 0, 576), 0.25)
+    fill(A("one", 0, 576), 1.0)
+    for h in range(8):
+        fill(A("UL", 8 * h, 8 * h + 8), 16 * h)
+    iota(A("ii", 0, 28), [[16, 28]], 0, 0)
+    iota(A("ii", 28, 56), [[0, 28]], 0, 1)
+    iota(A("ii", 84, 92), [[128, 4], [16, 2]], 0, 0)
+    aff(A("cb", 0, 576), A("qtr", 0, 576), [[0, 9], [1, 16], [-1, 4]], OP.is_equal, 0.0, 0, 0)
+    for k in range(4):
+        act(A("cl", 512 * k, 512 * k + 512), A("one", 0, 512), 0.0)
+    MASKS = {"m0": (0, 0, 1, 1.0), "lo": (1, 0, 16, 1.0), "hi": (2, 16, 32, 1.0), "h16": (3, 16, 32, 16.0),
+             "b0": (4, 7, 14, 1.0), "b1": (5, 0, 7, -1.0), "b2": (6, 21, 28, 1.0), "b3": (7, 14, 21, -1.0),
+             "c0": (8, 14, 28, 1.0), "c1": (9, 0, 14, -1.0), "p": (10, 0, 28, 1.0), "n": (11, 0, 28, -1.0)}
+
+    def mask(k):
+        j = MASKS[k][0]
+        return A("MT", 32 * j, 32 * j + 1)
+
+    def only(a):
+        return A("MT", 0, 1, 1, 32 * a, 32 * a + 32)
+
+    def phys(y, m, x):
+        ts(m, x, 1.0 / 7.0, OP.mult, -27.0 / 56.0, OP.add)
+        tt(y, m, x, OP.add)
+
+    def repeat_u(h):
+        pick("qB", "sB", (128 * h, 128 * h + 128), "qu", "su", 128, A("UL", 8 * h, 8 * h + 8))
+
+    ts(A("ii", 56, 84), A("ii", 28, 56), 15, OP.bitwise_and)
+    tt(A("KF", 0, 28), A("ii", 0, 28), A("ii", 56, 84), OP.add)
+    ts(A("KF", 0, 28), A("KF", 0, 28), 0.25, OP.mult)
+    phys(A("KL", 0, 7), A("ML", 0, 7), A("KF", 0, 7))
+    tt(A("DK", 0, 7), A("KF", 0, 7), A("KL", 0, 7), OP.subtract)
+    cp(A("PL", 0, 28), A("pi", 0, 28))
+
+    def masks():
+        fill(A("MR", 0, 384), 0.0)
+        for k in MASKS:
+            j, a, b, val = MASKS[k]
+            fill(A("MR", 32 * j + a, 32 * j + b), val)
+        tr(A("MT", 0, 384), A("MR", 0, 384))
+
+    def more_constants():
+        for k in range(4):
+            s = 4 * ((16 - 4 * k) % 16)
+            for a in range(4):
+                act(A("cl", 512 * k + 128 * a, 512 * k + 128 * a + 128, 1, 32 * a, 32 * a + 32), A("cb", s + 128 * a, s + 128 * a + 128, 1, 32 * a, 32 * a + 32))
+        fill(A("G", 0, TW), 0.0)
+        fill(A("WQ", 0, TW), 0.0)
+        quant(A("qcb", 0, 144), A("scb", 0, 144), A("cb", 0, 576))
+
+    def never(name, a, b, val):
+        aff(A(name, a, b), A("IOT", 0, b - a), [[0, b - a]], OP.is_equal, val, 1, 0)
+
+    iota(A("IOT", 0, C), [[1, C]], 0, 0)
+    never("DR", 0, 320, BIG)
+    never("DR", 320, 640, BIG)
+    aff(A("gm", 0, 8), A("one", 0, 8), [[-16, 8]], OP.is_ge, 0.0, 0, 1)
+    aff(A("gm", 0, 1), A("one", 0, 1), [[0, 1]], OP.is_ge, 0.0, 15, -1)
+    aff(A("eb", 0, 516), A("one", 0, 516), [[1, 516]], OP.is_equal, 0.0, -3, -4)
+    for c0 in (640, 984, 1328):
+        never("DR", c0, min(c0 + 344, 1664), BIG)
+    never("CURF", 0, 256, -BIG)
+    never("CURF", 256, 512, -BIG)
+    for name in ("W1", "W2", "SIG", "OD"):
+        n = SCRATCH[name][1][1]
+        iota(A(name, 0, n), [[0, n]], 0, 0)
+    BLK = [1, 2, 7, 14, 28, 56, 112, 224]
+
+    def resets(late):
+        if late:
+            fill(A("DR", 640, 1152, 128), -BIG)
+            fill(A("DR", 1152, 1664, 256), -BIG)
+            return
+        for s in (0, 7, 14, 21):
+            fill(A("DR", 128 + s, 256, 32), -BIG)
+        for s in (0, 14):
+            fill(A("DR", 256 + s, 384, 32), -BIG)
+        fill(A("DR", 384, 512, 32), -BIG)
+        fill(A("DR", 512, 640, 64), -BIG)
+
+    LB, FK = 4, 5
+
+    def counts(bank, ca, cas, cb_, cbs, local, start=True, stop=True):
+        for i, k in enumerate((0, 2, 1, 3)):
+            s = (16 - 4 * k) % 16
+            w, ws = (A("qcl", 128 * k, 128 * k + 128), A("scl", 128 * k, 128 * k + 128)) if local else (A("qcb", s, s + 128), A("scb", s, s + 128))
+            c, cs = (ca, cas) if k in (0, 2) else (cb_, cbs)
+            o = 2 if k in (2, 3) else 0
+            mm(ps(bank, 0, 128), w, ws, A(c, o, o + 128), A(cs, o, o + 128), start and i == 0, stop and i == 3)
+
+    def quant2(tile, ca, cas, cb_, cbs):
+        quant(A(ca, 0, 132), A(cas, 0, 132), A(tile, 0, 528))
+        quant(A(cb_, 0, 132), A(cbs, 0, 132), A(tile, 4, 532))
+
+    def wrap(dst, row, part=2):
+        if part != 1:
+            tr(A("TT", 0, C), A(row, 0, C))
+            tr(A("TT", C, 2 * C), A(row, 16, 16 + C))
+        if part == 0:
+            return
+        ts(A("CA", 0, 28), A("TT", 0, 896, 32), mask("lo"), OP.mult)
+        ts(A("CB", 0, 28), A("TT", 16, 896, 32), mask("hi"), OP.mult)
+        tt(A("CD", 0, 28), A("CA", 0, 28), A("CB", 0, 28), OP.add)
+        cp(A(dst, 0, 28, 2), A("CD", 0, 14))
+        cp(A(dst, 1, 28, 2), A("CD", 14, 28))
+
+    SBANK = [0, 1, 2, 3, 6, 7, 0, 1]
+    DBANK = [2, 3, 6, 7]
+    PBANK = [0, 1, 4, 2]
+    dst = T.cores[(rank + 1) % len(T.cores)]
+    rel = _relays(topo, core, dst)
+    eng = topo.engines(core, rel[0])
+    cut = [eng[:len(eng) // 2], eng[len(eng) // 2:]]
+    landed = 2 * sum(len(topo.engines(r, core)) for r in _relays(topo, T.cores[rank - 1], core))
+
+    for t in range(ROUNDS):
+        qx, sx, qp, sp = "qx%d" % t, "sx%d" % t, "qp%d" % t, "sp%d" % t
+        quant(A(qx, 0, C), A(sx, 0, C), A("xt" if t == 0 else "xn", 0, 1792))
+        for i in range(2):
+            pick(qp, sp, (HALF * i, HALF * i + HALF), qx, sx, C, A("PL", 14 * i, 14 * i + 14))
+        if t == 0:
+            quant(A("qu", 0, 128), A("su", 0, 128), A("ut", 0, 512))
+        for h in range(2):
+            if t == 0:
+                repeat_u(h)
+            for i, bank in enumerate(((0, 4), (1, 5))[h]):
+                o = (HALF * i, HALF * i + HALF)
+                mm(ps(bank, 0, HALF), A("qB", 128 * h, 128 * h + 128), A("sB", 128 * h, 128 * h + 128), A(qp, *o), A(sp, *o))
+        if t == 0:
+            masks()
+        for h in range(2):
+            for i, bank in enumerate(((0, 4), (1, 5))[h]):
+                for a in (2 * i, 2 * i + 1):
+                    out, in_ = A("BQ", 112 * h, 112 * h + 112, 1, 32 * a, 32 * a + 32), ps(bank, 112 * (a % 2), 112 * (a % 2) + 112, 1, 32 * a, 32 * a + 32)
+                    if i == 0:
+                        act(out, in_, only(a))
+                    else:
+                        ts(out, in_, only(a), OP.mult)
+
+        def scores(h):
+            mm(ps(SBANK[h], 0, C), A("qB", 128 * h, 128 * h + 128), A("sB", 128 * h, 128 * h + 128), A(qp, 0, C), A(sp, 0, C))
+
+        def evac(h):
+            if h > 5:
+                act(A("BF", C * (h - 6), C * (h - 5)), ps(SBANK[h], 0, C))
+                return
+            for a in range(4):
+                act(A("BQ", 112 * h, 112 * h + 112, 1, 32 * a, 32 * a + 32), ps(SBANK[h], 112 * a, 112 * a + 112, 1, 32 * a, 32 * a + 32))
+
+        def unpack(b):
+            mm(ps(DBANK[b], 0, C), A("qe", 128 * b, 128 * b + 128), A("se", 128 * b, 128 * b + 128), A(qp, 0, C), A(sp, 0, C))
+            act(A("HB", C * b, C * b + C), ps(DBANK[b], 0, C), 0.5)
+            if b < 2:
+                act(A("FB", C * b, C * b + C), ps(DBANK[b], 0, C))
+
+        if t == 0:
+            more_constants()
+            repeat_u(2)
+        scores(2)
+        evac(2)
+
+        def background(lev):
+            if t == 0:
+                if lev < 6:
+                    repeat_u(lev + 2)
+                if lev == 1:
+                    for b in range(4):
+                        quant(A("qe", 128 * b, 128 * b + 128), A("se", 128 * b, 128 * b + 128), A("eb", 3 - b, 515 - b))
+                    act(A("COL", 0, C), ind(A("IOT", 0, C), A("PL", 0, 28)))
+                if lev == 5:
+                    resets(True)
+                    ts(A("ii", 0, 8), A("ii", 28, 36), 96, OP.bitwise_and)
+                    tt(A("ii", 0, 8), A("ii", 0, 8), A("ii", 84, 92), OP.add)
+                    tt(A("ii", 0, 8), A("ii", 0, 8), A("ii", 56, 64), OP.add)
+                    cp(A("UL", 64, 72), A("ii", 0, 8))
+                    quant(A("qv", 0, 128), A("pv", 0, 128), A("vt", 0, 512))
+            scores(lev + 2)
+            evac(lev + 2)
+            if lev in (4, 5):
+                unpack(2 * (lev - 4))
+                unpack(2 * (lev - 4) + 1)
+
+        def keep(lev):
+            f = ps(FK, 0, 112, 4)
+            ts(A("CT", 0, 28), f, A("gm", lev, lev + 1), OP.mult)
+            if 0 < lev < 5:
+                tt(A("XF", 0, 28), f, A("XF" if lev > 1 else "KF", 0, 28), OP.add)
+            tt(A("CK", 0, 28), A("CK" if lev else "KF", 0, 28), A("CT", 0, 28), OP.add)
+
+        def spread(src, lev, c0=0):
+            for a in range(4):
+                (cp if a < 2 or lev in (0, 5) else act)(A("WQ", 112 * a, 112 * a + 112, 1, 32 * a, 32 * a + 32), A(src, c0, c0 + 112, 1, 32 * a, 32 * a + 32))
+
+        V = lambda n: A("TMP", 56 * n, 56 * n + 56)
+        L = lambda n: A("TMP", 56 * n, 56 * n + 56, 2)
+        R = lambda n: A("TMP", 56 * n + 1, 56 * n + 56, 2)
+        H = lambda n: A("TMP", 28 * n, 28 * n + 28)
+        s0, s1 = [[A("BQ", 112 * h + i, 112 * h + 112, 2) for i in range(2)] for h in range(2)]
+        tt(V(0), s0[1], s0[0], OP.is_lt)
+        tt(V(1), s1[0], s1[1], OP.max)
+        ts(V(2), V(0), -2 * BIG, OP.mult, BIG, OP.add)
+        ts(V(3), V(0), 2 * BIG, OP.mult, -BIG, OP.add)
+        cp(A("G", 256, 368, 2), V(0))
+        ts(A("G", 257, 368, 2), V(0), -1.0, OP.mult)
+        tt(V(2), s1[0], V(2), OP.min)
+        tt(V(3), s1[1], V(3), OP.min)
+        if t == 0:
+            fill(A("CUR", 0, 128), -BIG)
+            fill(A("MC", 0, 128), 0.0)
+        tt(V(4), V(2), V(3), OP.max)
+        if t == 0:
+            resets(False)
+        tt(H(10), L(4), R(4), OP.is_gt)
+        tt(H(11), L(4), R(1), OP.is_gt)
+        tt(H(12), L(1), R(4), OP.is_gt)
+        tt(H(13), L(1), R(1), OP.is_gt)
+        tt(H(14), H(10), H(11), OP.add)
+        tt(H(15), H(12), H(13), OP.add)
+        tt(H(16), H(10), H(12), OP.add)
+        tt(H(17), H(11), H(13), OP.add)
+        tt(H(18), H(15), H(14), OP.subtract)
+        tt(H(19), H(17), H(16), OP.subtract)
+        tt(H(20), H(14), L(0), OP.add)
+        tt(H(21), H(15), L(0), OP.subtract)
+        tt(H(22), R(0), H(16), OP.subtract)
+        tt(H(23), H(17), R(0), OP.add)
+        tt(H(18), H(18), L(0), OP.mult)
+        tt(H(19), H(19), R(0), OP.mult)
+        tt(A("G", 0, 112, 4), H(20), H(18), OP.add)
+        tt(A("G", 1, 112, 4), H(21), H(18), OP.subtract)
+        tt(A("G", 2, 112, 4), H(22), H(19), OP.subtract)
+        tt(A("G", 3, 112, 4), H(19), H(23), OP.subtract)
+        if t == 0:
+            for k in range(4):
+                quant(A("qcl", 128 * k, 128 * k + 128), A("scl", 128 * k, 128 * k + 128), A("cl", 512 * k, 512 * k + 512))
+        quant2("G", "ga", "gas", "gb", "gbs")
+        counts(LB, "ga", "gas", "gb", "gbs", True)
+        spread("G", 0, 256)
+        quant2("WQ", "wa", "was", "wb", "wbs")
+        counts(FK, "wa", "was", "wb", "wbs", False)
+        spread("G", 0)
+        tt(A("XL", 0, 7), ps(LB, 0, 28, 4), A("KL", 0, 7), OP.add)
+        ts(A("LL", 0, 7), A("XL", 0, 7), 4.0, OP.mult)
+        background(1)
+
+        for lev in range(2, 6):
+            scatter(A("CUR", 0, 128), A("LL", 0, 7), A("BQ", 112 * lev, 112 * lev + 112))
+            if lev == 2:
+                keep(0)
+                quant2("WQ", "wa", "was", "wb", "wbs")
+                counts(FK, "wa", "was", "wb", "wbs", False)
+            scan(A("KEY", 0, 128), A("DR", 128 * (lev - 1), 128 * lev), A("CUR", 0, 128))
+            tr(A("TQ", 0, 128), A("KEY", 0, 128))
+            one = lambda b: A("TQ", 32 * b, 32 * b + 1)
+            if lev in (2, 3):
+                w = BLK[lev]
+                for b in range(4):
+                    for j in range(28 // w):
+                        a = 32 * b + w * j
+                        ts(A("MC", a, a + w), A("KEY", a, a + w), one(b), OP.is_lt if j % 2 else OP.is_gt, mask(("b%d" if lev == 2 else "c%d") % j), OP.mult)
+            elif lev == 4:
+                for b in range(4):
+                    a = 32 * b
+                    ts(A("MC", a, a + 32), A("KEY", a, a + 32), one(b ^ 1), OP.is_lt if b % 2 else OP.is_gt, mask("n" if b % 2 else "p"), OP.mult)
+            else:
+                for i, m in enumerate(("MC", "MC2")):
+                    ts(A(m, 0, 64), A("KEY", 0, 64), one(2 + i), OP.is_gt, mask("p"), OP.mult)
+                    ts(A(m, 64, 128), A("KEY", 64, 128), one(i), OP.is_lt, mask("n"), OP.mult)
+                tt(A("MC", 0, 128), A("MC", 0, 128), A("MC2", 0, 128), OP.add)
+            cp(A("G", 0, 112), ind(A("MC", 0, 128), A("LL", 0, 7)))
+            if lev < 5:
+                quant2("G", "ga", "gas", "gb", "gbs")
+                counts(LB, "ga", "gas", "gb", "gbs", True)
+            spread("G", lev)
+            keep(lev - 1)
+            if lev == 4:
+                tt(A("XK", 0, 7), A("XL", 0, 7), A("DK", 0, 7), OP.add)
+            quant2("WQ", "wa", "was", "wb", "wbs")
+            counts(FK, "wa", "was", "wb", "wbs", False)
+            if lev < 5:
+                loc = ps(LB, 0, 28, 4)
+                if lev < 4:
+                    tt(A("XL", 0, 7), loc, A("XL", 0, 7), OP.add)
+                    ts(A("LL", 0, 7), A("XL", 0, 7), 4.0, OP.mult)
+                else:
+                    tt(A("XL", 0, 7), loc, A("XK", 0, 7), OP.add)
+                    phys(A("YL", 0, 7), A("ML", 0, 7), A("XL", 0, 7))
+                    ts(A("LL", 0, 7), A("YL", 0, 7), 4.0, OP.mult)
+            background(lev)
+
+        if t == ROUNDS - 1:
+            scatter(A("OD", 0, 480), A("R2", 0, 28), A("COL", C * t - C, C * t))
+        for lev in (6, 7):
+            tt(A("XF", 0, 28), ps(FK, 0, 112, 4), A("XF", 0, 28), OP.add)
+            phys(A("YF", 0, 28), A("MF", 0, 28), A("XF", 0, 28))
+            ts(A("LF", 0, 28), A("YF", 0, 28), 4.0, OP.mult)
+            scatter(A("CURF", 0, 512), A("LF", 0, 28), A("BF", C * (lev - 6), C * (lev - 5)))
+            scan(A("KEYF", 0, 512), A("DR", 640 + 512 * (lev - 6), 1152 + 512 * (lev - 6)), A("CURF", 0, 512))
+            cp(A("TMP", 0, 128), ind(A("KEYF", 0, 512), A("UL", 64, 72)))
+            tr(A("TF", 0, 128), A("TMP", 0, 128))
+            one = lambda s: A("TF", 32 * s, 32 * s + 1)
+            if lev == 6:
+                for s in range(4):
+                    ts(A("MCF", 128 * s, 128 * s + 128), A("KEYF", 128 * s, 128 * s + 128), one(s ^ 1), OP.is_lt if s % 2 else OP.is_gt, mask("n" if s % 2 else "p"), OP.mult)
+            else:
+                for i, m in ((1, "MCG"), (0, "MCF")):
+                    ts(A(m, 0, 256), A("KEYF", 0, 256), one(2 + i), OP.is_gt, mask("p"), OP.mult)
+                    ts(A(m, 256, 512), A("KEYF", 256, 512), one(i), OP.is_lt, mask("n"), OP.mult)
+                    if i:
+                        act(A("W2", 0, C), ind(A(m, 0, 512), A("LF", 0, 28)))
+            cp(A("W1", 0, C), ind(A("MCF", 0, 512), A("LF", 0, 28)))
+            keep(lev - 1)
+            quant2("W1", "wa", "was", "wb", "wbs")
+            counts(FK, "wa", "was", "wb", "wbs", False, True, lev == 6)
+            if lev == 7:
+                quant2("W2", "ga", "gas", "gb", "gbs")
+                counts(FK, "ga", "gas", "gb", "gbs", False, False, True)
+            if t == ROUNDS - 1:
+                wrap("CW", "OD", lev - 6)
+        keep(7)
+        ts(A("RL", 0, 28), A("CK", 0, 28), 4.0, OP.mult, mask("h16"), OP.add)
+        scatter(A("SIG", 0, 480), A("RL", 0, 28), A("IOT", 0, C))
+        wrap("ZL", "SIG")
+
+        for b in range(4):
+            (act if b else cp)(A("GZ", HALF * b, HALF * b + HALF), ind(A("HB", C * b, C * b + C), A("ZL", 0, 14)))
+        for b in range(4):
+            tt(A("ZT", b, 896, 4), ind(A("HB", C * b, C * b + C), A("ZL", 14, 28)), A("GZ", HALF * b, HALF * b + HALF), OP.add)
+        zc, zs = "zc%d" % t, "zs%d" % t
+        quant(A(zc, 0, HALF), A(zs, 0, HALF), A("ZT", 0, 896))
+
+        hazards("g", [(zc, 0, 128, 0, HALF, 1), (zs, 0, 128, 0, HALF, 1)], [])
+        for nm, hn, sn in ((zc, "hc%d" % t, "rc%d" % t), (zs, "hs%d" % t, "rs%d" % t)):
+            tf = []
+            for i in range(2):
+                rid, pid = topo.addr(rel[i], core)
+                s_, d_ = T[nm][:, i * HALF // 2:(i + 1) * HALF // 2], T[hn][:, :]
+                if nm == zc:
+                    s_, d_ = s_.bitcast(dt.uint8), d_.bitcast(dt.uint8)
+                tf.append(RemoteDMATransfer(dst_ids=[DstId(rid=rid, pnc=pid)], dma_engine_mask=_bits(cut[i]), remote_sem=T.sem[sn], src=s_, dst=d_))
+            g.remote_dma_fused(tf, local_sem=T.sem.snd)
+
+        ts(A("CT", 0, 28), A("CK", 0, 28), 56.0, OP.is_ge, -56.0, OP.mult)
+        tt(A("CA", 0, 28), A("CK", 0, 28), A("CT", 0, 28), OP.add)
+        ts(A("RM", 0, 28), A("CA", 0, 28), 4.0, OP.mult)
+        now = A("COL", C * t, C * t + C)
+        if t < ROUNDS - 1:
+            tt(A("KT", 0, 28), ps(FK, 0, 112, 4), A("XF", 0, 28), OP.add)
+            ts(A("R2", 0, 28), A("KT", 0, 28), 4.0, OP.mult, mask("h16"), OP.add)
+            scatter(A("SIG", 0, 480), A("R2", 0, 28), A("IOT", 0, C))
+            wrap("PL", "SIG")
+        else:
+            ts(A("R2", 0, 28), A("CW", 0, 28), mask("h16"), OP.add)
+            scatter(A("SIG", 0, 480), A("R2", 0, 28), A("IOT", 0, C))
+            wrap("IC", "SIG")
+
+        lc, ls = "lc%d" % t, "ls%d" % t
+        wait("t", "lz%d" % t, landed)
+        for b in (2, 0, 3, 1):
+            mm(ps(PBANK[b], 0, HALF), A("wq", 128 * b, 128 * b + 128), A("wp", 128 * b, 128 * b + 128), A(lc, 0, HALF), A(ls, 0, HALF))
+            act(A("PB", HALF * b, HALF * b + HALF), ps(PBANK[b], 0, HALF), 0.03125)
+        for b in (2, 3):
+            act(A("RG", C * (b - 2), C * (b - 1)), ind(A("PB", HALF * b, HALF * b + HALF), A("RM", 0, 28)))
+        if t < ROUNDS - 1:
+            act(A("COL", C * t + C, C * t + 2 * C), ind(now, A("PL", 0, 28)))
+        for b in (0, 1):
+            tt(A("xn", b, 1792, 4), ind(A("PB", HALF * b, HALF * b + HALF), A("RM", 0, 28)), A("FB", C * b, C * b + C), OP.add)
+        for b in (2, 3):
+            tt(A("xn", b, 1792, 4), A("RG", C * (b - 2), C * (b - 1)), ps(DBANK[b], 0, C), OP.add)
+
+    quant(A("qx3", 0, C), A("sx3", 0, C), A("xn", 0, 1792))
+    pick("qp3", "sp3", (0, C), "qx3", "sx3", C, A("IC", 0, 28))
+    mm(ps(0, 0, C), A("qv", 0, 128), A("pv", 0, 128), A("qp3", 0, C), A("sp3", 0, C))
+    dmas("y", [(ext(T.oc[:, :]), bc(A("qp3", 0, C)))], "dc")
+    dmas("s", [(ext(T.osc[4 * k:4 * k + 4, :]), A("sp3", 0, C, 1, 32 * k, 32 * k + 4)) for k in range(4)], "dq")
+    cp(A("yb", 0, C), ps(0, 0, C))
+    dmas("y", [(ext(T.y[:, :]), A("yb", 0, C))], "dy")
+    scatter(A("OD", 0, 480), A("RL", 0, 28), A("COL", C * t, C * t + C))
+    dmas("s", [(ext(T.od[h:h + 1, :]), A("OD", 16 * (h % 2), 16 * (h % 2) + C, 1, 16 * h, 16 * h + 1)) for h in range(8)], "dd")
+    for sem in count:
+        wait("g", sem, count[sem])
+    wait("g", "snd", 2 * len(eng) * ROUNDS)

@@ -3,9 +3,9 @@ from concourse.mybir import dt, AluOpType, ActivationFunctionType
 
 OP = AluOpType
 AF = ActivationFunctionType
-ROUNDS, C, HALF = 3, 448, 224
+ROUNDS, C, HALF, QS = 3, 448, 224, 112
 BIG = 1e29
-TW = 536
+BLOCK = (0, 2, 1, 3)
 
 SCRATCH = {}
 
@@ -19,30 +19,26 @@ def _mx(c, s, n):
     _sb(s, n, "uint8")
 
 
-for _n, _w in (("xt", 1792), ("xn", 1792), ("ut", 512), ("vt", 512), ("one", 576), ("qtr", 576), ("eb", 516), ("cb", 576), ("cl", 2048),
-               ("G", TW), ("WQ", TW), ("W1", TW), ("W2", TW), ("FB", 896), ("HB", 1792), ("ZT", 896), ("gm", 8)):
+for _n, _w in (("xt", 1792), ("xn", 1792), ("ut", 512), ("vt", 512), ("one", 516), ("eb", 516), ("wt6", 520), ("wt7", 776), ("G", 1024),
+               ("FB", 896), ("HB", 1792), ("ZT", 896), ("IOB", C), ("SIG", 480), ("TT", 992), ("COL", 3 * 480), ("MR", 384), ("MT", 384)):
     _sb(_n, _w, "bfloat16")
-for _n, _w in (("MR", 384), ("MT", 384), ("KF", 28), ("KL", 8), ("BQ", 672), ("BF", 2 * C), ("CUR", 128), ("CURF", 512), ("KEY", 128),
-               ("KEYF", 512), ("TQ", 128), ("TF", 128), ("MC", 128), ("MC2", 128), ("MCF", 512), ("MCG", 512), ("TMP", 1024),
-               ("DR", 1664), ("XL", 8), ("YL", 8), ("XK", 8), ("DK", 8), ("XF", 28), ("YF", 28), ("CK", 28), ("CT", 28), ("SIG", 480),
-               ("TT", 896), ("CA", 28), ("CB", 28), ("CD", 28), ("KT", 28), ("IOT", C), ("COL", 3 * C), ("OD", 480), ("GZ", 896),
-               ("PB", 896), ("RG", 2 * C), ("yb", C)):
+for _n, _w in (("RW", 384), ("CL", 384), ("MK", 12), ("QC", 8), ("KF", 16), ("KL", 16), ("DK", 16), ("KG", 8), ("OFS", 32), ("BQ", 7 * QS),
+               ("B7", HALF), ("CUR", 128), ("KEY", 128), ("KS", HALF), ("TQ", 128), ("MC", 128), ("TMP", 800), ("DR", 512), ("GR", 144),
+               ("G0", 144), ("TW", 288), ("TX", 288), ("XH", 128), ("XB", 48), ("W6", 256), ("K6", 128), ("W7", 512), ("K7", 256),
+               ("Y", 32), ("CK", 28), ("CA", 28), ("CT", 28), ("ZF", 512), ("OD", C), ("GZ", 896), ("PB", 896), ("RG", 2 * C), ("yb", C)):
     _sb(_n, _w)
-for _n, _w in (("pi", 28), ("ii", 92), ("ML", 8), ("MF", 28)):
+for _n, _w in (("pi", 28), ("ii", 64), ("ML", 16)):
     _sb(_n, _w, "int32")
-for _n, _w in (("LL", 8), ("LF", 28), ("RL", 28), ("RM", 28), ("R2", 28), ("ZL", 28), ("PL", 28), ("CW", 28), ("IC", 28), ("UL", 72)):
+for _n, _w in (("LS", 12), ("LL", 8), ("LG", 14), ("LH", 14), ("RL", 28), ("RM", 28), ("R2", 32), ("ZL", 32), ("PL", 32), ("IC", 32), ("UL", 64)):
     _sb(_n, _w, "uint16")
 _mx("qu", "su", 128)
 _mx("qB", "sB", 1024)
 _mx("qv", "pv", 128)
 _mx("wq", "wp", 512)
-_mx("qcb", "scb", 144)
-_mx("qcl", "scl", 512)
+_mx("q6", "s6", 130)
+_mx("q7", "s7", 194)
 _mx("qe", "se", 512)
-_mx("ga", "gas", 132)
-_mx("gb", "gbs", 132)
-_mx("wa", "was", 132)
-_mx("wb", "wbs", 132)
+_mx("qa", "sa", 256)
 for _t in range(ROUNDS + 1):
     _mx("qx%d" % _t, "sx%d" % _t, C)
     _mx("qp%d" % _t, "sp%d" % _t, C)
@@ -52,7 +48,7 @@ for _t in range(ROUNDS):
     _mx("hc%d" % _t, "hs%d" % _t, HALF // 2)
 SCRATCH["ps"] = ("psum", [128, 4096], "float32")
 
-SEMAPHORES = (["sv", "st", "ss", "sg", "snd", "dx", "dp", "du", "dw", "dv", "dy", "dc", "dd", "dq"]
+SEMAPHORES = (["sv", "st", "ss", "sg", "snd", "dx", "dx2", "dp", "du", "dw", "dv", "dy", "dy2", "dc", "dd", "dq"]
               + ["%s%d" % (_a, _t) for _a in ("rc", "rs", "lz") for _t in range(ROUNDS)])
 
 
@@ -109,6 +105,9 @@ def rank_program(g, core, T, topo):
         else:
             ap = t[:, c0:c1:st] if (p0, p1) == (0, 128) else t[p0:p1, c0:c1:st]
         return (ap, [(name, p0, p1, c0, c1, st)])
+
+    def AQ(name, a, c0, c1, st=1, n=1):
+        return A(name, c0, c1, st, 32 * a, 32 * (a + n))
 
     def ps(bank, c0, c1, st=1, p0=0, p1=128):
         x = A("ps", 512 * bank + c0, 512 * bank + c1, st, p0, p1)
@@ -189,9 +188,9 @@ def rank_program(g, core, T, topo):
     def cp(out, a):
         do("v", lambda: g.vector.tensor_copy(out[0], a[0]), [out], [a])
 
-    def act(out, a, scale=1.0):
-        if isinstance(scale, tuple):
-            do("s", lambda: g.scalar.activation(out[0], a[0], AF.Copy, scale=scale[0]), [out], [a, scale])
+    def act(out, a, scale=1.0, bias=None):
+        if bias is not None:
+            do("s", lambda: g.scalar.activation(out[0], a[0], AF.Identity, bias=bias[0]), [out], [a, bias])
         elif scale == 1.0:
             do("s", lambda: g.scalar.activation(out[0], a[0], AF.Copy), [out], [a])
         else:
@@ -206,7 +205,7 @@ def rank_program(g, core, T, topo):
         do("v", lambda: g.vector.tensor_copy(win[0].indirect(off[0]), vals[0]), [win], [vals, off])
 
     def scan(out, d0, d1):
-        do("v", lambda: g.vector.tensor_tensor_scan(out[0], d0[0], d1[0], -BIG, OP.min, OP.max), [out], [d0, d1])
+        do("v", lambda: g.vector.tensor_tensor_scan(out[0], d0[0], d1[0], BIG, OP.min, OP.max), [out], [d0, d1])
 
     def tr(out, a):
         do("v", lambda: g.vector.transpose(out[0], a[0]), [out], [a])
@@ -223,128 +222,136 @@ def rank_program(g, core, T, topo):
     def aff(out, in_, pattern, op, val, base, cm):
         do("g", lambda: g.affine_select(out[0], in_[0], pattern, op, val, base, cm), [out], [in_])
 
-    def iota(out, pattern, base, cm):
+    def iota(out, pattern, base, cm=0):
         do("g", lambda: g.iota(out[0], pattern, base, cm, allow_small_or_imprecise_dtypes=True), [out], [])
+
+    def never(name, a, b, val):
+        aff(A(name, a, b), A("ZF", 0, b - a), [[0, b - a]], OP.is_equal, val, 1, 0)
 
     def ext(ap):
         return (ap, [])
 
-    dmas("s", [(A("pi", 0, 28, 1, 16 * h, 16 * h + 16), ext(T.p[:, :])) for h in range(0, 8)], "dp")
-    dmas("y", [(A("xt", 0, 1792), ext(T.x[:, :]))], "dx")
-    dmas("y", [(A("ut", 0, 512), ext(T.u[:, :]))], "du")
+    dmas("s", [(A("ut", 0, 512), ext(T.u[:, :]))], "du")
+    dmas("y", [(A("xt", 0, 896), ext(T.x[:, 0:896]))], "dx")
+    dmas("s", [(A("xt", 896, 1792), ext(T.x[:, 896:1792]))], "dx2")
+    dmas("y", [(A("pi", 0, 28, 1, 16 * h, 16 * h + 16), ext(T.p[:, :])) for h in range(2)], "dp")
+    wait("y", "dx", 16)
     dmas("y", [(bc(A("wq", 0, 512)), ext(T.wc[:, :])), (A("wp", 0, 512), ext(T.ws[:, :]))], "dw")
     dmas("y", [(A("vt", 0, 512), ext(T.v[:, :]))], "dv")
 
-    fill(A("qtr", 0, 576), 0.25)
-    fill(A("one", 0, 576), 1.0)
-    for h in range(8):
-        fill(A("UL", 8 * h, 8 * h + 8), 16 * h)
-    iota(A("ii", 0, 28), [[16, 28]], 0, 0)
-    iota(A("ii", 28, 56), [[0, 28]], 0, 1)
-    iota(A("ii", 84, 92), [[128, 4], [16, 2]], 0, 0)
-    aff(A("cb", 0, 576), A("qtr", 0, 576), [[0, 9], [1, 16], [-1, 4]], OP.is_equal, 0.0, 0, 0)
-    for k in range(4):
-        act(A("cl", 512 * k, 512 * k + 512), A("one", 0, 512), 0.0)
-    MASKS = {"m0": (0, 0, 1, 1.0), "lo": (1, 0, 16, 1.0), "hi": (2, 16, 32, 1.0), "h16": (3, 16, 32, 16.0),
-             "b0": (4, 7, 14, 1.0), "b1": (5, 0, 7, -1.0), "b2": (6, 21, 28, 1.0), "b3": (7, 14, 21, -1.0),
-             "c0": (8, 14, 28, 1.0), "c1": (9, 0, 14, -1.0), "p": (10, 0, 28, 1.0), "n": (11, 0, 28, -1.0)}
+    iota(A("ii", 0, 64), [[16, 8], [0, 8]], 0)
+    ROWS = {"two": (0, ([[0, 2], [32, 4], [160, 2]], 0), ([[0, 2], [32, 4], [-128, 2]], 128)),
+            "q": (1, ([[1, 16]], 0), ([[1, 16]], 0)),
+            "one": (2, ([[0, 2], [32, 4], [34, 2]], 0), ([[0, 2], [32, 4], [-2, 2]], 2)),
+            "h16": (3, ([[0, 16]], 0), ([[0, 16]], 16)),
+            "upper": (4, ([[0, 16]], 1), ([[0, 2], [32, 4], [-2, 2]], 2)),
+            "h224": (5, ([[0, 16]], 224), ([[0, 16]], 224))}
+    for k in ROWS:
+        j, lo, hi = ROWS[k]
+        if lo == hi and len(lo[0]) == 1:
+            iota(A("RW", 32 * j, 32 * j + 32), [[0, 2]] + lo[0], lo[1])
+            continue
+        iota(A("RW", 32 * j, 32 * j + 16), *lo)
+        iota(A("RW", 32 * j + 16, 32 * j + 32), *hi)
+    for k in range(2):
+        iota(A("RW", 192 + 32 * k, 224 + 32 * k), [[16, 2], [32, 2], [1, 8]], 64 * k)
+        iota(A("RW", 256 + 32 * k, 288 + 32 * k), [[16, 2], [32, 8], [480, 2]], 256 * k)
+        iota(A("RW", 320 + 32 * k, 336 + 32 * k), [[32, 8], [-448, 2]], 496 + 256 * k)
+        iota(A("RW", 336 + 32 * k, 352 + 32 * k), [[32, 8], [480, 2]], 16 + 256 * k)
+    iota(A("KF", 0, 16), [[16, 16]], 0)
+    iota(A("ZF", 0, 512), [[0, 512]], 0)
+    never("DR", 0, 512, BIG)
+    iota(A("IOB", 0, C), [[1, C]], -HALF)
+    iota(A("QC", 0, 8), [[0, 8]], 0)
+    never("W6", 0, 129, -BIG)
+    never("W6", 129, 256, BIG)
+    never("K6", 0, 128, -BIG)
+    never("W7", 0, 257, -BIG)
+    never("W7", 257, 512, BIG)
+    never("K7", 0, 256, -BIG)
+
+    def lst(k, n=1):
+        j = ROWS[k][0] if k in ROWS else {"pairs": 6, "own": 8, "last": 10}[k]
+        return A("LS", j, j + n)
+
+    def col(k, p0=0, p1=128):
+        j = 32 * ROWS[k][0]
+        return A("CL", j, j + 1, 1, p0, p1)
+
+    MASKS = {"b0": (0, 7, 14, 1.0), "b1": (1, 0, 7, -1.0), "b2": (2, 21, 28, 1.0), "b3": (3, 14, 21, -1.0), "c0": (4, 14, 28, 1.0), "c1": (5, 0, 14, -1.0),
+             "p28": (6, 0, 28, 1.0), "n28": (7, 0, 28, -1.0), "p32": (8, 0, 32, 1.0), "n32": (9, 0, 32, -1.0), "p24": (10, 0, 24, 1.0), "n24": (11, 0, 24, -1.0)}
 
     def mask(k):
         j = MASKS[k][0]
-        return A("MT", 32 * j, 32 * j + 1)
+        return A("MK", j, j + 1)
 
-    def only(a):
-        return A("MT", 0, 1, 1, 32 * a, 32 * a + 32)
+    def repeat_u(h0, h1):
+        pick("qB", "sB", (128 * h0, 128 * h1), "qu", "su", 128, A("UL", 8 * h0, 8 * h1))
 
-    def phys(y, m, x):
-        ts(m, x, 1.0 / 7.0, OP.mult, -27.0 / 56.0, OP.add)
-        tt(y, m, x, OP.add)
+    fill(A("MR", 0, 384), 0.0)
+    fill(A("wt6", 0, 520), 0.0)
+    for k in MASKS:
+        j, a, b, val = MASKS[k]
+        fill(A("MR", 32 * j + a, 32 * j + b), val)
+    for a in range(4):
+        fill(AQ("wt6", a, 8 + 128 * a, 12 + 128 * a), 1.0 if a < 2 else -1.0)
+    fill(A("G", 0, 1024), 0.0)
+    tr(A("MT", 0, 384), A("MR", 0, 384))
+    cp(A("UL", 0, 64), A("ii", 0, 64))
+    quant(A("q6", 0, 130), A("s6", 0, 130), A("wt6", 0, 520))
+    for h in range(2):
+        ts(A("MK", 0, 12, 1, 64 * h, 64 * h + 64), A("MT", 0, 384, 32, 64 * h, 64 * h + 64), 1.0 - 2.0 * h, OP.mult)
+    quant(A("qa", 0, 256), A("sa", 0, 256), A("G", 0, 1024))
+    quant(A("qu", 0, 128), A("su", 0, 128), A("ut", 0, 512))
+    repeat_u(0, 2)
+    for name in ("GR", "G0", "TW", "TX", "MC", "CUR", "XH"):
+        fill(A(name, 0, SCRATCH[name][1][1]), 0.0)
+    for a in range(4):
+        cp(AQ("PL", a, 0, 28), AQ("pi", 0, 0, 28))
 
-    def repeat_u(h):
-        pick("qB", "sB", (128 * h, 128 * h + 128), "qu", "su", 128, A("UL", 8 * h, 8 * h + 8))
+    def lists():
+        tr(A("CL", 0, 384), A("RW", 0, 384))
+        cp(A("LS", 0, 12), A("CL", 0, 384, 32))
+        ts(A("KF", 0, 16), A("KF", 0, 16), col("q"), OP.add)
+        ts(A("ML", 0, 16), A("KF", 0, 16), 1.0 / 28.0, OP.mult, -27.0 / 56.0, OP.add)
+        ts(A("DK", 0, 16), A("ML", 0, 16), -4.0, OP.mult)
+        tt(A("KL", 0, 16), A("KF", 0, 16), A("DK", 0, 16), OP.subtract)
 
-    ts(A("ii", 56, 84), A("ii", 28, 56), 15, OP.bitwise_and)
-    tt(A("KF", 0, 28), A("ii", 0, 28), A("ii", 56, 84), OP.add)
-    ts(A("KF", 0, 28), A("KF", 0, 28), 0.25, OP.mult)
-    phys(A("KL", 0, 7), A("ML", 0, 7), A("KF", 0, 7))
-    tt(A("DK", 0, 7), A("KF", 0, 7), A("KL", 0, 7), OP.subtract)
-    cp(A("PL", 0, 28), A("pi", 0, 28))
-
-    def masks():
-        fill(A("MR", 0, 384), 0.0)
-        for k in MASKS:
-            j, a, b, val = MASKS[k]
-            fill(A("MR", 32 * j + a, 32 * j + b), val)
-        tr(A("MT", 0, 384), A("MR", 0, 384))
-
-    def more_constants():
-        for k in range(4):
-            s = 4 * ((16 - 4 * k) % 16)
-            for a in range(4):
-                act(A("cl", 512 * k + 128 * a, 512 * k + 128 * a + 128, 1, 32 * a, 32 * a + 32), A("cb", s + 128 * a, s + 128 * a + 128, 1, 32 * a, 32 * a + 32))
-        fill(A("G", 0, TW), 0.0)
-        fill(A("WQ", 0, TW), 0.0)
-        quant(A("qcb", 0, 144), A("scb", 0, 144), A("cb", 0, 576))
-
-    def never(name, a, b, val):
-        aff(A(name, a, b), A("IOT", 0, b - a), [[0, b - a]], OP.is_equal, val, 1, 0)
-
-    iota(A("IOT", 0, C), [[1, C]], 0, 0)
-    never("DR", 0, 320, BIG)
-    never("DR", 320, 640, BIG)
-    aff(A("gm", 0, 8), A("one", 0, 8), [[-16, 8]], OP.is_ge, 0.0, 0, 1)
-    aff(A("gm", 0, 1), A("one", 0, 1), [[0, 1]], OP.is_ge, 0.0, 15, -1)
-    aff(A("eb", 0, 516), A("one", 0, 516), [[1, 516]], OP.is_equal, 0.0, -3, -4)
-    for c0 in (640, 984, 1328):
-        never("DR", c0, min(c0 + 344, 1664), BIG)
-    never("CURF", 0, 256, -BIG)
-    never("CURF", 256, 512, -BIG)
-    for name in ("W1", "W2", "SIG", "OD"):
-        n = SCRATCH[name][1][1]
-        iota(A(name, 0, n), [[0, n]], 0, 0)
-    BLK = [1, 2, 7, 14, 28, 56, 112, 224]
-
-    def resets(late):
-        if late:
-            fill(A("DR", 640, 1152, 128), -BIG)
-            fill(A("DR", 1152, 1664, 256), -BIG)
-            return
+    def resets():
         for s in (0, 7, 14, 21):
-            fill(A("DR", 128 + s, 256, 32), -BIG)
+            fill(A("DR", s, 128, 32), -BIG)
         for s in (0, 14):
-            fill(A("DR", 256 + s, 384, 32), -BIG)
-        fill(A("DR", 384, 512, 32), -BIG)
-        fill(A("DR", 512, 640, 64), -BIG)
+            fill(A("DR", 128 + s, 256, 32), -BIG)
+        fill(A("DR", 256, 384, 32), -BIG)
+        fill(A("DR", 384, 496, 56), -BIG)
 
-    LB, FK = 4, 5
+    LB = 4
 
-    def counts(bank, ca, cas, cb_, cbs, local, start=True, stop=True):
-        for i, k in enumerate((0, 2, 1, 3)):
-            s = (16 - 4 * k) % 16
-            w, ws = (A("qcl", 128 * k, 128 * k + 128), A("scl", 128 * k, 128 * k + 128)) if local else (A("qcb", s, s + 128), A("scb", s, s + 128))
-            c, cs = (ca, cas) if k in (0, 2) else (cb_, cbs)
-            o = 2 if k in (2, 3) else 0
-            mm(ps(bank, 0, 128), w, ws, A(c, o, o + 128), A(cs, o, o + 128), start and i == 0, stop and i == 3)
+    def counts(lev):
+        n = HALF if lev == 7 else 128
+        quant(A("qa", 16, 16 + n), A("sa", 16, 16 + n), A("G", 64, 64 + 4 * n))
+        views = (("q7", "s7", 66, 16), ("q7", "s7", 64, 0), ("q7", "s7", 2, 128), ("q7", "s7", 0, QS)) if lev == 7 else (("q6", "s6", 2, 16), ("q6", "s6", 0, 0))
+        for i, (w, ws, a, b) in enumerate(views):
+            mm(ps(LB, 0, 128), A(w, a, a + 128), A(ws, a, a + 128), A("qa", b, b + 128), A("sa", b, b + 128), i == 0, i == len(views) - 1)
 
-    def quant2(tile, ca, cas, cb_, cbs):
-        quant(A(ca, 0, 132), A(cas, 0, 132), A(tile, 0, 528))
-        quant(A(cb_, 0, 132), A(cbs, 0, 132), A(tile, 4, 532))
+    def places(lev, base):
+        tr(A("TW", 0, 128), ps(LB, 0, 128))
+        tt(A("XH", 16 * lev, 16 * lev + 16), ind(A("TW", 0, 288), lst("upper" if lev == 7 else "one")), base, OP.add)
 
-    def wrap(dst, row, part=2):
-        if part != 1:
-            tr(A("TT", 0, C), A(row, 0, C))
-            tr(A("TT", C, 2 * C), A(row, 16, 16 + C))
-        if part == 0:
-            return
-        ts(A("CA", 0, 28), A("TT", 0, 896, 32), mask("lo"), OP.mult)
-        ts(A("CB", 0, 28), A("TT", 16, 896, 32), mask("hi"), OP.mult)
-        tt(A("CD", 0, 28), A("CA", 0, 28), A("CB", 0, 28), OP.add)
-        cp(A(dst, 0, 28, 2), A("CD", 0, 14))
-        cp(A(dst, 1, 28, 2), A("CD", 14, 28))
+    def turn(row, c0):
+        tr(A("TT", 0, 480), A(row, c0, c0 + 480))
+        tr(A("TT", 480, 480 + C), A(row, c0 + 16, c0 + 16 + C))
+
+    def fetch(dst, k, add):
+        ts(A(dst, 0, 32), ind(A("TT", 0, 992), lst(k, 2)), float(add), OP.add)
+
+    def lane(t, a, b):
+        return A("G", 64 + 4 * a + t, 64 + 4 * b, 4)
 
     SBANK = [0, 1, 2, 3, 6, 7, 0, 1]
     DBANK = [2, 3, 6, 7]
-    PBANK = [0, 1, 4, 2]
+    PBANK = [0, 1, 4, 5]
+    BLK = [1, 2, 7, 14, 28, 56, 112, 224]
     dst = T.cores[(rank + 1) % len(T.cores)]
     rel = _relays(topo, core, dst)
     eng = topo.engines(core, rel[0])
@@ -353,37 +360,34 @@ def rank_program(g, core, T, topo):
 
     for t in range(ROUNDS):
         qx, sx, qp, sp = "qx%d" % t, "sx%d" % t, "qp%d" % t, "sp%d" % t
-        quant(A(qx, 0, C), A(sx, 0, C), A("xt" if t == 0 else "xn", 0, 1792))
+        if t == 0:
+            for i in range(2):
+                quant(A(qx, HALF * i, HALF * i + HALF), A(sx, HALF * i, HALF * i + HALF), A("xt", 896 * i, 896 * i + 896))
+        else:
+            quant(A(qx, 0, C), A(sx, 0, C), A("xn", 0, 1792))
         for i in range(2):
             pick(qp, sp, (HALF * i, HALF * i + HALF), qx, sx, C, A("PL", 14 * i, 14 * i + 14))
-        if t == 0:
-            quant(A("qu", 0, 128), A("su", 0, 128), A("ut", 0, 512))
-        for h in range(2):
-            if t == 0:
-                repeat_u(h)
-            for i, bank in enumerate(((0, 4), (1, 5))[h]):
+        for i in range(2):
+            for h in range(2):
                 o = (HALF * i, HALF * i + HALF)
-                mm(ps(bank, 0, HALF), A("qB", 128 * h, 128 * h + 128), A("sB", 128 * h, 128 * h + 128), A(qp, *o), A(sp, *o))
+                mm(ps(((0, 4), (1, 5))[h][i], 0, HALF), A("qB", 128 * h, 128 * h + 128), A("sB", 128 * h, 128 * h + 128), A(qp, *o), A(sp, *o))
         if t == 0:
-            masks()
+            lists()
         for h in range(2):
             for i, bank in enumerate(((0, 4), (1, 5))[h]):
-                for a in (2 * i, 2 * i + 1):
-                    out, in_ = A("BQ", 112 * h, 112 * h + 112, 1, 32 * a, 32 * a + 32), ps(bank, 112 * (a % 2), 112 * (a % 2) + 112, 1, 32 * a, 32 * a + 32)
-                    if i == 0:
-                        act(out, in_, only(a))
-                    else:
-                        ts(out, in_, only(a), OP.mult)
+                for j in range(2):
+                    a = BLOCK[2 * i + j]
+                    (cp if i else act)(AQ("BQ", a, QS * h, QS * h + QS), ps(bank, QS * j, QS * j + QS, 1, 32 * a, 32 * a + 32))
 
         def scores(h):
             mm(ps(SBANK[h], 0, C), A("qB", 128 * h, 128 * h + 128), A("sB", 128 * h, 128 * h + 128), A(qp, 0, C), A(sp, 0, C))
-
-        def evac(h):
-            if h > 5:
-                act(A("BF", C * (h - 6), C * (h - 5)), ps(SBANK[h], 0, C))
-                return
             for a in range(4):
-                act(A("BQ", 112 * h, 112 * h + 112, 1, 32 * a, 32 * a + 32), ps(SBANK[h], 112 * a, 112 * a + 112, 1, 32 * a, 32 * a + 32))
+                if h < 7:
+                    c0 = QS * BLOCK[a]
+                    act(AQ("BQ", a, QS * h, QS * h + QS), ps(SBANK[h], c0, c0 + QS, 1, 32 * a, 32 * a + 32), -1.0 if h == 6 and a > 1 else 1.0)
+                else:
+                    c0 = HALF * (a % 2)
+                    act(AQ("B7", a, 0, HALF), ps(SBANK[h], c0, c0 + HALF, 1, 32 * a, 32 * a + 32), -1.0 if a % 2 else 1.0)
 
         def unpack(b):
             mm(ps(DBANK[b], 0, C), A("qe", 128 * b, 128 * b + 128), A("se", 128 * b, 128 * b + 128), A(qp, 0, C), A(sp, 0, C))
@@ -392,173 +396,170 @@ def rank_program(g, core, T, topo):
                 act(A("FB", C * b, C * b + C), ps(DBANK[b], 0, C))
 
         if t == 0:
-            more_constants()
-            repeat_u(2)
+            repeat_u(2, 4)
         scores(2)
-        evac(2)
+        scores(3)
+        if t:
+            scores(4)
+            scores(5)
 
         def background(lev):
-            if t == 0:
-                if lev < 6:
-                    repeat_u(lev + 2)
-                if lev == 1:
+            if t == 0 and lev == 1:
+                repeat_u(4, 6)
+                scores(4)
+                scores(5)
+            if lev == 2:
+                if t == 0:
+                    repeat_u(6, 8)
+                    fill(A("one", 0, 516), 1.0)
+                    aff(A("eb", 0, 516), A("one", 0, 516), [[1, 516]], OP.is_equal, 0.0, -3, -4)
+                    for name in ("SIG", "TT", "COL"):
+                        n = SCRATCH[name][1][1]
+                        iota(A(name, 0, n), [[0, n]], 0)
+                scores(6)
+                scores(7)
+            if lev == 3:
+                if t == 0:
                     for b in range(4):
                         quant(A("qe", 128 * b, 128 * b + 128), A("se", 128 * b, 128 * b + 128), A("eb", 3 - b, 515 - b))
-                    act(A("COL", 0, C), ind(A("IOT", 0, C), A("PL", 0, 28)))
-                if lev == 5:
-                    resets(True)
-                    ts(A("ii", 0, 8), A("ii", 28, 36), 96, OP.bitwise_and)
-                    tt(A("ii", 0, 8), A("ii", 0, 8), A("ii", 84, 92), OP.add)
-                    tt(A("ii", 0, 8), A("ii", 0, 8), A("ii", 56, 64), OP.add)
-                    cp(A("UL", 64, 72), A("ii", 0, 8))
+                    fill(AQ("QC", 2, 0, 1, 1, 2), float(QS))
+                    fill(AQ("QC", 2, 2, 3, 1, 2), 128.0)
+                    for a in (1, 3):
+                        fill(AQ("QC", a, 4, 5), float(HALF))
+                        fill(AQ("QC", a, 6, 7), 256.0)
+                    ts(A("CA", 0, 8), A("KF", 0, 8), col("h16"), OP.add, A("QC", 0, 1), OP.add)
+                    ts(A("KG", 0, 8), A("CA", 0, 8), A("QC", 4, 5), OP.add)
+                unpack(0)
+            if lev == 4:
+                unpack(1)
+                if t == 0:
+                    fill(A("wt7", 0, 776), 0.0)
+                    for a in range(4):
+                        fill(AQ("wt7", a, 264 + 128 * (a % 2), 268 + 128 * (a % 2)), -1.0 if a % 2 else 1.0)
+                    for m in range(4):
+                        tt(A("OFS", 8 * m, 8 * m + 8), A("KG", 0, 8), A("KL" if m < 2 else "KF", 0, 8), OP.subtract)
+                    quant(A("q7", 0, 194), A("s7", 0, 194), A("wt7", 0, 776))
+            if lev == 5:
+                unpack(2)
+                unpack(3)
+            if lev == 6:
+                for m in range(3):
+                    for a in range(4):
+                        act(AQ("CK", m, 7 * BLOCK[a], 7 * BLOCK[a] + 7), AQ("Y", a, 8 * m, 8 * m + 7))
+            if lev == 7:
+                if t == 0:
+                    act(A("COL", 16, 16 + C), ind(A("IOB", 0, C), A("PL", 0, 28)))
                     quant(A("qv", 0, 128), A("pv", 0, 128), A("vt", 0, 512))
-            scores(lev + 2)
-            evac(lev + 2)
-            if lev in (4, 5):
-                unpack(2 * (lev - 4))
-                unpack(2 * (lev - 4) + 1)
-
-        def keep(lev):
-            f = ps(FK, 0, 112, 4)
-            ts(A("CT", 0, 28), f, A("gm", lev, lev + 1), OP.mult)
-            if 0 < lev < 5:
-                tt(A("XF", 0, 28), f, A("XF" if lev > 1 else "KF", 0, 28), OP.add)
-            tt(A("CK", 0, 28), A("CK" if lev else "KF", 0, 28), A("CT", 0, 28), OP.add)
-
-        def spread(src, lev, c0=0):
-            for a in range(4):
-                (cp if a < 2 or lev in (0, 5) else act)(A("WQ", 112 * a, 112 * a + 112, 1, 32 * a, 32 * a + 32), A(src, c0, c0 + 112, 1, 32 * a, 32 * a + 32))
 
         V = lambda n: A("TMP", 56 * n, 56 * n + 56)
         L = lambda n: A("TMP", 56 * n, 56 * n + 56, 2)
         R = lambda n: A("TMP", 56 * n + 1, 56 * n + 56, 2)
         H = lambda n: A("TMP", 28 * n, 28 * n + 28)
-        s0, s1 = [[A("BQ", 112 * h + i, 112 * h + 112, 2) for i in range(2)] for h in range(2)]
+        four = lambda name, i: A(name, 16 + i, 128, 4)
+        s0, s1 = [[A("BQ", QS * h + i, QS * h + QS, 2) for i in range(2)] for h in range(2)]
         tt(V(0), s0[1], s0[0], OP.is_lt)
-        tt(V(1), s1[0], s1[1], OP.max)
+        if t == 0:
+            resets()
+        ts(V(1), V(0), 2 * BIG, OP.mult, -BIG, OP.add)
         ts(V(2), V(0), -2 * BIG, OP.mult, BIG, OP.add)
-        ts(V(3), V(0), 2 * BIG, OP.mult, -BIG, OP.add)
-        cp(A("G", 256, 368, 2), V(0))
-        ts(A("G", 257, 368, 2), V(0), -1.0, OP.mult)
-        tt(V(2), s1[0], V(2), OP.min)
-        tt(V(3), s1[1], V(3), OP.min)
-        if t == 0:
-            fill(A("CUR", 0, 128), -BIG)
-            fill(A("MC", 0, 128), 0.0)
-        tt(V(4), V(2), V(3), OP.max)
-        if t == 0:
-            resets(False)
-        tt(H(10), L(4), R(4), OP.is_gt)
-        tt(H(11), L(4), R(1), OP.is_gt)
-        tt(H(12), L(1), R(4), OP.is_gt)
-        tt(H(13), L(1), R(1), OP.is_gt)
-        tt(H(14), H(10), H(11), OP.add)
-        tt(H(15), H(12), H(13), OP.add)
-        tt(H(16), H(10), H(12), OP.add)
-        tt(H(17), H(11), H(13), OP.add)
-        tt(H(18), H(15), H(14), OP.subtract)
-        tt(H(19), H(17), H(16), OP.subtract)
-        tt(H(20), H(14), L(0), OP.add)
-        tt(H(21), H(15), L(0), OP.subtract)
-        tt(H(22), R(0), H(16), OP.subtract)
-        tt(H(23), H(17), R(0), OP.add)
-        tt(H(18), H(18), L(0), OP.mult)
-        tt(H(19), H(19), R(0), OP.mult)
-        tt(A("G", 0, 112, 4), H(20), H(18), OP.add)
-        tt(A("G", 1, 112, 4), H(21), H(18), OP.subtract)
-        tt(A("G", 2, 112, 4), H(22), H(19), OP.subtract)
-        tt(A("G", 3, 112, 4), H(19), H(23), OP.subtract)
-        if t == 0:
-            for k in range(4):
-                quant(A("qcl", 128 * k, 128 * k + 128), A("scl", 128 * k, 128 * k + 128), A("cl", 512 * k, 512 * k + 512))
-        quant2("G", "ga", "gas", "gb", "gbs")
-        counts(LB, "ga", "gas", "gb", "gbs", True)
-        spread("G", 0, 256)
-        quant2("WQ", "wa", "was", "wb", "wbs")
-        counts(FK, "wa", "was", "wb", "wbs", False)
-        spread("G", 0)
-        tt(A("XL", 0, 7), ps(LB, 0, 28, 4), A("KL", 0, 7), OP.add)
-        ts(A("LL", 0, 7), A("XL", 0, 7), 4.0, OP.mult)
+        cp(A("G0", 16, 128, 2), V(0))
+        ts(A("G0", 17, 128, 2), V(0), -1.0, OP.mult)
+        tt(V(3), s1[1], V(1), OP.min)
+        tt(V(4), s1[0], V(2), OP.min)
+        tr(A("TX", 0, 128), A("G0", 16, 144))
+        tt(V(5), s1[0], V(3), OP.max)
+        tt(V(6), s1[1], V(4), OP.max)
+        tr(A("TX", 128, 256), A("G0", 0, 128))
+        tt(H(14), L(5), R(5), OP.is_gt)
+        tt(H(15), L(5), R(6), OP.is_gt)
+        tt(H(16), L(6), R(5), OP.is_gt)
+        tt(H(17), L(6), R(6), OP.is_gt)
+        tt(H(18), four("G0", 0), H(14), OP.add)
+        tt(H(19), four("G0", 3), H(15), OP.subtract)
+        tt(H(20), four("G0", 1), H(16), OP.add)
+        tt(H(21), four("G0", 2), H(14), OP.subtract)
+        tt(four("GR", 0), H(18), H(15), OP.add)
+        tt(four("GR", 3), H(19), H(17), OP.subtract)
+        tt(four("GR", 1), H(20), H(17), OP.add)
+        tt(four("GR", 2), H(21), H(16), OP.subtract)
+        tr(A("TW", 0, 128), A("GR", 16, 144))
+        tr(A("TW", 128, 256), A("GR", 0, 128))
+        tt(A("XH", 16, 32), ind(A("TW", 0, 288), lst("two")), A("KL", 0, 16), OP.add)
+        tt(A("XH", 0, 16), ind(A("TX", 0, 288), lst("two")), A("KL", 0, 16), OP.add)
+        cp(A("LL", 0, 7), A("XH", 16, 23))
         background(1)
 
         for lev in range(2, 6):
-            scatter(A("CUR", 0, 128), A("LL", 0, 7), A("BQ", 112 * lev, 112 * lev + 112))
-            if lev == 2:
-                keep(0)
-                quant2("WQ", "wa", "was", "wb", "wbs")
-                counts(FK, "wa", "was", "wb", "wbs", False)
-            scan(A("KEY", 0, 128), A("DR", 128 * (lev - 1), 128 * lev), A("CUR", 0, 128))
-            tr(A("TQ", 0, 128), A("KEY", 0, 128))
+            w = BLK[lev]
+            n = QS if lev == 5 else 128
+            scatter(A("CUR", 0, 128), A("LL", 0, 7), A("BQ", QS * lev, QS * lev + QS))
+            if lev == 4:
+                tt(A("XB", 0, 16), A("XH", 48, 64), A("DK", 0, 16), OP.add)
+            scan(A("KEY", 0, n), A("DR", 128 * (lev - 2), 128 * (lev - 2) + n), A("CUR", 0, n))
             one = lambda b: A("TQ", 32 * b, 32 * b + 1)
-            if lev in (2, 3):
-                w = BLK[lev]
+            if lev < 4:
+                tr(A("TQ", 0, 128), A("KEY", 0, 128))
                 for b in range(4):
                     for j in range(28 // w):
                         a = 32 * b + w * j
                         ts(A("MC", a, a + w), A("KEY", a, a + w), one(b), OP.is_lt if j % 2 else OP.is_gt, mask(("b%d" if lev == 2 else "c%d") % j), OP.mult)
-            elif lev == 4:
-                for b in range(4):
-                    a = 32 * b
-                    ts(A("MC", a, a + 32), A("KEY", a, a + 32), one(b ^ 1), OP.is_lt if b % 2 else OP.is_gt, mask("n" if b % 2 else "p"), OP.mult)
+                cp(lane(0, 0, QS), ind(A("MC", 0, 128), A("LL", 0, 7)))
             else:
-                for i, m in enumerate(("MC", "MC2")):
-                    ts(A(m, 0, 64), A("KEY", 0, 64), one(2 + i), OP.is_gt, mask("p"), OP.mult)
-                    ts(A(m, 64, 128), A("KEY", 64, 128), one(i), OP.is_lt, mask("n"), OP.mult)
-                tt(A("MC", 0, 128), A("MC", 0, 128), A("MC2", 0, 128), OP.add)
-            cp(A("G", 0, 112), ind(A("MC", 0, 128), A("LL", 0, 7)))
-            if lev < 5:
-                quant2("G", "ga", "gas", "gb", "gbs")
-                counts(LB, "ga", "gas", "gb", "gbs", True)
-            spread("G", lev)
-            keep(lev - 1)
-            if lev == 4:
-                tt(A("XK", 0, 7), A("XL", 0, 7), A("DK", 0, 7), OP.add)
-            quant2("WQ", "wa", "was", "wb", "wbs")
-            counts(FK, "wa", "was", "wb", "wbs", False)
-            if lev < 5:
-                loc = ps(LB, 0, 28, 4)
-                if lev < 4:
-                    tt(A("XL", 0, 7), loc, A("XL", 0, 7), OP.add)
-                    ts(A("LL", 0, 7), A("XL", 0, 7), 4.0, OP.mult)
+                act(A("KS", 0, QS), ind(A("KEY", 0, 128), A("LL", 0, 7)))
+                if lev == 4:
+                    tr(A("TQ", 0, 128), A("KEY", 0, 128))
+                    for b in range(4):
+                        ts(lane(0, w * b, w * b + w), A("KS", w * b, w * b + w), one(b ^ 1), OP.is_lt if b % 2 else OP.is_gt, mask("n28" if b % 2 else "p28"), OP.mult)
                 else:
-                    tt(A("XL", 0, 7), loc, A("XK", 0, 7), OP.add)
-                    phys(A("YL", 0, 7), A("ML", 0, 7), A("XL", 0, 7))
-                    ts(A("LL", 0, 7), A("YL", 0, 7), 4.0, OP.mult)
+                    tr(A("TQ", 0, 64), A("KEY", 0, 64))
+                    tr(A("TQ", 64, 128), A("KEY", w, w + 64))
+                    for i, k in enumerate(("32", "24")):
+                        ts(lane(i, 0, w), A("KS", 0, w), one(2 + i), OP.is_gt, mask("p" + k), OP.mult)
+                        ts(lane(i, w, QS), A("KS", w, QS), one(i), OP.is_lt, mask("n" + k), OP.mult)
+            counts(lev)
             background(lev)
+            places(lev, A("XB", 0, 16) if lev == 4 else A("XH", 16 * lev - 16, 16 * lev))
+            if lev < 5:
+                cp(A("LL", 0, 7), A("XH", 16 * lev, 16 * lev + 7))
 
-        if t == ROUNDS - 1:
-            scatter(A("OD", 0, 480), A("R2", 0, 28), A("COL", C * t - C, C * t))
-        for lev in (6, 7):
-            tt(A("XF", 0, 28), ps(FK, 0, 112, 4), A("XF", 0, 28), OP.add)
-            phys(A("YF", 0, 28), A("MF", 0, 28), A("XF", 0, 28))
-            ts(A("LF", 0, 28), A("YF", 0, 28), 4.0, OP.mult)
-            scatter(A("CURF", 0, 512), A("LF", 0, 28), A("BF", C * (lev - 6), C * (lev - 5)))
-            scan(A("KEYF", 0, 512), A("DR", 640 + 512 * (lev - 6), 1152 + 512 * (lev - 6)), A("CURF", 0, 512))
-            cp(A("TMP", 0, 128), ind(A("KEYF", 0, 512), A("UL", 64, 72)))
-            tr(A("TF", 0, 128), A("TMP", 0, 128))
-            one = lambda s: A("TF", 32 * s, 32 * s + 1)
-            if lev == 6:
-                for s in range(4):
-                    ts(A("MCF", 128 * s, 128 * s + 128), A("KEYF", 128 * s, 128 * s + 128), one(s ^ 1), OP.is_lt if s % 2 else OP.is_gt, mask("n" if s % 2 else "p"), OP.mult)
-            else:
-                for i, m in ((1, "MCG"), (0, "MCF")):
-                    ts(A(m, 0, 256), A("KEYF", 0, 256), one(2 + i), OP.is_gt, mask("p"), OP.mult)
-                    ts(A(m, 256, 512), A("KEYF", 256, 512), one(i), OP.is_lt, mask("n"), OP.mult)
-                    if i:
-                        act(A("W2", 0, C), ind(A(m, 0, 512), A("LF", 0, 28)))
-            cp(A("W1", 0, C), ind(A("MCF", 0, 512), A("LF", 0, 28)))
-            keep(lev - 1)
-            quant2("W1", "wa", "was", "wb", "wbs")
-            counts(FK, "wa", "was", "wb", "wbs", False, True, lev == 6)
-            if lev == 7:
-                quant2("W2", "ga", "gas", "gb", "gbs")
-                counts(FK, "ga", "gas", "gb", "gbs", False, False, True)
-            if t == ROUNDS - 1:
-                wrap("CW", "OD", lev - 6)
-        keep(7)
-        ts(A("RL", 0, 28), A("CK", 0, 28), 4.0, OP.mult, mask("h16"), OP.add)
-        scatter(A("SIG", 0, 480), A("RL", 0, 28), A("IOT", 0, C))
-        wrap("ZL", "SIG")
+        ts(A("LL", 0, 7), A("XH", 80, 87), A("QC", 2, 3), OP.add)
+        cp(A("LG", 0, 7), A("XH", 80, 87))
+        scatter(A("W6", 0, 256), A("LL", 0, 7), A("BQ", QS * 6, QS * 7))
+        ts(A("XB", 16, 32), A("XH", 80, 96), A("QC", 0, 1), OP.add)
+        scan(A("K6", 0, QS), A("W6", 128, 128 + QS), A("W6", 0, QS))
+        tt(A("Y", 0, 32), ind(A("XH", 0, 128), lst("pairs", 2)), A("OFS", 0, 32), OP.add)
+        act(A("KS", 0, QS), ind(A("K6", 0, 128), A("LG", 0, 7)))
+        for h in range(2):
+            tr(AQ("TQ", 2 * h, 0, 128, 1, 2), AQ("K6", 2 - 2 * h, 0, 128, 1, 2))
+        for b in range(4):
+            ts(lane(b, 0, QS), A("KS", 0, QS), A("TQ", 32 * b, 32 * b + 1), OP.add, 0.0, OP.is_gt)
+        counts(6)
+        background(6)
+        places(6, A("XB", 16, 32))
+
+        for h in range(2):
+            for d in range(2):
+                ts(AQ("LH", 2 * d, 7 * h, 7 * h + 7, 1, 2), AQ("XH", 2 * h, 96, 103, 1, 2), AQ("QC", 2 * d, 6, 7, 1, 2), OP.add)
+        scatter(A("W7", 0, 512), A("LH", 0, 14), A("B7", 0, HALF))
+        ts(A("LG", 0, 14), A("LH", 0, 14), A("QC", 6, 7), OP.subtract)
+        ts(A("XB", 32, 48), A("XH", 96, 112), A("QC", 4, 5), OP.add)
+        scan(A("K7", 0, HALF), A("W7", 256, 256 + HALF), A("W7", 0, HALF))
+        for p0, p1 in ((0, 64), (64, 96)):
+            cp(A("RL", 0, 28, 1, p0, p1), A("CK", 0, 28, 1, p0, p1))
+        act(A("KS", 0, HALF), ind(A("K7", 0, 256), A("LG", 0, 14)))
+        for a in range(4):
+            tr(AQ("TQ", a, 0, 128), AQ("K7", a ^ 1, 128 * (a // 2), 128 * (a // 2) + 128))
+        for b in range(4):
+            ts(lane(b, 0, HALF), A("KS", 0, HALF), A("TQ", 32 * b, 32 * b + 1), OP.add, 0.0, OP.is_gt)
+        counts(7)
+        background(7)
+        places(7, A("XB", 32, 48))
+        for a in range(4):
+            ts(AQ("RL", 3, 7 * BLOCK[a], 7 * BLOCK[a] + 7), AQ("XH", a, 112, 119), col("h16", 32 * a, 32 * a + 32), OP.add)
+
+        scatter(A("SIG", 0, 480), A("RL", 0, 28), A("IOB", 0, C))
+        turn("SIG", 0)
+        fetch("ZL", "own", HALF)
 
         for b in range(4):
             (act if b else cp)(A("GZ", HALF * b, HALF * b + HALF), ind(A("HB", C * b, C * b + C), A("ZL", 0, 14)))
@@ -578,43 +579,55 @@ def rank_program(g, core, T, topo):
                 tf.append(RemoteDMATransfer(dst_ids=[DstId(rid=rid, pnc=pid)], dma_engine_mask=_bits(cut[i]), remote_sem=T.sem[sn], src=s_, dst=d_))
             g.remote_dma_fused(tf, local_sem=T.sem.snd)
 
-        ts(A("CT", 0, 28), A("CK", 0, 28), 56.0, OP.is_ge, -56.0, OP.mult)
-        tt(A("CA", 0, 28), A("CK", 0, 28), A("CT", 0, 28), OP.add)
-        ts(A("RM", 0, 28), A("CA", 0, 28), 4.0, OP.mult)
-        now = A("COL", C * t, C * t + C)
+        ts(A("CA", 0, 28), A("RL", 0, 28), col("h16"), OP.subtract)
+        now = A("COL", 480 * t + 16, 480 * t + 16 + C)
         if t < ROUNDS - 1:
-            tt(A("KT", 0, 28), ps(FK, 0, 112, 4), A("XF", 0, 28), OP.add)
-            ts(A("R2", 0, 28), A("KT", 0, 28), 4.0, OP.mult, mask("h16"), OP.add)
-            scatter(A("SIG", 0, 480), A("R2", 0, 28), A("IOT", 0, C))
-            wrap("PL", "SIG")
-        else:
-            ts(A("R2", 0, 28), A("CW", 0, 28), mask("h16"), OP.add)
-            scatter(A("SIG", 0, 480), A("R2", 0, 28), A("IOT", 0, C))
-            wrap("IC", "SIG")
+            fetch("PL", "last", HALF)
+        ts(A("CT", 0, 28), A("CA", 0, 28), float(HALF), OP.is_ge, -float(HALF), OP.mult)
+        if t < ROUNDS - 1:
+            for a in range(3):
+                cp(AQ("PL", a, 0, 28), AQ("PL", 3, 0, 28))
+        tt(A("CA", 0, 28), A("CA", 0, 28), A("CT", 0, 28), OP.add)
+        cp(A("RM", 0, 28), A("CA", 0, 28))
+        if t < ROUNDS - 1:
+            act(A("COL", 480 * t + 496, 480 * t + 496 + C), ind(now, A("PL", 0, 28)))
+            act(A("G", 64, 576), A("one", 0, 512), 0.0)
+        if t == ROUNDS - 2:
+            turn("COL", 480 * t + 480)
+            fetch("R2", "last", HALF + 16)
+        if t == ROUNDS - 1:
+            act(A("OD", 0, C), ind(now, A("ZL", 0, 28)), bias=col("h224"))
+            dmas("y", [(ext(T.od[h:h + 1, :]), A("OD", 0, C, 1, 16 * h, 16 * h + 1)) for h in range(8)], "dd")
+            scatter(A("SIG", 0, 480), A("R2", 0, 28), A("IOB", 0, C))
+            turn("SIG", 0)
+            fetch("IC", "last", HALF)
 
         lc, ls = "lc%d" % t, "ls%d" % t
         wait("t", "lz%d" % t, landed)
         for b in (2, 0, 3, 1):
             mm(ps(PBANK[b], 0, HALF), A("wq", 128 * b, 128 * b + 128), A("wp", 128 * b, 128 * b + 128), A(lc, 0, HALF), A(ls, 0, HALF))
-            act(A("PB", HALF * b, HALF * b + HALF), ps(PBANK[b], 0, HALF), 0.03125)
+            if b > 1:
+                act(A("PB", HALF * b, HALF * b + HALF), ps(PBANK[b], 0, HALF), 0.03125)
+            else:
+                ts(A("PB", HALF * b, HALF * b + HALF), ps(PBANK[b], 0, HALF), 0.03125, OP.mult)
         for b in (2, 3):
             act(A("RG", C * (b - 2), C * (b - 1)), ind(A("PB", HALF * b, HALF * b + HALF), A("RM", 0, 28)))
-        if t < ROUNDS - 1:
-            act(A("COL", C * t + C, C * t + 2 * C), ind(now, A("PL", 0, 28)))
         for b in (0, 1):
             tt(A("xn", b, 1792, 4), ind(A("PB", HALF * b, HALF * b + HALF), A("RM", 0, 28)), A("FB", C * b, C * b + C), OP.add)
         for b in (2, 3):
             tt(A("xn", b, 1792, 4), A("RG", C * (b - 2), C * (b - 1)), ps(DBANK[b], 0, C), OP.add)
 
     quant(A("qx3", 0, C), A("sx3", 0, C), A("xn", 0, 1792))
-    pick("qp3", "sp3", (0, C), "qx3", "sx3", C, A("IC", 0, 28))
-    mm(ps(0, 0, C), A("qv", 0, 128), A("pv", 0, 128), A("qp3", 0, C), A("sp3", 0, C))
+    for i in range(2):
+        o = (HALF * i, HALF * i + HALF)
+        pick("qp3", "sp3", o, "qx3", "sx3", C, A("IC", 14 * i, 14 * i + 14))
+        mm(ps(i, 0, HALF), A("qv", 0, 128), A("pv", 0, 128), A("qp3", *o), A("sp3", *o))
     dmas("y", [(ext(T.oc[:, :]), bc(A("qp3", 0, C)))], "dc")
+    act(A("yb", 0, HALF), ps(0, 0, HALF))
+    cp(A("yb", HALF, C), ps(1, 0, HALF))
+    dmas("s", [(ext(T.y[:, 0:HALF]), A("yb", 0, HALF))], "dy")
+    dmas("y", [(ext(T.y[:, HALF:C]), A("yb", HALF, C))], "dy2")
     dmas("s", [(ext(T.osc[4 * k:4 * k + 4, :]), A("sp3", 0, C, 1, 32 * k, 32 * k + 4)) for k in range(4)], "dq")
-    cp(A("yb", 0, C), ps(0, 0, C))
-    dmas("y", [(ext(T.y[:, :]), A("yb", 0, C))], "dy")
-    scatter(A("OD", 0, 480), A("RL", 0, 28), A("COL", C * t, C * t + C))
-    dmas("s", [(ext(T.od[h:h + 1, :]), A("OD", 16 * (h % 2), 16 * (h % 2) + C, 1, 16 * h, 16 * h + 1)) for h in range(8)], "dd")
     for sem in count:
         wait("g", sem, count[sem])
     wait("g", "snd", 2 * len(eng) * ROUNDS)

@@ -5,6 +5,7 @@ OP = AluOpType
 AF = ActivationFunctionType
 ROUNDS, C, HALF, QS = 3, 448, 224, 112
 BIG = 1e29
+LIFT = 64
 BLOCK = (0, 2, 1, 3)
 
 SCRATCH = {}
@@ -19,20 +20,29 @@ def _mx(c, s, n):
     _sb(s, n, "uint8")
 
 
-for _n, _w in (("xt", 1792), ("xn", 1792), ("ut", 512), ("vt", 512), ("one", 516), ("eb", 516), ("wt6", 520), ("wt7", 776), ("G", 1024),
-               ("FB", 896), ("HB", 1792), ("ZT", 896), ("IOB", C), ("SIG", 480), ("TT", 992), ("COL", 3 * 480), ("MR", 384), ("MT", 384)):
+PARTS = {}
+_z = 0
+for _n, _w in (("MB", 144), ("GR", 144), ("G0", 144), ("LR", 144), ("DKR", 144), ("MP", 128), ("LC", 128), ("T1", 288), ("TX", 288), ("TL", 288), ("CS", 288)):
+    PARTS[_n] = ("Z", _z)
+    _z += _w
+for _k, _n in enumerate(("MK", "QC", "KF", "KL", "DK", "KG", "OFS", "Y", "CK", "CA", "CT", "NS")):
+    PARTS[_n] = ("S", 32 * _k)
+for _n, _w in (("Z", _z), ("xt", 1792), ("xn", 1792), ("ut", 512), ("vt", 512), ("one", 516), ("eb", 516), ("wt6", 520), ("wt7", 776), ("G", 1024),
+               ("FB", 896), ("HB", 1792), ("ZT", 896), ("IOB", C), ("SIG", 480), ("TT", 992), ("COL", 3 * 480), ("MR", 384), ("MT", 384),
+               ("PH", QS), ("MKL", QS), ("TB", 256), ("DB", 256), ("DT", 288), ("UW", 896), ("UT", 896), ("RN", 480)):
     _sb(_n, _w, "bfloat16")
-for _n, _w in (("RW", 384), ("CL", 384), ("MK", 12), ("QC", 8), ("KF", 16), ("KL", 16), ("DK", 16), ("KG", 8), ("OFS", 32), ("BQ", 7 * QS),
-               ("B7", HALF), ("CUR", 128), ("KEY", 128), ("KS", HALF), ("TQ", 128), ("MC", 128), ("TMP", 800), ("DR", 512), ("GR", 144),
-               ("G0", 144), ("TW", 288), ("TX", 288), ("XH", 128), ("XB", 48), ("W6", 256), ("K6", 128), ("W7", 512), ("K7", 256),
-               ("Y", 32), ("CK", 28), ("CA", 28), ("CT", 28), ("ZF", 512), ("OD", C), ("GZ", 896), ("PB", 896), ("RG", 2 * C), ("yb", C)):
+for _n, _w in (("RW", 512), ("CL", 512), ("S", 384), ("BQ", 7 * QS),
+               ("B7", HALF), ("CUR", 128), ("CU5", 128), ("KEY", 128), ("KS", HALF), ("TQ", 128), ("MC", 256), ("TMP", 800), ("DR", 512),
+               ("TW", 160), ("XH", 128), ("XB", 48), ("W6", 256), ("K6", 128), ("W7", 512), ("K7", 256),
+               ("ZF", 512), ("OD", C), ("GZ", 896), ("PB", 896), ("RG", 2 * C), ("yb", C)):
     _sb(_n, _w)
-for _n, _w in (("pi", 28), ("ii", 64), ("ML", 16)):
+for _n, _w in (("pi", 28), ("ii", 16), ("ML", 16), ("NI", 28), ("NA", 28)):
     _sb(_n, _w, "int32")
-for _n, _w in (("LS", 12), ("LL", 8), ("LG", 14), ("LH", 14), ("RL", 28), ("RM", 28), ("R2", 32), ("ZL", 32), ("PL", 32), ("IC", 32), ("UL", 64)):
+for _n, _w in (("LS", 16), ("LL", 16), ("L2", 16), ("LG", 14), ("LH", 14), ("RL", 28), ("RM", 32), ("R2", 32), ("ZL", 32), ("PL", 32), ("IC", 32),
+               ("UL", 16), ("NL", 28)):
     _sb(_n, _w, "uint16")
 _mx("qu", "su", 128)
-_mx("qB", "sB", 1024)
+_mx("qB", "sB", 256)
 _mx("qv", "pv", 128)
 _mx("wq", "wp", 512)
 _mx("q6", "s6", 130)
@@ -41,7 +51,8 @@ _mx("qe", "se", 512)
 _mx("qa", "sa", 256)
 for _t in range(ROUNDS + 1):
     _mx("qx%d" % _t, "sx%d" % _t, C)
-    _mx("qp%d" % _t, "sp%d" % _t, C)
+for _n in ("p0", "p3", "f0", "f1"):
+    _mx("q" + _n, "s" + _n, C)
 for _t in range(ROUNDS):
     _mx("zc%d" % _t, "zs%d" % _t, HALF)
     _mx("lc%d" % _t, "ls%d" % _t, HALF)
@@ -49,14 +60,14 @@ for _t in range(ROUNDS):
 SCRATCH["ps"] = ("psum", [128, 4096], "float32")
 
 SEMAPHORES = (["sv", "st", "ss", "sg", "snd", "dx", "dx2", "dp", "du", "dw", "dv", "dy", "dy2", "dc", "dd", "dq"]
-              + ["%s%d" % (_a, _t) for _a in ("rc", "rs", "lz") for _t in range(ROUNDS)])
+              + ["%s%d" % (_a, _t) for _a in ("rc", "lz") for _t in range(ROUNDS)])
 
 
 def _relays(topo, src, dst):
     ok = [c for c in topo.cores_of(src) if c != src and topo.may_write(c, dst)]
     near = [c for c in ok if topo.die(c) == topo.die(src)]
     far = [c for c in ok if topo.die(c) != topo.die(src)]
-    return [near[0], far[0]]
+    return [near[0], far[0], near[1], far[1]]
 
 
 def _bits(engines):
@@ -74,17 +85,18 @@ def _relay_program(g, core, T, topo):
         if core not in rel:
             continue
         h = rel.index(core)
-        a, b = h * HALF // 2, (h + 1) * HALF // 2
+        a, b = h % 2 * HALF // 2, (h % 2 + 1) * HALF // 2
         rid, pid = topo.addr(dst, core)
         m = topo.mask(core, dst)
         k = len(topo.engines(core, dst))
         half = len(topo.engines(T.cores[r], core)) // 2
         for t in range(ROUNDS):
             g.wait_ge(T.sem["rc%d" % t], half)
-            g.remote_dma(T["lc%d" % t][:, a:b].bitcast(dt.uint8), T["hc%d" % t][:, :].bitcast(dt.uint8), T.sem["lz%d" % t], T.sem.snd, pid, rid, m)
-            g.wait_ge(T.sem["rs%d" % t], half)
-            g.remote_dma(T["ls%d" % t][:, a:b], T["hs%d" % t][:, :], T.sem["lz%d" % t], T.sem.snd, pid, rid, m)
-        g.wait_ge(T.sem.snd, 2 * k * ROUNDS)
+            if h < 2:
+                g.remote_dma(T["lc%d" % t][:, a:b].bitcast(dt.uint8), T["hc%d" % t][:, :].bitcast(dt.uint8), T.sem["lz%d" % t], T.sem.snd, pid, rid, m)
+            else:
+                g.remote_dma(T["ls%d" % t][:, a:b], T["hs%d" % t][:, :], T.sem["lz%d" % t], T.sem.snd, pid, rid, m)
+        g.wait_ge(T.sem.snd, k * ROUNDS)
 
 
 def rank_program(g, core, T, topo):
@@ -99,6 +111,8 @@ def rank_program(g, core, T, topo):
     hist = {}
 
     def A(name, c0, c1, st=1, p0=0, p1=128):
+        if name in PARTS:
+            name, c0, c1 = PARTS[name][0], c0 + PARTS[name][1], c1 + PARTS[name][1]
         t = T[name]
         if st == 1:
             ap = t[:, c0:c1] if (p0, p1) == (0, 128) else t[p0:p1, c0:c1]
@@ -188,11 +202,11 @@ def rank_program(g, core, T, topo):
     def cp(out, a):
         do("v", lambda: g.vector.tensor_copy(out[0], a[0]), [out], [a])
 
-    def act(out, a, scale=1.0, bias=None):
+    def act(out, a, scale=1.0, bias=None, func=None):
         if bias is not None:
-            do("s", lambda: g.scalar.activation(out[0], a[0], AF.Identity, bias=bias[0]), [out], [a, bias])
+            do("s", lambda: g.scalar.activation(out[0], a[0], func or AF.Identity, bias=bias[0]), [out], [a, bias])
         elif scale == 1.0:
-            do("s", lambda: g.scalar.activation(out[0], a[0], AF.Copy), [out], [a])
+            do("s", lambda: g.scalar.activation(out[0], a[0], func or AF.Copy), [out], [a])
         else:
             do("s", lambda: g.scalar.activation(out[0], a[0], AF.Copy, scale=scale), [out], [a])
 
@@ -204,8 +218,8 @@ def rank_program(g, core, T, topo):
     def scatter(win, off, vals):
         do("v", lambda: g.vector.tensor_copy(win[0].indirect(off[0]), vals[0]), [win], [vals, off])
 
-    def scan(out, d0, d1):
-        do("v", lambda: g.vector.tensor_tensor_scan(out[0], d0[0], d1[0], BIG, OP.min, OP.max), [out], [d0, d1])
+    def scan(out, d0, d1, first=BIG, op0=OP.min, op1=OP.max):
+        do("v", lambda: g.vector.tensor_tensor_scan(out[0], d0[0], d1[0], first, op0, op1), [out], [d0, d1])
 
     def tr(out, a):
         do("v", lambda: g.vector.transpose(out[0], a[0]), [out], [a])
@@ -228,6 +242,11 @@ def rank_program(g, core, T, topo):
     def never(name, a, b, val):
         aff(A(name, a, b), A("ZF", 0, b - a), [[0, b - a]], OP.is_equal, val, 1, 0)
 
+    def const(name, a, b, val, st=1, p0=0, p1=128):
+        for c0 in range(a, b, 512 * st):
+            c1 = min(c0 + 512 * st, b)
+            act(A(name, c0, c1, st, p0, p1), A("one", 0, len(range(c0, c1, st)), 1, p0, p1), val)
+
     def ext(ap):
         return (ap, [])
 
@@ -239,40 +258,35 @@ def rank_program(g, core, T, topo):
     dmas("y", [(bc(A("wq", 0, 512)), ext(T.wc[:, :])), (A("wp", 0, 512), ext(T.ws[:, :]))], "dw")
     dmas("y", [(A("vt", 0, 512), ext(T.v[:, :]))], "dv")
 
-    iota(A("ii", 0, 64), [[16, 8], [0, 8]], 0)
-    ROWS = {"two": (0, ([[0, 2], [32, 4], [160, 2]], 0), ([[0, 2], [32, 4], [-128, 2]], 128)),
-            "q": (1, ([[1, 16]], 0), ([[1, 16]], 0)),
-            "one": (2, ([[0, 2], [32, 4], [34, 2]], 0), ([[0, 2], [32, 4], [-2, 2]], 2)),
-            "h16": (3, ([[0, 16]], 0), ([[0, 16]], 16)),
-            "upper": (4, ([[0, 16]], 1), ([[0, 2], [32, 4], [-2, 2]], 2)),
-            "h224": (5, ([[0, 16]], 224), ([[0, 16]], 224))}
-    for k in ROWS:
-        j, lo, hi = ROWS[k]
-        if lo == hi and len(lo[0]) == 1:
-            iota(A("RW", 32 * j, 32 * j + 32), [[0, 2]] + lo[0], lo[1])
-            continue
-        iota(A("RW", 32 * j, 32 * j + 16), *lo)
-        iota(A("RW", 32 * j + 16, 32 * j + 32), *hi)
-    for k in range(2):
-        iota(A("RW", 192 + 32 * k, 224 + 32 * k), [[16, 2], [32, 2], [1, 8]], 64 * k)
-        iota(A("RW", 256 + 32 * k, 288 + 32 * k), [[16, 2], [32, 8], [480, 2]], 256 * k)
-        iota(A("RW", 320 + 32 * k, 336 + 32 * k), [[32, 8], [-448, 2]], 496 + 256 * k)
-        iota(A("RW", 336 + 32 * k, 352 + 32 * k), [[32, 8], [480, 2]], 16 + 256 * k)
-    iota(A("KF", 0, 16), [[16, 16]], 0)
-    iota(A("ZF", 0, 512), [[0, 512]], 0)
-    never("DR", 0, 512, BIG)
-    iota(A("IOB", 0, C), [[1, C]], -HALF)
-    iota(A("QC", 0, 8), [[0, 8]], 0)
-    never("W6", 0, 129, -BIG)
-    never("W6", 129, 256, BIG)
-    never("K6", 0, 128, -BIG)
-    never("W7", 0, 257, -BIG)
-    never("W7", 257, 512, BIG)
-    never("K7", 0, 256, -BIG)
+    ROWS = {"two": (0, [([[0, 2], [32, 4], [160, 2]], 0), ([[0, 2], [32, 4], [-128, 2]], 128)]),
+            "drop": (1, [([[0, 32]], -LIFT)]),
+            "end": (2, [([[0, 2], [32, 4], [160, 2]], 31), ([[0, 2], [32, 4], [-128, 2]], 159)]),
+            "h16": (3, [([[16, 2], [0, 16]], 0)]),
+            "one": (4, [([[0, 2], [32, 4], [34, 2]], 0), ([[0, 2], [32, 4], [-2, 2]], 2)]),
+            "h224": (5, [([[0, 32]], HALF)]),
+            "upper": (6, [([[0, 16]], 1), ([[0, 2], [32, 4], [-2, 2]], 2)]),
+            "none": (7, [([[0, 32]], 0)]),
+            "pairs": (8, [([[16, 2], [32, 2], [1, 8]], 64 * k) for k in range(2)]),
+            "own": (10, [([[16, 2], [32, 8], [480, 2]], 256 * k) for k in range(2)]),
+            "last": (12, [x for k in range(2) for x in (([[32, 8], [-448, 2]], 496 + 256 * k), ([[32, 8], [480, 2]], 16 + 256 * k))]),
+            "mine": (14, [x for k in range(2) for x in (([[32, 8], [-448, 2]], 480 + 256 * k), ([[32, 8], [480, 2]], 16 + 256 * k))])}
+
+    def rows(names):
+        for k in names:
+            c0 = 32 * ROWS[k][0]
+            for pattern, base in ROWS[k][1]:
+                n = 1
+                for step, cnt in pattern:
+                    n *= cnt
+                iota(A("RW", c0, c0 + n), pattern, base)
+                c0 += n
+
+    def lists(j0, j1):
+        tr(A("CL", 32 * j0, 32 * j1), A("RW", 32 * j0, 32 * j1))
+        cp(A("LS", j0, j1), A("CL", 32 * j0, 32 * j1, 32))
 
     def lst(k, n=1):
-        j = ROWS[k][0] if k in ROWS else {"pairs": 6, "own": 8, "last": 10}[k]
-        return A("LS", j, j + n)
+        return A("LS", ROWS[k][0], ROWS[k][0] + n)
 
     def col(k, p0=0, p1=128):
         j = 32 * ROWS[k][0]
@@ -285,47 +299,92 @@ def rank_program(g, core, T, topo):
         j = MASKS[k][0]
         return A("MK", j, j + 1)
 
-    def repeat_u(h0, h1):
-        pick("qB", "sB", (128 * h0, 128 * h1), "qu", "su", 128, A("UL", 8 * h0, 8 * h1))
+    for a, b in ((0, 16), (128, 160), (272, 304), (416, 448), (560, 592), (704, 976)):
+        fill(A("Z", a, b), 0.0)
+    iota(A("ii", 0, 16), [[16, 8], [0, 2]], 0)
+    iota(A("one", 0, 516), [[0, 516]], 1)
+    rows(("two", "drop", "end", "h16"))
+    iota(A("PH", 0, QS), [[32, 4], [1, 28]], 0)
+    for b in range(4):
+        iota(A("LC", 32 * b, 32 * b + 28), [[14, 2], [135, 2], [1, 7]], 32 * b)
+    iota(A("MC", 0, 256), [[0, 256]], 0)
+    iota(A("XH", 0, 128), [[0, 128]], 0)
+    iota(A("DKR", 16, 128), [[-4, 4], [0, 28]], LIFT)
+    aff(A("eb", 0, 516), A("one", 0, 516), [[1, 516]], OP.is_equal, 0.0, -3, -4)
+    rows(("one", "h224", "upper", "none", "pairs", "own", "last", "mine"))
+    iota(A("ZF", 0, 260), [[0, 260]], 0)
+    never("W6", 0, 129, -BIG)
+    never("W6", 129, 256, BIG)
+    never("K6", 0, 128, -BIG)
+    iota(A("IOB", 0, C), [[1, C]], -HALF)
+    never("W7", 0, 257, -BIG)
+    never("W7", 257, 512, BIG)
+    never("K7", 0, 256, -BIG)
+    for name in ("SIG", "TT", "RN", "UW", "COL"):
+        iota(A(name, 0, SCRATCH[name][1][1]), [[0, SCRATCH[name][1][1]]], 0)
 
     fill(A("MR", 0, 384), 0.0)
-    fill(A("wt6", 0, 520), 0.0)
+    cp(A("UL", 0, 16), A("ii", 0, 16))
     for k in MASKS:
         j, a, b, val = MASKS[k]
         fill(A("MR", 32 * j + a, 32 * j + b), val)
-    for a in range(4):
-        fill(AQ("wt6", a, 8 + 128 * a, 12 + 128 * a), 1.0 if a < 2 else -1.0)
-    fill(A("G", 0, 1024), 0.0)
-    tr(A("MT", 0, 384), A("MR", 0, 384))
-    cp(A("UL", 0, 64), A("ii", 0, 64))
-    quant(A("q6", 0, 130), A("s6", 0, 130), A("wt6", 0, 520))
-    for h in range(2):
-        ts(A("MK", 0, 12, 1, 64 * h, 64 * h + 64), A("MT", 0, 384, 32, 64 * h, 64 * h + 64), 1.0 - 2.0 * h, OP.mult)
-    quant(A("qa", 0, 256), A("sa", 0, 256), A("G", 0, 1024))
-    quant(A("qu", 0, 128), A("su", 0, 128), A("ut", 0, 512))
-    repeat_u(0, 2)
-    for name in ("GR", "G0", "TW", "TX", "MC", "CUR", "XH"):
-        fill(A(name, 0, SCRATCH[name][1][1]), 0.0)
+    fill(A("MR", 32 * 6 + 31, 32 * 8, 32), -float(LIFT))
     for a in range(4):
         cp(AQ("PL", a, 0, 28), AQ("pi", 0, 0, 28))
+    tr(A("MT", 0, 384), A("MR", 0, 384))
+    fill(A("DB", 0, 256), -BIG)
+    cp(A("MK", 0, 8), A("MT", 0, 256, 32))
+    quant(A("qu", 0, 128), A("su", 0, 128), A("ut", 0, 512))
+    for j in range(4):
+        ts(A("MP", 7 * j, 7 * j + 7), A("one", 0, 7), mask("b%d" % j), OP.mult)
+    const("DR", 0, 512, BIG)
+    const("CUR", 0, 128, 0.0)
+    for name in ("T1", "TX", "TL", "CS"):
+        const(name, 256, 288, 0.0)
+    for a, b, st in ((0, 128, 32), (7, 128, 32), (14, 256, 32), (21, 128, 32), (128, 384, 32), (256 + 63, 384, 64), (384, 496, 56)):
+        const("DR", a, b, -BIG, st)
+    const("CUR", 31, 128, BIG, 64)
+    const("CUR", 63, 128, -BIG, 64)
+    pick("qB", "sB", (0, 256), "qu", "su", 128, A("UL", 0, 16))
 
-    def lists():
-        tr(A("CL", 0, 384), A("RW", 0, 384))
-        cp(A("LS", 0, 12), A("CL", 0, 384, 32))
-        ts(A("KF", 0, 16), A("KF", 0, 16), col("q"), OP.add)
-        ts(A("ML", 0, 16), A("KF", 0, 16), 1.0 / 28.0, OP.mult, -27.0 / 56.0, OP.add)
-        ts(A("DK", 0, 16), A("ML", 0, 16), -4.0, OP.mult)
-        tt(A("KL", 0, 16), A("KF", 0, 16), A("DK", 0, 16), OP.subtract)
-
-    def resets():
-        for s in (0, 7, 14, 21):
-            fill(A("DR", s, 128, 32), -BIG)
-        for s in (0, 14):
-            fill(A("DR", 128 + s, 256, 32), -BIG)
-        fill(A("DR", 256, 384, 32), -BIG)
-        fill(A("DR", 384, 496, 56), -BIG)
+    def first(lev, point):
+        key = (lev, point)
+        if key == (2, 0):
+            turn2("DT", "DKR")
+        if key == (3, 0):
+            quant(A("q6", 0, 130), A("s6", 0, 130), A("wt6", 0, 520))
+        if lev == 3 and point > 0:
+            b = point - 1
+            quant(A("qe", 128 * b, 128 * b + 128), A("se", 128 * b, 128 * b + 128), A("eb", 3 - b, 515 - b))
+        if lev == 4 and point in (0, 3, 4):
+            j = 4 + 4 * (0, 0, 0, 1, 2)[point]
+            tr(A("CL", 32 * j, 32 * j + 128), A("RW", 32 * j, 32 * j + 128))
+        if key == (4, 2):
+            quant(A("qa", 0, 256), A("sa", 0, 256), A("G", 0, 1024))
+        if key == (5, 0):
+            cp(A("LS", 4, 16), A("CL", 128, 512, 32))
+        if key == (6, 0):
+            quant(A("q7", 0, 194), A("s7", 0, 194), A("wt7", 0, 776))
+            quant(A("qv", 0, 128), A("pv", 0, 128), A("vt", 0, 512))
 
     LB = 4
+
+    def turn2(out, row):
+        tr(A(out, 0, 128), A(row, 16, 144))
+        tr(A(out, 128, 256), A(row, 0, 128))
+
+    def sums(lev, once):
+        once(lev, 3)
+        turn2("TB", "MB")
+        once(lev, 4)
+        for c0 in (0, 128):
+            scan(A("CS", c0, c0 + 128), A("DB", c0, c0 + 128), A("TB", c0, c0 + 128), -BIG, OP.max, OP.add)
+        cp(A("LL", 0, 16), ind(A("CS", 0, 288), lst("end")))
+        if lev == 2:
+            cp(A("DB", 0, 256, 32), A("CS", 31, 256, 32))
+        if lev == 3:
+            tt(A("DB", 0, 256, 32), A("CS", 31, 256, 32), A("DT", 0, 256, 32), OP.add)
+        act(A("XH", 16 * lev, 16 * lev + 16), ind(A("CS", 0, 288), lst("end")))
 
     def counts(lev):
         n = HALF if lev == 7 else 128
@@ -336,7 +395,7 @@ def rank_program(g, core, T, topo):
 
     def places(lev, base):
         tr(A("TW", 0, 128), ps(LB, 0, 128))
-        tt(A("XH", 16 * lev, 16 * lev + 16), ind(A("TW", 0, 288), lst("upper" if lev == 7 else "one")), base, OP.add)
+        tt(A("XH", 16 * lev, 16 * lev + 16), ind(A("TW", 0, 160), lst("upper" if lev == 7 else "one")), base, OP.add)
 
     def turn(row, c0):
         tr(A("TT", 0, 480), A(row, c0, c0 + 480))
@@ -348,7 +407,6 @@ def rank_program(g, core, T, topo):
     def lane(t, a, b):
         return A("G", 64 + 4 * a + t, 64 + 4 * b, 4)
 
-    SBANK = [0, 1, 2, 3, 6, 7, 0, 1]
     DBANK = [2, 3, 6, 7]
     PBANK = [0, 1, 4, 5]
     BLK = [1, 2, 7, 14, 28, 56, 112, 224]
@@ -356,100 +414,112 @@ def rank_program(g, core, T, topo):
     rel = _relays(topo, core, dst)
     eng = topo.engines(core, rel[0])
     cut = [eng[:len(eng) // 2], eng[len(eng) // 2:]]
-    landed = 2 * sum(len(topo.engines(r, core)) for r in _relays(topo, T.cores[rank - 1], core))
+    landed = sum(len(topo.engines(r, core)) for r in _relays(topo, T.cores[rank - 1], core))
 
     for t in range(ROUNDS):
-        qx, sx, qp, sp = "qx%d" % t, "sx%d" % t, "qp%d" % t, "sp%d" % t
-        if t == 0:
-            for i in range(2):
-                quant(A(qx, HALF * i, HALF * i + HALF), A(sx, HALF * i, HALF * i + HALF), A("xt", 896 * i, 896 * i + 896))
-        else:
-            quant(A(qx, 0, C), A(sx, 0, C), A("xn", 0, 1792))
+        last = t == ROUNDS - 1
+        qx, sx = "qx%d" % t, "sx%d" % t
+        qp, sp = (qx, sx) if t else ("qp0", "sp0")
         for i in range(2):
-            pick(qp, sp, (HALF * i, HALF * i + HALF), qx, sx, C, A("PL", 14 * i, 14 * i + 14))
+            quant(A(qx, HALF * i, HALF * i + HALF), A(sx, HALF * i, HALF * i + HALF), A("xn" if t else "xt", 896 * i, 896 * i + 896))
         for i in range(2):
-            for h in range(2):
-                o = (HALF * i, HALF * i + HALF)
-                mm(ps(((0, 4), (1, 5))[h][i], 0, HALF), A("qB", 128 * h, 128 * h + 128), A("sB", 128 * h, 128 * h + 128), A(qp, *o), A(sp, *o))
+            o = (HALF * i, HALF * i + HALF)
+            if t == 0:
+                pick(qp, sp, o, qx, sx, C, A("PL", 14 * i, 14 * i + 14))
+            mm(ps(i, 0, HALF), A("qB", 0, 128), A("sB", 0, 128), A(qp, *o), A(sp, *o))
+        mm(ps(5, 0, C), A("qB", 128, 256), A("sB", 128, 256), A(qp, 0, C), A(sp, 0, C))
         if t == 0:
-            lists()
-        for h in range(2):
-            for i, bank in enumerate(((0, 4), (1, 5))[h]):
-                for j in range(2):
-                    a = BLOCK[2 * i + j]
-                    (cp if i else act)(AQ("BQ", a, QS * h, QS * h + QS), ps(bank, QS * j, QS * j + QS, 1, 32 * a, 32 * a + 32))
+            cp(A("MP", 32, 64), A("MP", 0, 32))
+            lists(0, 4)
+            cp(A("MP", 64, 128), A("MP", 0, 64))
+        once = first if t == 0 else (lambda lev, point: None)
 
-        def scores(h):
-            mm(ps(SBANK[h], 0, C), A("qB", 128 * h, 128 * h + 128), A("sB", 128 * h, 128 * h + 128), A(qp, 0, C), A(sp, 0, C))
-            for a in range(4):
-                if h < 7:
-                    c0 = QS * BLOCK[a]
-                    act(AQ("BQ", a, QS * h, QS * h + QS), ps(SBANK[h], c0, c0 + QS, 1, 32 * a, 32 * a + 32), -1.0 if h == 6 and a > 1 else 1.0)
+        def scores(h, blocks=range(4), by=act):
+            p = (32 * (h % 4), 32 * (h % 4) + 32)
+            for k in blocks:
+                a = BLOCK[k]
+                if h < 4:
+                    by(AQ("BQ", a, QS * h, QS * h + QS), ps(k // 2, QS * (k % 2), QS * (k % 2) + QS, 1, *p))
+                elif h < 7:
+                    by(AQ("BQ", a, QS * h, QS * h + QS), ps(5, QS * k, QS * k + QS, 1, *p), -1.0 if h == 6 and a > 1 else 1.0)
                 else:
-                    c0 = HALF * (a % 2)
-                    act(AQ("B7", a, 0, HALF), ps(SBANK[h], c0, c0 + HALF, 1, 32 * a, 32 * a + 32), -1.0 if a % 2 else 1.0)
+                    by(AQ("B7", k, 0, HALF), ps(5, HALF * (k % 2), HALF * (k % 2) + HALF, 1, *p), -1.0 if k % 2 else 1.0)
 
-        def unpack(b):
-            mm(ps(DBANK[b], 0, C), A("qe", 128 * b, 128 * b + 128), A("se", 128 * b, 128 * b + 128), A(qp, 0, C), A(sp, 0, C))
+        def unpack(b, q, s):
+            mm(ps(DBANK[b], 0, C), A("qe", 128 * b, 128 * b + 128), A("se", 128 * b, 128 * b + 128), A(q, 0, C), A(s, 0, C))
+
+        def halves(b):
+            unpack(b, qp, sp)
             act(A("HB", C * b, C * b + C), ps(DBANK[b], 0, C), 0.5)
-            if b < 2:
+            if last and b < 2:
                 act(A("FB", C * b, C * b + C), ps(DBANK[b], 0, C))
 
-        if t == 0:
-            repeat_u(2, 4)
-        scores(2)
-        scores(3)
-        if t:
-            scores(4)
-            scores(5)
+        for h in range(2):
+            scores(h, (0, 1))
+            scores(h, (2, 3), cp)
+        for h in range(2, 6):
+            scores(h)
+        now = A("COL", 480 * t + 16, 480 * t + 16 + C)
 
         def background(lev):
-            if t == 0 and lev == 1:
-                repeat_u(4, 6)
-                scores(4)
-                scores(5)
             if lev == 2:
-                if t == 0:
-                    repeat_u(6, 8)
-                    fill(A("one", 0, 516), 1.0)
-                    aff(A("eb", 0, 516), A("one", 0, 516), [[1, 516]], OP.is_equal, 0.0, -3, -4)
-                    for name in ("SIG", "TT", "COL"):
-                        n = SCRATCH[name][1][1]
-                        iota(A(name, 0, n), [[0, n]], 0)
                 scores(6)
                 scores(7)
+                if t == 0:
+                    const("wt6", 0, 520, 0.0)
+                    for a in range(4):
+                        const("wt6", 8 + 128 * a, 12 + 128 * a, 1.0 if a < 2 else -1.0, 1, 32 * a, 32 * a + 32)
+                else:
+                    const("G", 64, 576, 0.0)
             if lev == 3:
                 if t == 0:
-                    for b in range(4):
-                        quant(A("qe", 128 * b, 128 * b + 128), A("se", 128 * b, 128 * b + 128), A("eb", 3 - b, 515 - b))
-                    fill(AQ("QC", 2, 0, 1, 1, 2), float(QS))
-                    fill(AQ("QC", 2, 2, 3, 1, 2), 128.0)
+                    const("G", 0, 1024, 0.0)
+                    for name, a, b in (("CU5", 0, 128), ("TW", 128, 160), ("DT", 256, 288), ("QC", 0, 8)):
+                        const(name, a, b, 0.0)
+                    for h in range(2):
+                        act(A("MK", 8, 12, 1, 64 * h, 64 * h + 64), A("MT", 256, 384, 32, 64 * h, 64 * h + 64), 1.0 - 2.0 * h)
+                    const("QC", 0, 1, float(QS), 1, 64, 128)
+                    const("QC", 2, 3, 128.0, 1, 64, 128)
                     for a in (1, 3):
-                        fill(AQ("QC", a, 4, 5), float(HALF))
-                        fill(AQ("QC", a, 6, 7), 256.0)
-                    ts(A("CA", 0, 8), A("KF", 0, 8), col("h16"), OP.add, A("QC", 0, 1), OP.add)
-                    ts(A("KG", 0, 8), A("CA", 0, 8), A("QC", 4, 5), OP.add)
-                unpack(0)
+                        const("QC", 4, 5, float(HALF), 1, 32 * a, 32 * a + 32)
+                        const("QC", 6, 7, 256.0, 1, 32 * a, 32 * a + 32)
+                else:
+                    halves(0)
+                    act(now, ind(A("COL", 480 * t - 464, 480 * t - 16), A("PL", 0, 28)))
             if lev == 4:
-                unpack(1)
                 if t == 0:
-                    fill(A("wt7", 0, 776), 0.0)
-                    for a in range(4):
-                        fill(AQ("wt7", a, 264 + 128 * (a % 2), 268 + 128 * (a % 2)), -1.0 if a % 2 else 1.0)
-                    for m in range(4):
-                        tt(A("OFS", 8 * m, 8 * m + 8), A("KG", 0, 8), A("KL" if m < 2 else "KF", 0, 8), OP.subtract)
-                    quant(A("q7", 0, 194), A("s7", 0, 194), A("wt7", 0, 776))
+                    act(A("QC", 1, 2), col("h16"), bias=A("QC", 0, 1))
+                    halves(0)
+                    act(A("QC", 3, 4), A("QC", 1, 2), bias=A("QC", 4, 5))
+                halves(1)
+                if t == 0:
+                    act(A("QC", 5, 6), A("QC", 3, 4), bias=col("drop"))
             if lev == 5:
-                unpack(2)
-                unpack(3)
+                if t == 0:
+                    for m in range(2):
+                        act(A("OFS", 8 * m, 8 * m + 16), ind(A("DT", 0, 288), lst("two")), bias=A("QC", 5, 6))
+                    act(A("OFS", 16, 32), A("ZF", 0, 16), bias=A("QC", 3, 4))
+                    const("wt7", 0, 776, 0.0)
+                    for a in range(4):
+                        const("wt7", 264 + 128 * (a % 2), 268 + 128 * (a % 2), -1.0 if a % 2 else 1.0, 1, 32 * a, 32 * a + 32)
+                else:
+                    halves(2)
+                    halves(3)
+                if last:
+                    turn("COL", 480 * t)
             if lev == 6:
                 for m in range(3):
                     for a in range(4):
                         act(AQ("CK", m, 7 * BLOCK[a], 7 * BLOCK[a] + 7), AQ("Y", a, 8 * m, 8 * m + 7))
+                if t == 0:
+                    halves(2)
+                    first(6, 0)
+                if last:
+                    fetch("R2", "last", HALF + 16)
             if lev == 7:
                 if t == 0:
-                    act(A("COL", 16, 16 + C), ind(A("IOB", 0, C), A("PL", 0, 28)))
-                    quant(A("qv", 0, 128), A("pv", 0, 128), A("vt", 0, 512))
+                    halves(3)
+                    act(now, ind(A("IOB", 0, C), A("PL", 0, 28)))
 
         V = lambda n: A("TMP", 56 * n, 56 * n + 56)
         L = lambda n: A("TMP", 56 * n, 56 * n + 56, 2)
@@ -458,18 +528,14 @@ def rank_program(g, core, T, topo):
         four = lambda name, i: A(name, 16 + i, 128, 4)
         s0, s1 = [[A("BQ", QS * h + i, QS * h + QS, 2) for i in range(2)] for h in range(2)]
         tt(V(0), s0[1], s0[0], OP.is_lt)
-        if t == 0:
-            resets()
         ts(V(1), V(0), 2 * BIG, OP.mult, -BIG, OP.add)
         ts(V(2), V(0), -2 * BIG, OP.mult, BIG, OP.add)
-        cp(A("G0", 16, 128, 2), V(0))
-        ts(A("G0", 17, 128, 2), V(0), -1.0, OP.mult)
+        tt(A("G0", 16, 128, 2), A("PH", 0, QS, 2), V(0), OP.add)
         tt(V(3), s1[1], V(1), OP.min)
         tt(V(4), s1[0], V(2), OP.min)
-        tr(A("TX", 0, 128), A("G0", 16, 144))
+        tt(A("G0", 17, 128, 2), A("PH", 1, QS, 2), V(0), OP.subtract)
         tt(V(5), s1[0], V(3), OP.max)
         tt(V(6), s1[1], V(4), OP.max)
-        tr(A("TX", 128, 256), A("G0", 0, 128))
         tt(H(14), L(5), R(5), OP.is_gt)
         tt(H(15), L(5), R(6), OP.is_gt)
         tt(H(16), L(6), R(5), OP.is_gt)
@@ -482,45 +548,58 @@ def rank_program(g, core, T, topo):
         tt(four("GR", 3), H(19), H(17), OP.subtract)
         tt(four("GR", 1), H(20), H(17), OP.add)
         tt(four("GR", 2), H(21), H(16), OP.subtract)
-        tr(A("TW", 0, 128), A("GR", 16, 144))
-        tr(A("TW", 128, 256), A("GR", 0, 128))
-        tt(A("XH", 16, 32), ind(A("TW", 0, 288), lst("two")), A("KL", 0, 16), OP.add)
-        tt(A("XH", 0, 16), ind(A("TX", 0, 288), lst("two")), A("KL", 0, 16), OP.add)
-        cp(A("LL", 0, 7), A("XH", 16, 23))
-        background(1)
+        tr(A("TX", 0, 128), A("G0", 16, 144))
+        turn2("T1", "GR")
+        tr(A("TX", 128, 256), A("G0", 0, 128))
+        cp(A("LL", 0, 16), ind(A("T1", 0, 288), lst("two")))
+        cp(A("DB", 0, 256, 32), A("T1", 0, 256, 32))
+        act(A("LR", 16, 128), ind(A("LC", 0, 128), A("LL", 0, 7)))
+        act(A("MKL", 0, QS), ind(A("MP", 0, 128), A("LL", 0, 7)))
+        act(A("XH", 16, 32), ind(A("T1", 0, 288), lst("two")))
+        act(A("XH", 0, 16), ind(A("TX", 0, 288), lst("two")))
 
         for lev in range(2, 6):
             w = BLK[lev]
-            n = QS if lev == 5 else 128
-            scatter(A("CUR", 0, 128), A("LL", 0, 7), A("BQ", QS * lev, QS * lev + QS))
-            if lev == 4:
-                tt(A("XB", 0, 16), A("XH", 48, 64), A("DK", 0, 16), OP.add)
-            scan(A("KEY", 0, n), A("DR", 128 * (lev - 2), 128 * (lev - 2) + n), A("CUR", 0, n))
+            n, cur = (QS, "CU5") if lev == 5 else (128, "CUR")
+            scatter(A(cur, 0, 128), A("LL", 0, 7), A("BQ", QS * lev, QS * lev + QS))
+            once(lev, 0)
+            scan(A("KEY", 0, n), A("DR", 128 * (lev - 2), 128 * (lev - 2) + n), A(cur, 0, n))
+            once(lev, 1)
             one = lambda b: A("TQ", 32 * b, 32 * b + 1)
-            if lev < 4:
-                tr(A("TQ", 0, 128), A("KEY", 0, 128))
-                for b in range(4):
-                    for j in range(28 // w):
-                        a = 32 * b + w * j
-                        ts(A("MC", a, a + w), A("KEY", a, a + w), one(b), OP.is_lt if j % 2 else OP.is_gt, mask(("b%d" if lev == 2 else "c%d") % j), OP.mult)
-                cp(lane(0, 0, QS), ind(A("MC", 0, 128), A("LL", 0, 7)))
-            else:
+            if lev > 3:
                 act(A("KS", 0, QS), ind(A("KEY", 0, 128), A("LL", 0, 7)))
-                if lev == 4:
-                    tr(A("TQ", 0, 128), A("KEY", 0, 128))
-                    for b in range(4):
-                        ts(lane(0, w * b, w * b + w), A("KS", w * b, w * b + w), one(b ^ 1), OP.is_lt if b % 2 else OP.is_gt, mask("n28" if b % 2 else "p28"), OP.mult)
-                else:
-                    tr(A("TQ", 0, 64), A("KEY", 0, 64))
-                    tr(A("TQ", 64, 128), A("KEY", w, w + 64))
-                    for i, k in enumerate(("32", "24")):
-                        ts(lane(i, 0, w), A("KS", 0, w), one(2 + i), OP.is_gt, mask("p" + k), OP.mult)
-                        ts(lane(i, w, QS), A("KS", w, QS), one(i), OP.is_lt, mask("n" + k), OP.mult)
-            counts(lev)
-            background(lev)
-            places(lev, A("XB", 0, 16) if lev == 4 else A("XH", 16 * lev - 16, 16 * lev))
+            if lev == 2:
+                turn2("TL", "LR")
             if lev < 5:
-                cp(A("LL", 0, 7), A("XH", 16 * lev, 16 * lev + 7))
+                tr(A("TQ", 0, 128), A("KEY", 0, 128))
+            once(lev, 2)
+            if lev == 2:
+                cp(A("L2", 0, 16), ind(A("TL", 0, 288), lst("two")))
+                for b in range(4):
+                    for j in range(2):
+                        ts(A("MC", 128 * j + 32 * b, 128 * j + 32 * b + 28), A("KEY", 32 * b, 32 * b + 28), one(b), OP.is_lt if j else OP.is_gt)
+                tt(A("MB", 16, 128), ind(A("MC", 0, 256), A("L2", 0, 7)), A("MKL", 0, QS), OP.mult)
+            elif lev == 3:
+                for b in range(4):
+                    for j in range(2):
+                        a = 32 * b + w * j
+                        ts(A("MC", a, a + w), A("KEY", a, a + w), one(b), OP.is_lt if j else OP.is_gt, mask("c%d" % j), OP.mult)
+                cp(A("MB", 16, 128), ind(A("MC", 0, 128), A("LL", 0, 7)))
+            elif lev == 4:
+                for b in range(4):
+                    ts(A("MB", 16 + w * b, 16 + w * b + w), A("KS", w * b, w * b + w), one(b ^ 1), OP.is_lt if b % 2 else OP.is_gt, mask("n28" if b % 2 else "p28"), OP.mult)
+            else:
+                tr(A("TQ", 0, 64), A("KEY", 0, 64))
+                tr(A("TQ", 64, 128), A("KEY", w, w + 64))
+                for i, k in enumerate(("32", "24")):
+                    ts(lane(i, 0, w), A("KS", 0, w), one(2 + i), OP.is_gt, mask("p" + k), OP.mult)
+                    ts(lane(i, w, QS), A("KS", w, QS), one(i), OP.is_lt, mask("n" + k), OP.mult)
+            if lev < 5:
+                background(lev)
+                sums(lev, once)
+        counts(5)
+        background(5)
+        places(5, A("XH", 64, 80))
 
         ts(A("LL", 0, 7), A("XH", 80, 87), A("QC", 2, 3), OP.add)
         cp(A("LG", 0, 7), A("XH", 80, 87))
@@ -549,7 +628,9 @@ def rank_program(g, core, T, topo):
         act(A("KS", 0, HALF), ind(A("K7", 0, 256), A("LG", 0, 14)))
         for a in range(4):
             tr(AQ("TQ", a, 0, 128), AQ("K7", a ^ 1, 128 * (a // 2), 128 * (a // 2) + 128))
-        for b in range(4):
+        act(A("RG", 0, HALF), A("KS", 0, HALF), bias=A("TQ", 96, 97), func=AF.Sign)
+        act(lane(3, 0, HALF), A("RG", 0, HALF), func=AF.Relu)
+        for b in range(3):
             ts(lane(b, 0, HALF), A("KS", 0, HALF), A("TQ", 32 * b, 32 * b + 1), OP.add, 0.0, OP.is_gt)
         counts(7)
         background(7)
@@ -569,55 +650,69 @@ def rank_program(g, core, T, topo):
         quant(A(zc, 0, HALF), A(zs, 0, HALF), A("ZT", 0, 896))
 
         hazards("g", [(zc, 0, 128, 0, HALF, 1), (zs, 0, 128, 0, HALF, 1)], [])
-        for nm, hn, sn in ((zc, "hc%d" % t, "rc%d" % t), (zs, "hs%d" % t, "rs%d" % t)):
+        for k, (nm, hn) in enumerate(((zc, "hc%d" % t), (zs, "hs%d" % t))):
             tf = []
             for i in range(2):
-                rid, pid = topo.addr(rel[i], core)
+                rid, pid = topo.addr(rel[2 * k + i], core)
                 s_, d_ = T[nm][:, i * HALF // 2:(i + 1) * HALF // 2], T[hn][:, :]
                 if nm == zc:
                     s_, d_ = s_.bitcast(dt.uint8), d_.bitcast(dt.uint8)
-                tf.append(RemoteDMATransfer(dst_ids=[DstId(rid=rid, pnc=pid)], dma_engine_mask=_bits(cut[i]), remote_sem=T.sem[sn], src=s_, dst=d_))
+                tf.append(RemoteDMATransfer(dst_ids=[DstId(rid=rid, pnc=pid)], dma_engine_mask=_bits(cut[i]), remote_sem=T.sem["rc%d" % t], src=s_, dst=d_))
             g.remote_dma_fused(tf, local_sem=T.sem.snd)
 
-        ts(A("CA", 0, 28), A("RL", 0, 28), col("h16"), OP.subtract)
-        now = A("COL", 480 * t + 16, 480 * t + 16 + C)
-        if t < ROUNDS - 1:
+        if not last:
             fetch("PL", "last", HALF)
-        ts(A("CT", 0, 28), A("CA", 0, 28), float(HALF), OP.is_ge, -float(HALF), OP.mult)
-        if t < ROUNDS - 1:
+        ts(A("CA", 0, 28), A("RL", 0, 28), col("h16"), OP.subtract)
+        if not last:
             for a in range(3):
                 cp(AQ("PL", a, 0, 28), AQ("PL", 3, 0, 28))
-        tt(A("CA", 0, 28), A("CA", 0, 28), A("CT", 0, 28), OP.add)
-        cp(A("RM", 0, 28), A("CA", 0, 28))
-        if t < ROUNDS - 1:
-            act(A("COL", 480 * t + 496, 480 * t + 496 + C), ind(now, A("PL", 0, 28)))
-            act(A("G", 64, 576), A("one", 0, 512), 0.0)
-        if t == ROUNDS - 2:
-            turn("COL", 480 * t + 480)
-            fetch("R2", "last", HALF + 16)
-        if t == ROUNDS - 1:
+        ts(A("CT", 0, 28), A("CA", 0, 28), float(HALF), OP.is_ge, -float(HALF), OP.mult)
+        if not last:
+            qf, sf = "qf%d" % t, "sf%d" % t
+            cp(A("NI", 0, 28), A("PL", 0, 28))
+            for i in (0, 16):
+                tt(A("UW", i, 896, 32), A("CA", 0, 28), A("CT", 0, 28), OP.add)
+            ts(A("NA", 0, 28), A("NI", 0, 28), 496, OP.bitwise_and)
+            tr(A("UT", 0, C), A("UW", 0, C))
+            tt(A("NS", 0, 28), A("NI", 0, 28), A("NA", 0, 28), OP.add)
+            tr(A("UT", C, 896), A("UW", C, 896))
+            ts(A("NL", 0, 28), A("NS", 0, 28), col("h16"), OP.add)
+            pick(qf, sf, (0, C), qp, sp, C, A("PL", 0, 28))
+            act(A("RN", 16, 16 + C), ind(A("UT", 0, 896), A("NL", 0, 28)))
+            for b in range(4):
+                unpack(b, qf, sf)
+                if b < 2:
+                    act(A("FB", C * b, C * b + C), ps(DBANK[b], 0, C))
+            turn("RN", 0)
+            fetch("RM", "mine", 0)
+        else:
+            tt(A("CA", 0, 28), A("CA", 0, 28), A("CT", 0, 28), OP.add)
             act(A("OD", 0, C), ind(now, A("ZL", 0, 28)), bias=col("h224"))
             dmas("y", [(ext(T.od[h:h + 1, :]), A("OD", 0, C, 1, 16 * h, 16 * h + 1)) for h in range(8)], "dd")
             scatter(A("SIG", 0, 480), A("R2", 0, 28), A("IOB", 0, C))
+            cp(A("RM", 0, 28), A("CA", 0, 28))
             turn("SIG", 0)
             fetch("IC", "last", HALF)
 
         lc, ls = "lc%d" % t, "ls%d" % t
         wait("t", "lz%d" % t, landed)
-        for b in (2, 0, 3, 1):
+        for b in (0, 1, 2, 3):
             mm(ps(PBANK[b], 0, HALF), A("wq", 128 * b, 128 * b + 128), A("wp", 128 * b, 128 * b + 128), A(lc, 0, HALF), A(ls, 0, HALF))
-            if b > 1:
+            if b:
                 act(A("PB", HALF * b, HALF * b + HALF), ps(PBANK[b], 0, HALF), 0.03125)
             else:
                 ts(A("PB", HALF * b, HALF * b + HALF), ps(PBANK[b], 0, HALF), 0.03125, OP.mult)
-        for b in (2, 3):
-            act(A("RG", C * (b - 2), C * (b - 1)), ind(A("PB", HALF * b, HALF * b + HALF), A("RM", 0, 28)))
+        act(A("RG", 0, C), ind(A("PB", 2 * HALF, 3 * HALF), A("RM", 0, 28)))
+        for i in range(2):
+            act(A("RG", C + HALF * i, C + HALF * i + HALF), ind(A("PB", 3 * HALF, 4 * HALF), A("RM", 14 * i, 14 * i + 14)))
         for b in (0, 1):
             tt(A("xn", b, 1792, 4), ind(A("PB", HALF * b, HALF * b + HALF), A("RM", 0, 28)), A("FB", C * b, C * b + C), OP.add)
-        for b in (2, 3):
-            tt(A("xn", b, 1792, 4), A("RG", C * (b - 2), C * (b - 1)), ps(DBANK[b], 0, C), OP.add)
+        tt(A("xn", 2, 1792, 4), A("RG", 0, C), ps(DBANK[2], 0, C), OP.add)
+        for i in range(2):
+            tt(A("xn", 896 * i + 3, 896 * i + 896, 4), A("RG", C + HALF * i, C + HALF * i + HALF), ps(DBANK[3], HALF * i, HALF * i + HALF), OP.add)
 
-    quant(A("qx3", 0, C), A("sx3", 0, C), A("xn", 0, 1792))
+    for i in range(2):
+        quant(A("qx3", HALF * i, HALF * i + HALF), A("sx3", HALF * i, HALF * i + HALF), A("xn", 896 * i, 896 * i + 896))
     for i in range(2):
         o = (HALF * i, HALF * i + HALF)
         pick("qp3", "sp3", o, "qx3", "sx3", C, A("IC", 14 * i, 14 * i + 14))

@@ -5,6 +5,7 @@ OP = AluOpType
 AF = ActivationFunctionType
 ROUNDS, C, HALF, QS = 3, 448, 224, 112
 BIG = 1e29
+SAME = False
 LIFT = 64
 BLOCK = (0, 2, 1, 3)
 
@@ -22,23 +23,23 @@ def _mx(c, s, n):
 
 PARTS = {}
 _z = 0
-for _n, _w in (("MB", 144), ("GR", 144), ("G0", 144), ("LR", 144), ("DKR", 144), ("MP", 128), ("LC", 128), ("T1", 288), ("TX", 288), ("TL", 288), ("CS", 288)):
+for _n, _w in (("MB", 144), ("GR", 144), ("G0", 144), ("LR", 144), ("DKR", 144), ("MB1", 144), ("MP", 128), ("LC", 128), ("T1", 288), ("TX", 288), ("TL", 288), ("CS", 288)):
     PARTS[_n] = ("Z", _z)
     _z += _w
-for _k, _n in enumerate(("MK", "QC", "KF", "KL", "DK", "KG", "OFS", "Y", "CK", "CA", "CT", "NS")):
+for _k, _n in enumerate(("MK", "QC", "OFS", "Y", "CK", "CA", "CT", "NS")):
     PARTS[_n] = ("S", 32 * _k)
-for _n, _w in (("Z", _z), ("xt", 1792), ("xn", 1792), ("ut", 512), ("vt", 512), ("one", 516), ("eb", 516), ("wt6", 520), ("wt7", 776), ("G", 1024),
-               ("FB", 896), ("HB", 1792), ("ZT", 896), ("IOB", C), ("SIG", 480), ("TT", 992), ("COL", 3 * 480), ("MR", 384), ("MT", 384),
-               ("PH", QS), ("MKL", QS), ("TB", 256), ("DB", 256), ("DT", 288), ("UW", 896), ("UT", 896), ("RN", 480)):
+for _n, _w in (("Z", _z), ("xt", 1792), ("xn", 1792), ("ut", 512), ("vt", 512), ("one", 516), ("eb", 516), ("wt6", 520), ("wt7", 776), ("G", 1088),
+               ("FB", 896), ("HB", 1792), ("ZT", 896), ("IOB", C), ("SIG", 480), ("TT", 1024), ("COL", 3 * 480), ("MR", 320), ("MT", 320),
+               ("PH", QS), ("MKL", QS), ("TB", 512), ("DB", 256), ("D5", 512), ("C5", 576), ("DT", 288), ("UW", 896), ("UT", 896), ("RN", 480)):
     _sb(_n, _w, "bfloat16")
-for _n, _w in (("RW", 512), ("CL", 512), ("S", 384), ("BQ", 7 * QS),
+for _n, _w in (("RW", 544), ("CL", 544), ("K5", 128), ("S", 256), ("PR", 2 * QS), ("BQ", 7 * QS),
                ("B7", HALF), ("CUR", 128), ("CU5", 128), ("KEY", 128), ("KS", HALF), ("TQ", 128), ("MC", 256), ("TMP", 800), ("DR", 512),
                ("TW", 160), ("XH", 128), ("XB", 48), ("W6", 256), ("K6", 128), ("W7", 512), ("K7", 256),
                ("ZF", 512), ("OD", C), ("GZ", 896), ("PB", 896), ("RG", 2 * C), ("yb", C)):
     _sb(_n, _w)
-for _n, _w in (("pi", 28), ("ii", 16), ("ML", 16), ("NI", 28), ("NA", 28)):
+for _n, _w in (("pi", 28), ("ii", 16), ("NI", 28), ("NA", 28)):
     _sb(_n, _w, "int32")
-for _n, _w in (("LS", 16), ("LL", 16), ("L2", 16), ("LG", 14), ("LH", 14), ("RL", 28), ("RM", 32), ("R2", 32), ("ZL", 32), ("PL", 32), ("IC", 32),
+for _n, _w in (("LS", 20), ("LL", 16), ("L2", 16), ("LG", 16), ("LH", 14), ("RL", 28), ("RM", 32), ("R2", 32), ("ZL", 32), ("PL", 32), ("IC", 32),
                ("UL", 16), ("NL", 28)):
     _sb(_n, _w, "uint16")
 _mx("qu", "su", 128)
@@ -48,18 +49,19 @@ _mx("wq", "wp", 512)
 _mx("q6", "s6", 130)
 _mx("q7", "s7", 194)
 _mx("qe", "se", 512)
-_mx("qa", "sa", 256)
+_mx("qa", "sa", 272)
 for _t in range(ROUNDS + 1):
     _mx("qx%d" % _t, "sx%d" % _t, C)
-for _n in ("p0", "p3", "f0", "f1"):
+for _n in ("p0", "f0", "f1", "f2"):
     _mx("q" + _n, "s" + _n, C)
 for _t in range(ROUNDS):
     _mx("zc%d" % _t, "zs%d" % _t, HALF)
     _mx("lc%d" % _t, "ls%d" % _t, HALF)
-    _mx("hc%d" % _t, "hs%d" % _t, HALF // 2)
+    _sb("hc%d" % _t, QS, "float8_e4m3fn_x4")
+    _sb("hs%d" % _t, HALF, "uint8")
 SCRATCH["ps"] = ("psum", [128, 4096], "float32")
 
-SEMAPHORES = (["sv", "st", "ss", "sg", "snd", "dx", "dx2", "dp", "du", "dw", "dv", "dy", "dy2", "dc", "dd", "dq"]
+SEMAPHORES = (["sv", "st", "ss", "sg", "snd", "dx", "dx2", "dp", "du", "dw", "dv", "dy0", "dy1", "dc0", "dc1", "dd", "dq"]
               + ["%s%d" % (_a, _t) for _a in ("rc", "lz") for _t in range(ROUNDS)])
 
 
@@ -67,7 +69,7 @@ def _relays(topo, src, dst):
     ok = [c for c in topo.cores_of(src) if c != src and topo.may_write(c, dst)]
     near = [c for c in ok if topo.die(c) == topo.die(src)]
     far = [c for c in ok if topo.die(c) != topo.die(src)]
-    return [near[0], far[0], near[1], far[1]]
+    return [near[0], far[0], near[1]]
 
 
 def _bits(engines):
@@ -85,17 +87,16 @@ def _relay_program(g, core, T, topo):
         if core not in rel:
             continue
         h = rel.index(core)
-        a, b = h % 2 * HALF // 2, (h % 2 + 1) * HALF // 2
         rid, pid = topo.addr(dst, core)
         m = topo.mask(core, dst)
         k = len(topo.engines(core, dst))
-        half = len(topo.engines(T.cores[r], core)) // 2
+        came = len(topo.engines(T.cores[r], core)) // (2 if h < 2 else 1)
         for t in range(ROUNDS):
-            g.wait_ge(T.sem["rc%d" % t], half)
+            g.wait_ge(T.sem["rc%d" % t], came)
             if h < 2:
-                g.remote_dma(T["lc%d" % t][:, a:b].bitcast(dt.uint8), T["hc%d" % t][:, :].bitcast(dt.uint8), T.sem["lz%d" % t], T.sem.snd, pid, rid, m)
+                g.remote_dma(T["lc%d" % t][:, h * QS:(h + 1) * QS].bitcast(dt.uint8), T["hc%d" % t][:, :].bitcast(dt.uint8), T.sem["lz%d" % t], T.sem.snd, pid, rid, m)
             else:
-                g.remote_dma(T["ls%d" % t][:, a:b], T["hs%d" % t][:, :], T.sem["lz%d" % t], T.sem.snd, pid, rid, m)
+                g.remote_dma(T["ls%d" % t][:, :], T["hs%d" % t][:, :], T.sem["lz%d" % t], T.sem.snd, pid, rid, m)
         g.wait_ge(T.sem.snd, k * ROUNDS)
 
 
@@ -123,6 +124,9 @@ def rank_program(g, core, T, topo):
     def AQ(name, a, c0, c1, st=1, n=1):
         return A(name, c0, c1, st, 32 * a, 32 * (a + n))
 
+    def back(name, c0, c1):
+        return (T[name][:, c1 - 1:c0 - 1:-1] if c0 else T[name][:, c1 - 1::-1], [(name, 0, 128, c0, c1, 1)])
+
     def ps(bank, c0, c1, st=1, p0=0, p1=128):
         x = A("ps", 512 * bank + c0, 512 * bank + c1, st, p0, p1)
         return (x[0], [("ps%d" % bank, 0, 128, 0, 512, 1)])
@@ -136,10 +140,14 @@ def rank_program(g, core, T, topo):
     def u32(x):
         return (x[0].bitcast(dt.uint32), x[1])
 
+    known = {}
+
     def wait(q, sem, val):
         if seen.get((q, sem), 0) < val:
             Q[q].wait_ge(T.sem[sem], val)
             seen[(q, sem)] = val
+            for s, v in known.get((sem, val), ()):
+                seen[(q, s)] = max(seen.get((q, s), 0), v)
 
     def hazards(q, reads, writes):
         need = {}
@@ -155,8 +163,10 @@ def rank_program(g, core, T, topo):
                         continue
                     if not bank and not w and not ew:
                         continue
+                    if eq == q and w and SAME:
+                        continue
                     need[sem] = max(need.get(sem, 0), val)
-        for sem in need:
+        for sem in sorted(need, key=lambda s: -len(known.get((s, need[s]), ()))):
             wait(q, sem, need[sem])
 
     def note(q, sem, val, reads, writes):
@@ -176,6 +186,7 @@ def rank_program(g, core, T, topo):
         sem = ESEM[q]
         count[sem] += 1
         call().then_inc(T.sem[sem], 1)
+        known[(sem, count[sem])] = [(k[1], seen[k]) for k in seen if k[0] == q]
         note(q, sem, count[sem], reads, writes)
 
     def dmas(q, pairs, sem):
@@ -210,10 +221,13 @@ def rank_program(g, core, T, topo):
         else:
             do("s", lambda: g.scalar.activation(out[0], a[0], AF.Copy, scale=scale), [out], [a])
 
-    def pick(qo, so, o, qi, si, w, off):
-        act(A(so, *o), ind(A(si, 0, w), off))
+    def codes(qo, o, qi, w, off):
         src = A(qi, 0, w)
         do("v", lambda: g.vector.tensor_copy(u32(A(qo, *o))[0], u32(src)[0].indirect(off[0])), [A(qo, *o)], [src, off])
+
+    def pick(qo, so, o, qi, si, w, off):
+        act(A(so, *o), ind(A(si, 0, w), off))
+        codes(qo, o, qi, w, off)
 
     def scatter(win, off, vals):
         do("v", lambda: g.vector.tensor_copy(win[0].indirect(off[0]), vals[0]), [win], [vals, off])
@@ -267,9 +281,13 @@ def rank_program(g, core, T, topo):
             "upper": (6, [([[0, 16]], 1), ([[0, 2], [32, 4], [-2, 2]], 2)]),
             "none": (7, [([[0, 32]], 0)]),
             "pairs": (8, [([[16, 2], [32, 2], [1, 8]], 64 * k) for k in range(2)]),
-            "own": (10, [([[16, 2], [32, 8], [480, 2]], 256 * k) for k in range(2)]),
-            "last": (12, [x for k in range(2) for x in (([[32, 8], [-448, 2]], 496 + 256 * k), ([[32, 8], [480, 2]], 16 + 256 * k))]),
-            "mine": (14, [x for k in range(2) for x in (([[32, 8], [-448, 2]], 480 + 256 * k), ([[32, 8], [480, 2]], 16 + 256 * k))])}
+            "own": (10, [([[16, 2], [32, 8], [256, 2]], 0)]),
+            "gap": (11, [([[0, 32]], 0)]),
+            "last": (12, [([[32, 8], [-224, 2]], 272), ([[32, 8], [256, 2]], 16)]),
+            "gap2": (13, [([[0, 32]], 0)]),
+            "mine": (14, [([[32, 8], [-224, 2]], 256), ([[32, 8], [256, 2]], 16)]),
+            "gap3": (15, [([[0, 32]], 0)]),
+            "wide": (16, [([[0, 2], [64, 4], [320, 2]], 63), ([[0, 2], [64, 4], [-256, 2]], 319)])}
 
     def rows(names):
         for k in names:
@@ -281,10 +299,6 @@ def rank_program(g, core, T, topo):
                 iota(A("RW", c0, c0 + n), pattern, base)
                 c0 += n
 
-    def lists(j0, j1):
-        tr(A("CL", 32 * j0, 32 * j1), A("RW", 32 * j0, 32 * j1))
-        cp(A("LS", j0, j1), A("CL", 32 * j0, 32 * j1, 32))
-
     def lst(k, n=1):
         return A("LS", ROWS[k][0], ROWS[k][0] + n)
 
@@ -293,13 +307,16 @@ def rank_program(g, core, T, topo):
         return A("CL", j, j + 1, 1, p0, p1)
 
     MASKS = {"b0": (0, 7, 14, 1.0), "b1": (1, 0, 7, -1.0), "b2": (2, 21, 28, 1.0), "b3": (3, 14, 21, -1.0), "c0": (4, 14, 28, 1.0), "c1": (5, 0, 14, -1.0),
-             "p28": (6, 0, 28, 1.0), "n28": (7, 0, 28, -1.0), "p32": (8, 0, 32, 1.0), "n32": (9, 0, 32, -1.0), "p24": (10, 0, 24, 1.0), "n24": (11, 0, 24, -1.0)}
+             "p28": (6, 0, 28, 1.0), "n28": (7, 0, 28, -1.0), "p24": (8, 0, 24, 1.0), "n24": (9, 8, 32, -1.0)}
 
     def mask(k):
         j = MASKS[k][0]
         return A("MK", j, j + 1)
 
-    for a, b in ((0, 16), (128, 160), (272, 304), (416, 448), (560, 592), (704, 976)):
+    def zero(name, a, b):
+        iota(A(name, a, b), [[0, b - a]], 0)
+
+    for a, b in ((0, 16), (128, 160), (272, 304), (416, 448), (560, 592), (704, 736), (848, 1120)):
         fill(A("Z", a, b), 0.0)
     iota(A("ii", 0, 16), [[16, 8], [0, 2]], 0)
     iota(A("one", 0, 516), [[0, 516]], 1)
@@ -307,65 +324,92 @@ def rank_program(g, core, T, topo):
     iota(A("PH", 0, QS), [[32, 4], [1, 28]], 0)
     for b in range(4):
         iota(A("LC", 32 * b, 32 * b + 28), [[14, 2], [135, 2], [1, 7]], 32 * b)
-    iota(A("MC", 0, 256), [[0, 256]], 0)
-    iota(A("XH", 0, 128), [[0, 128]], 0)
+    for name in ("T1", "TX", "TL", "CS", "DT"):
+        zero(name, 256, 288)
+    zero("MC", 0, 256)
     iota(A("DKR", 16, 128), [[-4, 4], [0, 28]], LIFT)
+    zero("XH", 0, 128)
     aff(A("eb", 0, 516), A("one", 0, 516), [[1, 516]], OP.is_equal, 0.0, -3, -4)
-    rows(("one", "h224", "upper", "none", "pairs", "own", "last", "mine"))
-    iota(A("ZF", 0, 260), [[0, 260]], 0)
+    rows(("one", "h224", "upper", "none", "pairs", "own", "gap", "last", "gap2", "mine", "gap3", "wide"))
+    for name, a, b in (("QC", 0, 8), ("CU5", 0, 128), ("C5", 512, 576), ("wt6", 0, 520), ("TW", 128, 160), ("ZF", 0, 260)):
+        zero(name, a, b)
     never("W6", 0, 129, -BIG)
     never("W6", 129, 256, BIG)
     never("K6", 0, 128, -BIG)
-    iota(A("IOB", 0, C), [[1, C]], -HALF)
+    zero("wt7", 0, 776)
+    zero("G", 576, 1088)
     never("W7", 0, 257, -BIG)
     never("W7", 257, 512, BIG)
-    never("K7", 0, 256, -BIG)
-    for name in ("SIG", "TT", "RN", "UW", "COL"):
-        iota(A(name, 0, SCRATCH[name][1][1]), [[0, SCRATCH[name][1][1]]], 0)
+    zero("K7", HALF, 256)
+    iota(A("IOB", 0, C), [[1, C]], -HALF)
+    for name, a, b in (("SIG", 0, 16), ("SIG", C, 480), ("TT", 480, 512), ("TT", 992, 1024), ("RN", 0, 16), ("RN", 464, 480),
+                       ("COL", 960, 976), ("COL", 1424, 1440), ("UW", 0, 896)):
+        zero(name, a, b)
 
-    fill(A("MR", 0, 384), 0.0)
+    fill(A("MR", 0, 320), 0.0)
     cp(A("UL", 0, 16), A("ii", 0, 16))
     for k in MASKS:
         j, a, b, val = MASKS[k]
         fill(A("MR", 32 * j + a, 32 * j + b), val)
     fill(A("MR", 32 * 6 + 31, 32 * 8, 32), -float(LIFT))
-    for a in range(4):
-        cp(AQ("PL", a, 0, 28), AQ("pi", 0, 0, 28))
-    tr(A("MT", 0, 384), A("MR", 0, 384))
+    fill(A("MR", 32 * 8 + 31, 32 * 9 + 1), -float(QS))
+    tr(A("MT", 0, 320), A("MR", 0, 320))
     fill(A("DB", 0, 256), -BIG)
-    cp(A("MK", 0, 8), A("MT", 0, 256, 32))
-    quant(A("qu", 0, 128), A("su", 0, 128), A("ut", 0, 512))
-    for j in range(4):
-        ts(A("MP", 7 * j, 7 * j + 7), A("one", 0, 7), mask("b%d" % j), OP.mult)
+    cp(A("MK", 0, 10), A("MT", 0, 320, 32))
     const("DR", 0, 512, BIG)
     const("CUR", 0, 128, 0.0)
-    for name in ("T1", "TX", "TL", "CS"):
-        const(name, 256, 288, 0.0)
-    for a, b, st in ((0, 128, 32), (7, 128, 32), (14, 256, 32), (21, 128, 32), (128, 384, 32), (256 + 63, 384, 64), (384, 496, 56)):
-        const("DR", a, b, -BIG, st)
-    const("CUR", 31, 128, BIG, 64)
-    const("CUR", 63, 128, -BIG, 64)
-    pick("qB", "sB", (0, 256), "qu", "su", 128, A("UL", 0, 16))
+    const("PR", 0, 2 * QS, -BIG)
 
-    def first(lev, point):
-        key = (lev, point)
-        if key == (2, 0):
-            turn2("DT", "DKR")
-        if key == (3, 0):
-            quant(A("q6", 0, 130), A("s6", 0, 130), A("wt6", 0, 520))
-        if lev == 3 and point > 0:
-            b = point - 1
-            quant(A("qe", 128 * b, 128 * b + 128), A("se", 128 * b, 128 * b + 128), A("eb", 3 - b, 515 - b))
-        if lev == 4 and point in (0, 3, 4):
-            j = 4 + 4 * (0, 0, 0, 1, 2)[point]
-            tr(A("CL", 32 * j, 32 * j + 128), A("RW", 32 * j, 32 * j + 128))
-        if key == (4, 2):
-            quant(A("qa", 0, 256), A("sa", 0, 256), A("G", 0, 1024))
-        if key == (5, 0):
-            cp(A("LS", 4, 16), A("CL", 128, 512, 32))
-        if key == (6, 0):
-            quant(A("q7", 0, 194), A("s7", 0, 194), A("wt7", 0, 776))
-            quant(A("qv", 0, 128), A("pv", 0, 128), A("vt", 0, 512))
+    todo = []
+
+    def later(ns, f, *args):
+        todo.append((ns, lambda: f(*args)))
+
+    def first(ns=150):
+        while todo and todo[0][0] <= ns:
+            ns -= max(todo[0][0], 1)
+            todo.pop(0)[1]()
+
+    for a, b, st in ((0, 128, 32), (7, 128, 32), (14, 256, 32), (21, 128, 32)):
+        later(60, fill, A("DR", a, b, st), -BIG)
+    later(60, tr, A("DT", 0, 128), A("DKR", 16, 144))
+    later(60, tr, A("DT", 128, 256), A("DKR", 0, 128))
+    later(60, fill, A("CUR", 31, 128, 64), BIG)
+    later(60, fill, A("CUR", 63, 128, 64), -BIG)
+    later(60, fill, A("DR", 128, 384, 32), -BIG)
+    later(60, fill, A("DR", 256 + 63, 384, 64), -BIG)
+    later(60, fill, A("DR", 384, 496, 56), -BIG)
+    later(60, fill, A("K5", 0, 8), BIG)
+    later(60, fill, A("K5", 120, 128), -BIG)
+    for b in range(4):
+        later(140, quant, A("qe", 128 * b, 128 * b + 128), A("se", 128 * b, 128 * b + 128), A("eb", 3 - b, 515 - b))
+    for c0 in range(128, 544, 128):
+        later(120, tr, A("CL", c0, min(c0 + 128, 544)), A("RW", c0, min(c0 + 128, 544)))
+    later(60, fill, AQ("QC", 2, 0, 1, 1, 2), float(QS))
+    later(60, fill, AQ("QC", 2, 2, 3, 1, 2), 128.0)
+    later(60, cp, A("LS", 4, 17), A("CL", 128, 544, 32))
+    for a in (1, 3):
+        later(60, fill, AQ("QC", a, 4, 5), float(HALF))
+        later(60, fill, AQ("QC", a, 6, 7), 256.0)
+
+    def weights(lev):
+        if lev == 6:
+            for a in range(4):
+                later(60, fill, AQ("wt6", a, 8 + 128 * a, 12 + 128 * a), 1.0 if a < 2 else -1.0)
+            later(140, quant, A("qa", 0, 128), A("sa", 0, 128), A("G", 0, 512))
+            later(140, quant, A("q6", 0, 130), A("s6", 0, 130), A("wt6", 0, 520))
+            later(140, quant, A("qv", 0, 128), A("pv", 0, 128), A("vt", 0, 512))
+            return
+        for a in range(4):
+            later(60, fill, AQ("wt7", a, 264 + 128 * (a % 2), 268 + 128 * (a % 2) - a // 2), -1.0 if a % 2 else 1.0)
+        later(200, quant, A("q7", 0, 194), A("s7", 0, 194), A("wt7", 0, 776))
+
+    for j in range(4):
+        ts(A("MP", 7 * j, 7 * j + 7), A("one", 0, 7), mask("b%d" % j), OP.mult)
+    quant(A("qu", 0, 128), A("su", 0, 128), A("ut", 0, 512))
+    for a in range(4):
+        cp(AQ("PL", a, 0, 28), AQ("pi", 0, 0, 28))
+    pick("qB", "sB", (0, 256), "qu", "su", 128, A("UL", 0, 16))
 
     LB = 4
 
@@ -373,36 +417,56 @@ def rank_program(g, core, T, topo):
         tr(A(out, 0, 128), A(row, 16, 144))
         tr(A(out, 128, 256), A(row, 0, 128))
 
-    def sums(lev, once):
-        once(lev, 3)
-        turn2("TB", "MB")
-        once(lev, 4)
-        for c0 in (0, 128):
-            scan(A("CS", c0, c0 + 128), A("DB", c0, c0 + 128), A("TB", c0, c0 + 128), -BIG, OP.max, OP.add)
-        cp(A("LL", 0, 16), ind(A("CS", 0, 288), lst("end")))
+    def sums(lev):
+        first()
+        if lev < 5:
+            turn2("TB", "MB")
+            first()
+            for c0 in (0, 128):
+                scan(A("CS", c0, c0 + 128), A("DB", c0, c0 + 128), A("TB", c0, c0 + 128), -BIG, OP.max, OP.add)
+            new = ind(A("CS", 0, 288), lst("end"))
+            first()
+            cp(A("LL", 0, 16), new)
+        else:
+            for c0, r0 in ((0, 16), (256, 0)):
+                for i, row in enumerate(("MB", "MB1")):
+                    tr(A("TB", c0 + i, c0 + 256, 2), A(row, r0, r0 + 128))
+            for c0 in (0, 256):
+                scan(A("C5", c0, c0 + 256), A("D5", c0, c0 + 256), A("TB", c0, c0 + 256), -BIG, OP.max, OP.add)
+            new = ind(A("C5", 0, 576), lst("wide"))
+            first()
+            ts(A("LL", 0, 16), new, A("QC", 2, 3), OP.add)
+            cp(A("LG", 0, 16), new)
+            act(A("XB", 16, 32), new, bias=A("QC", 0, 1))
         if lev == 2:
             cp(A("DB", 0, 256, 32), A("CS", 31, 256, 32))
         if lev == 3:
             tt(A("DB", 0, 256, 32), A("CS", 31, 256, 32), A("DT", 0, 256, 32), OP.add)
-        act(A("XH", 16 * lev, 16 * lev + 16), ind(A("CS", 0, 288), lst("end")))
+        if lev == 4:
+            ts(A("D5", 0, 512, 64), A("CS", 31, 256, 32), float(QS), OP.add)
+        act(A("XH", 16 * lev, 16 * lev + 16), new)
 
     def counts(lev):
-        n = HALF if lev == 7 else 128
-        quant(A("qa", 16, 16 + n), A("sa", 16, 16 + n), A("G", 64, 64 + 4 * n))
+        for c0 in (16, 144) if lev == 7 else (16,):
+            quant(A("qa", c0, c0 + 128), A("sa", c0, c0 + 128), A("G", 4 * c0, 4 * c0 + 512))
         views = (("q7", "s7", 66, 16), ("q7", "s7", 64, 0), ("q7", "s7", 2, 128), ("q7", "s7", 0, QS)) if lev == 7 else (("q6", "s6", 2, 16), ("q6", "s6", 0, 0))
         for i, (w, ws, a, b) in enumerate(views):
             mm(ps(LB, 0, 128), A(w, a, a + 128), A(ws, a, a + 128), A("qa", b, b + 128), A("sa", b, b + 128), i == 0, i == len(views) - 1)
 
     def places(lev, base):
-        tr(A("TW", 0, 128), ps(LB, 0, 128))
         tt(A("XH", 16 * lev, 16 * lev + 16), ind(A("TW", 0, 160), lst("upper" if lev == 7 else "one")), base, OP.add)
 
-    def turn(row, c0):
-        tr(A("TT", 0, 480), A(row, c0, c0 + 480))
-        tr(A("TT", 480, 480 + C), A(row, c0 + 16, c0 + 16 + C))
+    def turn(row, c0, halves=(0, 1)):
+        for i in halves:
+            tr(A("TT", 512 * i, 512 * i + 256), A(row, c0 + HALF * i, c0 + HALF * i + 256))
+            tr(A("TT", 512 * i + 256, 512 * i + 480), A(row, c0 + HALF * i + 16, c0 + HALF * i + 240))
 
-    def fetch(dst, k, add):
-        ts(A(dst, 0, 32), ind(A("TT", 0, 992), lst(k, 2)), float(add), OP.add)
+    def fetch(dst, k, add, halves=(0, 1), step=14):
+        for i in halves:
+            ts(A(dst, step * i, step * i + 16), ind(A("TT", 512 * i, 512 * i + 512), lst(k)), float(add), OP.add)
+
+    def slots(c0, c1):
+        scatter(A("RN", 0, 480), A("R2", c0, c1), A("IOB", 16 * c0, 16 * c1))
 
     def lane(t, a, b):
         return A("G", 64 + 4 * a + t, 64 + 4 * b, 4)
@@ -422,17 +486,15 @@ def rank_program(g, core, T, topo):
         qp, sp = (qx, sx) if t else ("qp0", "sp0")
         for i in range(2):
             quant(A(qx, HALF * i, HALF * i + HALF), A(sx, HALF * i, HALF * i + HALF), A("xn" if t else "xt", 896 * i, 896 * i + 896))
+        if t == 0:
+            tr(A("CL", 0, 128), A("RW", 0, 128))
+            cp(A("MP", 32, 64), A("MP", 0, 32))
         for i in range(2):
             o = (HALF * i, HALF * i + HALF)
             if t == 0:
                 pick(qp, sp, o, qx, sx, C, A("PL", 14 * i, 14 * i + 14))
             mm(ps(i, 0, HALF), A("qB", 0, 128), A("sB", 0, 128), A(qp, *o), A(sp, *o))
         mm(ps(5, 0, C), A("qB", 128, 256), A("sB", 128, 256), A(qp, 0, C), A(sp, 0, C))
-        if t == 0:
-            cp(A("MP", 32, 64), A("MP", 0, 32))
-            lists(0, 4)
-            cp(A("MP", 64, 128), A("MP", 0, 64))
-        once = first if t == 0 else (lambda lev, point: None)
 
         def scores(h, blocks=range(4), by=act):
             p = (32 * (h % 4), 32 * (h % 4) + 32)
@@ -451,95 +513,72 @@ def rank_program(g, core, T, topo):
         def halves(b):
             unpack(b, qp, sp)
             act(A("HB", C * b, C * b + C), ps(DBANK[b], 0, C), 0.5)
-            if last and b < 2:
-                act(A("FB", C * b, C * b + C), ps(DBANK[b], 0, C))
 
-        for h in range(2):
-            scores(h, (0, 1))
-            scores(h, (2, 3), cp)
-        for h in range(2, 6):
-            scores(h)
+        scores(0, (0, 1), cp)
+        if t == 0:
+            cp(A("LS", 0, 4), A("CL", 0, 128, 32))
+            cp(A("MP", 64, 128), A("MP", 0, 64))
+            first(120)
+        scores(0, (2, 3), cp)
+        scores(1, (0, 1))
+        scores(1, (2,), cp)
         now = A("COL", 480 * t + 16, 480 * t + 16 + C)
 
         def background(lev):
             if lev == 2:
-                scores(6)
-                scores(7)
-                if t == 0:
-                    const("wt6", 0, 520, 0.0)
-                    for a in range(4):
-                        const("wt6", 8 + 128 * a, 12 + 128 * a, 1.0 if a < 2 else -1.0, 1, 32 * a, 32 * a + 32)
-                else:
-                    const("G", 64, 576, 0.0)
+                scores(3)
+                scores(4)
             if lev == 3:
+                scores(5)
                 if t == 0:
-                    const("G", 0, 1024, 0.0)
-                    for name, a, b in (("CU5", 0, 128), ("TW", 128, 160), ("DT", 256, 288), ("QC", 0, 8)):
-                        const(name, a, b, 0.0)
-                    for h in range(2):
-                        act(A("MK", 8, 12, 1, 64 * h, 64 * h + 64), A("MT", 256, 384, 32, 64 * h, 64 * h + 64), 1.0 - 2.0 * h)
-                    const("QC", 0, 1, float(QS), 1, 64, 128)
-                    const("QC", 2, 3, 128.0, 1, 64, 128)
-                    for a in (1, 3):
-                        const("QC", 4, 5, float(HALF), 1, 32 * a, 32 * a + 32)
-                        const("QC", 6, 7, 256.0, 1, 32 * a, 32 * a + 32)
+                    const("D5", 0, 512, -BIG)
+                    const("G", 0, 576, 0.0)
                 else:
-                    halves(0)
                     act(now, ind(A("COL", 480 * t - 464, 480 * t - 16), A("PL", 0, 28)))
             if lev == 4:
-                if t == 0:
-                    act(A("QC", 1, 2), col("h16"), bias=A("QC", 0, 1))
-                    halves(0)
-                    act(A("QC", 3, 4), A("QC", 1, 2), bias=A("QC", 4, 5))
-                halves(1)
-                if t == 0:
-                    act(A("QC", 5, 6), A("QC", 3, 4), bias=col("drop"))
+                scores(6)
             if lev == 5:
                 if t == 0:
+                    act(A("QC", 1, 2), col("h16"), bias=A("QC", 0, 1))
+                    act(A("QC", 3, 4), A("QC", 1, 2), bias=A("QC", 4, 5))
+                    act(A("QC", 5, 6), A("QC", 3, 4), bias=col("drop"))
                     for m in range(2):
                         act(A("OFS", 8 * m, 8 * m + 16), ind(A("DT", 0, 288), lst("two")), bias=A("QC", 5, 6))
                     act(A("OFS", 16, 32), A("ZF", 0, 16), bias=A("QC", 3, 4))
-                    const("wt7", 0, 776, 0.0)
-                    for a in range(4):
-                        const("wt7", 264 + 128 * (a % 2), 268 + 128 * (a % 2), -1.0 if a % 2 else 1.0, 1, 32 * a, 32 * a + 32)
                 else:
-                    halves(2)
-                    halves(3)
-                if last:
-                    turn("COL", 480 * t)
+                    scores(7)
             if lev == 6:
+                if t == 0:
+                    scores(7)
+                for b in range(2 if t == 0 else 3):
+                    halves(b)
                 for m in range(3):
                     for a in range(4):
-                        act(AQ("CK", m, 7 * BLOCK[a], 7 * BLOCK[a] + 7), AQ("Y", a, 8 * m, 8 * m + 7))
-                if t == 0:
-                    halves(2)
-                    first(6, 0)
-                if last:
-                    fetch("R2", "last", HALF + 16)
+                        later(60, cp, AQ("RL", m, 7 * BLOCK[a], 7 * BLOCK[a] + 7), AQ("Y", a, 8 * m, 8 * m + 7))
             if lev == 7:
+                for b in range(2 if t == 0 else 3, 4):
+                    halves(b)
                 if t == 0:
-                    halves(3)
                     act(now, ind(A("IOB", 0, C), A("PL", 0, 28)))
 
         V = lambda n: A("TMP", 56 * n, 56 * n + 56)
-        L = lambda n: A("TMP", 56 * n, 56 * n + 56, 2)
-        R = lambda n: A("TMP", 56 * n + 1, 56 * n + 56, 2)
         H = lambda n: A("TMP", 28 * n, 28 * n + 28)
         four = lambda name, i: A(name, 16 + i, 128, 4)
         s0, s1 = [[A("BQ", QS * h + i, QS * h + QS, 2) for i in range(2)] for h in range(2)]
         tt(V(0), s0[1], s0[0], OP.is_lt)
-        ts(V(1), V(0), 2 * BIG, OP.mult, -BIG, OP.add)
-        ts(V(2), V(0), -2 * BIG, OP.mult, BIG, OP.add)
+        scores(1, (3,), cp)
+        scores(2)
+        ts(A("PR", 0, QS, 2), V(0), 2 * BIG, OP.mult, -BIG, OP.add)
+        ts(A("PR", QS + 1, 2 * QS, 2), V(0), -2 * BIG, OP.mult, BIG, OP.add)
         tt(A("G0", 16, 128, 2), A("PH", 0, QS, 2), V(0), OP.add)
-        tt(V(3), s1[1], V(1), OP.min)
-        tt(V(4), s1[0], V(2), OP.min)
+        scan(back("TMP", QS, 2 * QS), back("PR", 0, QS), back("BQ", QS, 2 * QS))
+        scan(A("TMP", 2 * QS, 3 * QS), A("PR", QS, 2 * QS), A("BQ", QS, 2 * QS))
         tt(A("G0", 17, 128, 2), A("PH", 1, QS, 2), V(0), OP.subtract)
-        tt(V(5), s1[0], V(3), OP.max)
-        tt(V(6), s1[1], V(4), OP.max)
-        tt(H(14), L(5), R(5), OP.is_gt)
-        tt(H(15), L(5), R(6), OP.is_gt)
-        tt(H(16), L(6), R(5), OP.is_gt)
-        tt(H(17), L(6), R(6), OP.is_gt)
+        key = lambda i: A("TMP", QS * (1 + i % 2) + i, QS * (2 + i % 2), 4)
+        tt(H(14), key(0), key(2), OP.is_gt)
+        tt(H(15), key(0), key(3), OP.is_gt)
+        tt(H(16), key(1), key(2), OP.is_gt)
+        tt(H(17), key(1), key(3), OP.is_gt)
         tt(H(18), four("G0", 0), H(14), OP.add)
         tt(H(19), four("G0", 3), H(15), OP.subtract)
         tt(H(20), four("G0", 1), H(16), OP.add)
@@ -551,8 +590,10 @@ def rank_program(g, core, T, topo):
         tr(A("TX", 0, 128), A("G0", 16, 144))
         turn2("T1", "GR")
         tr(A("TX", 128, 256), A("G0", 0, 128))
+        first(60)
         cp(A("LL", 0, 16), ind(A("T1", 0, 288), lst("two")))
         cp(A("DB", 0, 256, 32), A("T1", 0, 256, 32))
+        first(60)
         act(A("LR", 16, 128), ind(A("LC", 0, 128), A("LL", 0, 7)))
         act(A("MKL", 0, QS), ind(A("MP", 0, 128), A("LL", 0, 7)))
         act(A("XH", 16, 32), ind(A("T1", 0, 288), lst("two")))
@@ -560,19 +601,25 @@ def rank_program(g, core, T, topo):
 
         for lev in range(2, 6):
             w = BLK[lev]
-            n, cur = (QS, "CU5") if lev == 5 else (128, "CUR")
+            if t == 0 and lev == 5:
+                weights(6)
+            n, cur, key = (QS, "CU5", A("K5", 8, 120)) if lev == 5 else (128, "CUR", A("KEY", 0, 128))
             scatter(A(cur, 0, 128), A("LL", 0, 7), A("BQ", QS * lev, QS * lev + QS))
-            once(lev, 0)
-            scan(A("KEY", 0, n), A("DR", 128 * (lev - 2), 128 * (lev - 2) + n), A(cur, 0, n))
-            once(lev, 1)
+            first()
+            scan(key, A("DR", 128 * (lev - 2), 128 * (lev - 2) + n), A(cur, 0, n))
             one = lambda b: A("TQ", 32 * b, 32 * b + 1)
             if lev > 3:
-                act(A("KS", 0, QS), ind(A("KEY", 0, 128), A("LL", 0, 7)))
+                act(A("KS", 0, QS), ind(key, A("LL", 0, 7)))
             if lev == 2:
                 turn2("TL", "LR")
-            if lev < 5:
-                tr(A("TQ", 0, 128), A("KEY", 0, 128))
-            once(lev, 2)
+            else:
+                first()
+            tr(A("TQ", 0, 128), A("K5" if lev == 5 else "KEY", 0, 128))
+            if lev > 2:
+                first(260 if lev > 3 else 150)
+            if last and lev > 3:
+                turn("COL", 480 * t, (lev - 4,))
+                later(100, fetch, "R2", "last", HALF + 16, (lev - 4,))
             if lev == 2:
                 cp(A("L2", 0, 16), ind(A("TL", 0, 288), lst("two")))
                 for b in range(4):
@@ -589,119 +636,139 @@ def rank_program(g, core, T, topo):
                 for b in range(4):
                     ts(A("MB", 16 + w * b, 16 + w * b + w), A("KS", w * b, w * b + w), one(b ^ 1), OP.is_lt if b % 2 else OP.is_gt, mask("n28" if b % 2 else "p28"), OP.mult)
             else:
-                tr(A("TQ", 0, 64), A("KEY", 0, 64))
-                tr(A("TQ", 64, 128), A("KEY", w, w + 64))
-                for i, k in enumerate(("32", "24")):
-                    ts(lane(i, 0, w), A("KS", 0, w), one(2 + i), OP.is_gt, mask("p" + k), OP.mult)
-                    ts(lane(i, w, QS), A("KS", w, QS), one(i), OP.is_lt, mask("n" + k), OP.mult)
-            if lev < 5:
-                background(lev)
-                sums(lev, once)
-        counts(5)
-        background(5)
-        places(5, A("XH", 64, 80))
+                ts(A("MB", 16, 16 + w), A("KS", 0, w), one(2), OP.is_gt)
+                ts(A("MB", 16 + w, 128), A("KS", w, QS), one(0), OP.is_lt, mask("n24"), OP.mult)
+                ts(A("MB1", 16, 16 + w), A("KS", 0, w), one(3), OP.is_gt, mask("p24"), OP.mult)
+                ts(A("MB1", 16 + w, 128), A("KS", w, QS), one(1), OP.is_lt, -1.0, OP.mult)
+            background(lev)
+            sums(lev)
 
-        ts(A("LL", 0, 7), A("XH", 80, 87), A("QC", 2, 3), OP.add)
-        cp(A("LG", 0, 7), A("XH", 80, 87))
         scatter(A("W6", 0, 256), A("LL", 0, 7), A("BQ", QS * 6, QS * 7))
-        ts(A("XB", 16, 32), A("XH", 80, 96), A("QC", 0, 1), OP.add)
+        if t == 0:
+            weights(7)
+        first()
         scan(A("K6", 0, QS), A("W6", 128, 128 + QS), A("W6", 0, QS))
-        tt(A("Y", 0, 32), ind(A("XH", 0, 128), lst("pairs", 2)), A("OFS", 0, 32), OP.add)
         act(A("KS", 0, QS), ind(A("K6", 0, 128), A("LG", 0, 7)))
+        tt(A("Y", 0, 32), ind(A("XH", 0, 128), lst("pairs", 2)), A("OFS", 0, 32), OP.add)
         for h in range(2):
             tr(AQ("TQ", 2 * h, 0, 128, 1, 2), AQ("K6", 2 - 2 * h, 0, 128, 1, 2))
+        background(6)
+        first()
         for b in range(4):
             ts(lane(b, 0, QS), A("KS", 0, QS), A("TQ", 32 * b, 32 * b + 1), OP.add, 0.0, OP.is_gt)
+        first()
         counts(6)
-        background(6)
+        if last:
+            slots(0, 6)
+        else:
+            first(400)
+        tr(A("TW", 0, 128), ps(LB, 0, 128))
+        first()
         places(6, A("XB", 16, 32))
+        first()
 
         for h in range(2):
             for d in range(2):
                 ts(AQ("LH", 2 * d, 7 * h, 7 * h + 7, 1, 2), AQ("XH", 2 * h, 96, 103, 1, 2), AQ("QC", 2 * d, 6, 7, 1, 2), OP.add)
+        first()
         scatter(A("W7", 0, 512), A("LH", 0, 14), A("B7", 0, HALF))
         ts(A("LG", 0, 14), A("LH", 0, 14), A("QC", 6, 7), OP.subtract)
         ts(A("XB", 32, 48), A("XH", 96, 112), A("QC", 4, 5), OP.add)
         scan(A("K7", 0, HALF), A("W7", 256, 256 + HALF), A("W7", 0, HALF))
-        for p0, p1 in ((0, 64), (64, 96)):
-            cp(A("RL", 0, 28, 1, p0, p1), A("CK", 0, 28, 1, p0, p1))
         act(A("KS", 0, HALF), ind(A("K7", 0, 256), A("LG", 0, 14)))
+        first()
         for a in range(4):
-            tr(AQ("TQ", a, 0, 128), AQ("K7", a ^ 1, 128 * (a // 2), 128 * (a // 2) + 128))
-        act(A("RG", 0, HALF), A("KS", 0, HALF), bias=A("TQ", 96, 97), func=AF.Sign)
-        act(lane(3, 0, HALF), A("RG", 0, HALF), func=AF.Relu)
+            n = 128 if a < 2 else 96
+            tr(AQ("TQ", a, 0, n), AQ("K7", a ^ 1, 128 * (a // 2), 128 * (a // 2) + n))
+        first()
+        act(AQ("RG", 0, 0, HALF, 1, 2), AQ("KS", 0, 0, HALF, 1, 2), bias=AQ("TQ", 0, 96, 97, 1, 2), func=AF.Sign)
+        act(AQ("G", 0, 67, 64 + 4 * HALF, 4, 2), AQ("RG", 0, 0, HALF, 1, 2), func=AF.Relu)
         for b in range(3):
             ts(lane(b, 0, HALF), A("KS", 0, HALF), A("TQ", 32 * b, 32 * b + 1), OP.add, 0.0, OP.is_gt)
         counts(7)
+        if last:
+            slots(6, 16)
+        first(10000)
         background(7)
+        tr(A("TW", 0, 128), ps(LB, 0, 128))
         places(7, A("XB", 32, 48))
         for a in range(4):
             ts(AQ("RL", 3, 7 * BLOCK[a], 7 * BLOCK[a] + 7), AQ("XH", a, 112, 119), col("h16", 32 * a, 32 * a + 32), OP.add)
 
         scatter(A("SIG", 0, 480), A("RL", 0, 28), A("IOB", 0, C))
-        turn("SIG", 0)
-        fetch("ZL", "own", HALF)
+        ts(A("CA", 0, 28), A("RL", 0, 28), col("h16"), OP.subtract)
+        turn("SIG", 0, (0,))
+        ts(A("CT", 0, 28), A("CA", 0, 28), float(HALF), OP.is_ge, -float(HALF), OP.mult)
+        fetch("ZL", "own", HALF, (0,), 16)
+        turn("SIG", 0, (1,))
+        if not last:
+            fetch("PL", "last", HALF, (0,))
+        fetch("ZL", "own", HALF, (1,), 16)
 
         for b in range(4):
-            (act if b else cp)(A("GZ", HALF * b, HALF * b + HALF), ind(A("HB", C * b, C * b + C), A("ZL", 0, 14)))
+            act(A("GZ", HALF * b, HALF * b + HALF), ind(A("HB", C * b, C * b + C), A("ZL", 0, 14)))
+        qf, sf = "qf%d" % t, "sf%d" % t
+        if not last:
+            fetch("PL", "last", HALF, (1,))
+            for i in (0, 16):
+                tt(A("UW", i, 896, 32), A("CA", 0, 28), A("CT", 0, 28), OP.add)
+        else:
+            tt(A("CA", 0, 28), A("CA", 0, 28), A("CT", 0, 28), OP.add)
+            for b in range(2):
+                act(A("FB", C * b, C * b + C), ps(DBANK[b], 0, C))
         for b in range(4):
-            tt(A("ZT", b, 896, 4), ind(A("HB", C * b, C * b + C), A("ZL", 14, 28)), A("GZ", HALF * b, HALF * b + HALF), OP.add)
+            tt(A("ZT", b, 896, 4), ind(A("HB", C * b, C * b + C), A("ZL", 16, 30)), A("GZ", HALF * b, HALF * b + HALF), OP.add)
+        if not last:
+            for a in range(3):
+                cp(AQ("PL", a, 0, 28), AQ("PL", 3, 0, 28))
+            act(A("FB", 0, C), ind(A("HB", 0, C), A("PL", 0, 28)), 2.0)
+            act(A(sf, 0, C), ind(A(sp, 0, C), A("PL", 0, 28)))
         zc, zs = "zc%d" % t, "zs%d" % t
         quant(A(zc, 0, HALF), A(zs, 0, HALF), A("ZT", 0, 896))
 
         hazards("g", [(zc, 0, 128, 0, HALF, 1), (zs, 0, 128, 0, HALF, 1)], [])
-        for k, (nm, hn) in enumerate(((zc, "hc%d" % t), (zs, "hs%d" % t))):
-            tf = []
-            for i in range(2):
-                rid, pid = topo.addr(rel[2 * k + i], core)
-                s_, d_ = T[nm][:, i * HALF // 2:(i + 1) * HALF // 2], T[hn][:, :]
-                if nm == zc:
-                    s_, d_ = s_.bitcast(dt.uint8), d_.bitcast(dt.uint8)
-                tf.append(RemoteDMATransfer(dst_ids=[DstId(rid=rid, pnc=pid)], dma_engine_mask=_bits(cut[i]), remote_sem=T.sem["rc%d" % t], src=s_, dst=d_))
-            g.remote_dma_fused(tf, local_sem=T.sem.snd)
+        tf = []
+        for i in range(2):
+            rid, pid = topo.addr(rel[i], core)
+            s_, d_ = T[zc][:, i * QS:(i + 1) * QS].bitcast(dt.uint8), T["hc%d" % t][:, :].bitcast(dt.uint8)
+            tf.append(RemoteDMATransfer(dst_ids=[DstId(rid=rid, pnc=pid)], dma_engine_mask=_bits(cut[i]), remote_sem=T.sem["rc%d" % t], src=s_, dst=d_))
+        g.remote_dma_fused(tf, local_sem=T.sem.snd)
+        rid, pid = topo.addr(rel[2], core)
+        g.remote_dma(T["hs%d" % t][:, :], T[zs][:, :], T.sem["rc%d" % t], T.sem.snd, pid, rid, _bits(eng))
 
         if not last:
-            fetch("PL", "last", HALF)
-        ts(A("CA", 0, 28), A("RL", 0, 28), col("h16"), OP.subtract)
-        if not last:
-            for a in range(3):
-                cp(AQ("PL", a, 0, 28), AQ("PL", 3, 0, 28))
-        ts(A("CT", 0, 28), A("CA", 0, 28), float(HALF), OP.is_ge, -float(HALF), OP.mult)
-        if not last:
-            qf, sf = "qf%d" % t, "sf%d" % t
             cp(A("NI", 0, 28), A("PL", 0, 28))
-            for i in (0, 16):
-                tt(A("UW", i, 896, 32), A("CA", 0, 28), A("CT", 0, 28), OP.add)
-            ts(A("NA", 0, 28), A("NI", 0, 28), 496, OP.bitwise_and)
             tr(A("UT", 0, C), A("UW", 0, C))
-            tt(A("NS", 0, 28), A("NI", 0, 28), A("NA", 0, 28), OP.add)
+            ts(A("NA", 0, 28), A("NI", 0, 28), 496, OP.bitwise_and)
             tr(A("UT", C, 896), A("UW", C, 896))
+            tt(A("NS", 0, 28), A("NI", 0, 28), A("NA", 0, 28), OP.add)
             ts(A("NL", 0, 28), A("NS", 0, 28), col("h16"), OP.add)
-            pick(qf, sf, (0, C), qp, sp, C, A("PL", 0, 28))
-            act(A("RN", 16, 16 + C), ind(A("UT", 0, 896), A("NL", 0, 28)))
-            for b in range(4):
-                unpack(b, qf, sf)
-                if b < 2:
-                    act(A("FB", C * b, C * b + C), ps(DBANK[b], 0, C))
+            codes(qf, (0, C), qp, C, A("PL", 0, 28))
+            for a, b in ((0, 16), (16, 28)):
+                act(A("RN", 16 + 16 * a, 16 + 16 * b), ind(A("UT", 0, 896), A("NL", a, b)))
+            act(A("FB", C, 2 * C), ind(A("HB", C, 2 * C), A("PL", 0, 28)), 2.0)
             turn("RN", 0)
             fetch("RM", "mine", 0)
         else:
-            tt(A("CA", 0, 28), A("CA", 0, 28), A("CT", 0, 28), OP.add)
-            act(A("OD", 0, C), ind(now, A("ZL", 0, 28)), bias=col("h224"))
-            dmas("y", [(ext(T.od[h:h + 1, :]), A("OD", 0, C, 1, 16 * h, 16 * h + 1)) for h in range(8)], "dd")
-            scatter(A("SIG", 0, 480), A("R2", 0, 28), A("IOB", 0, C))
             cp(A("RM", 0, 28), A("CA", 0, 28))
-            turn("SIG", 0)
+            slots(16, 28)
+            for i in range(2):
+                act(A("OD", HALF * i, HALF * i + HALF), ind(now, A("ZL", 16 * i, 16 * i + 14)), bias=col("h224"))
+            dmas("y", [(ext(T.od[:, :]), (T.OD[0:128:16, :], A("OD", 0, C)[1]))], "dd")
+            turn("RN", 0)
             fetch("IC", "last", HALF)
 
         lc, ls = "lc%d" % t, "ls%d" % t
         wait("t", "lz%d" % t, landed)
-        for b in (0, 1, 2, 3):
+        for b in (0, 2, 1, 3):
             mm(ps(PBANK[b], 0, HALF), A("wq", 128 * b, 128 * b + 128), A("wp", 128 * b, 128 * b + 128), A(lc, 0, HALF), A(ls, 0, HALF))
-            if b:
+            if b > 1:
                 act(A("PB", HALF * b, HALF * b + HALF), ps(PBANK[b], 0, HALF), 0.03125)
             else:
                 ts(A("PB", HALF * b, HALF * b + HALF), ps(PBANK[b], 0, HALF), 0.03125, OP.mult)
+        if not last:
+            for b in (2, 3):
+                unpack(b, qf, sf)
         act(A("RG", 0, C), ind(A("PB", 2 * HALF, 3 * HALF), A("RM", 0, 28)))
         for i in range(2):
             act(A("RG", C + HALF * i, C + HALF * i + HALF), ind(A("PB", 3 * HALF, 4 * HALF), A("RM", 14 * i, 14 * i + 14)))
@@ -715,14 +782,13 @@ def rank_program(g, core, T, topo):
         quant(A("qx3", HALF * i, HALF * i + HALF), A("sx3", HALF * i, HALF * i + HALF), A("xn", 896 * i, 896 * i + 896))
     for i in range(2):
         o = (HALF * i, HALF * i + HALF)
-        pick("qp3", "sp3", o, "qx3", "sx3", C, A("IC", 14 * i, 14 * i + 14))
-        mm(ps(i, 0, HALF), A("qv", 0, 128), A("pv", 0, 128), A("qp3", *o), A("sp3", *o))
-    dmas("y", [(ext(T.oc[:, :]), bc(A("qp3", 0, C)))], "dc")
-    act(A("yb", 0, HALF), ps(0, 0, HALF))
-    cp(A("yb", HALF, C), ps(1, 0, HALF))
-    dmas("s", [(ext(T.y[:, 0:HALF]), A("yb", 0, HALF))], "dy")
-    dmas("y", [(ext(T.y[:, HALF:C]), A("yb", HALF, C))], "dy2")
-    dmas("s", [(ext(T.osc[4 * k:4 * k + 4, :]), A("sp3", 0, C, 1, 32 * k, 32 * k + 4)) for k in range(4)], "dq")
+        pick("qf2", "sf2", o, "qx3", "sx3", C, A("IC", 14 * i, 14 * i + 14))
+        mm(ps(i, 0, HALF), A("qv", 0, 128), A("pv", 0, 128), A("qf2", *o), A("sf2", *o))
+        dmas("y", [(ext(T.oc[:, 896 * i:896 * i + 896]), bc(A("qf2", *o)))], "dc%d" % i)
+    dmas("s", [(ext(T.osc[4 * k:4 * k + 4, :]), A("sf2", 0, C, 1, 32 * k, 32 * k + 4)) for k in range(4)], "dq")
+    for i in range(2):
+        cp(A("yb", HALF * i, HALF * i + HALF), ps(i, 0, HALF))
+        dmas("y", [(ext(T.y[:, HALF * i:HALF * i + HALF]), A("yb", HALF * i, HALF * i + HALF))], "dy%d" % i)
     for sem in count:
         wait("g", sem, count[sem])
     wait("g", "snd", 2 * len(eng) * ROUNDS)

@@ -1,13 +1,13 @@
-from concourse.bass import DstId, RemoteDMATransfer
 from concourse.mybir import dt, AluOpType, ActivationFunctionType
 
 OP = AluOpType
 AF = ActivationFunctionType
 ROUNDS, C, HALF, QS = 3, 448, 224, 112
 BIG = 1e29
-SAME = False
 LIFT = 64
+TINY = 2.0 ** -120
 BLOCK = (0, 2, 1, 3)
+PIECES = ((0, 128), (128, HALF))
 
 SCRATCH = {}
 
@@ -23,23 +23,24 @@ def _mx(c, s, n):
 
 PARTS = {}
 _z = 0
-for _n, _w in (("MB", 144), ("GR", 144), ("G0", 144), ("LR", 144), ("DKR", 144), ("MB1", 144), ("MP", 128), ("LC", 128), ("T1", 288), ("TX", 288), ("TL", 288), ("CS", 288)):
+for _n, _w in (("MB", 144), ("GR", 432), ("DKR", 144), ("MB1", 144), ("MP", 128), ("MP3", 144), ("T1", 288), ("CS", 288)):
     PARTS[_n] = ("Z", _z)
     _z += _w
-for _k, _n in enumerate(("MK", "QC", "OFS", "Y", "CK", "CA", "CT", "NS")):
+for _k, _n in enumerate(("MK", "QC", "OFS", "Y", "CK", "CA", "CT", "NS", "XF", "X7")):
     PARTS[_n] = ("S", 32 * _k)
-for _n, _w in (("Z", _z), ("xt", 1792), ("xn", 1792), ("ut", 512), ("vt", 512), ("one", 516), ("eb", 516), ("wt6", 520), ("wt7", 776), ("G", 1088),
-               ("FB", 896), ("HB", 1792), ("ZT", 896), ("IOB", C), ("SIG", 480), ("TT", 1024), ("COL", 3 * 480), ("MR", 320), ("MT", 320),
-               ("PH", QS), ("MKL", QS), ("TB", 512), ("DB", 256), ("D5", 512), ("C5", 576), ("DT", 288), ("UW", 896), ("UT", 896), ("RN", 480)):
+for _n, _w in (("Z", _z), ("xt", 1792), ("xn", 1792), ("ut", 512), ("vt", 512), ("one", 516), ("eb", 516), ("wt6", 520), ("wt7", 536), ("G", 1088),
+               ("FB", 896), ("FK", 896), ("HB", 1792), ("ZT", 1024), ("IOB", C), ("SIG", 480), ("TT", 1024), ("COL", 3 * 480), ("MR", 320), ("MT", 320),
+               ("PH", QS), ("MKL", QS), ("TB", 512), ("DB", 256), ("D3", 256), ("D5", 512), ("C5", 576), ("DT", 288), ("UW", 896), ("UT", 896),
+               ("RN", 480), ("RI", 480), ("G3", 336), ("R3", 336)):
     _sb(_n, _w, "bfloat16")
-for _n, _w in (("RW", 544), ("CL", 544), ("K5", 128), ("S", 256), ("PR", 2 * QS), ("BQ", 7 * QS),
-               ("B7", HALF), ("CUR", 128), ("CU5", 128), ("KEY", 128), ("KS", HALF), ("TQ", 128), ("MC", 256), ("TMP", 800), ("DR", 512),
-               ("TW", 160), ("XH", 128), ("XB", 48), ("W6", 256), ("K6", 128), ("W7", 512), ("K7", 256),
-               ("ZF", 512), ("OD", C), ("GZ", 896), ("PB", 896), ("RG", 2 * C), ("yb", C)):
+for _n, _w in (("RW", 544), ("CL", 544), ("K5", 128), ("S", 320), ("PR", 2 * QS), ("BQ", 8 * QS),
+               ("CUR", 416), ("CU5", 128), ("KEY", 144), ("KS", HALF), ("TQ", 128), ("T7", HALF), ("MC", 144), ("T6", 256), ("TMP", 336), ("DR", 512),
+               ("TW", 160), ("XH", 128), ("XB", 32), ("W6", 128), ("K6", 128), ("W7", HALF), ("K7", HALF), ("SG", HALF),
+               ("ZF", 260), ("OD", C), ("GZ", 896), ("PB", C), ("PK", 2 * C), ("yb", C)):
     _sb(_n, _w)
 for _n, _w in (("pi", 28), ("ii", 16), ("NI", 28), ("NA", 28)):
     _sb(_n, _w, "int32")
-for _n, _w in (("LS", 20), ("LL", 16), ("L2", 16), ("LG", 16), ("LH", 14), ("RL", 28), ("RM", 32), ("R2", 32), ("ZL", 32), ("PL", 32), ("IC", 32),
+for _n, _w in (("LS", 20), ("LL", 16), ("LG", 16), ("RK", 28), ("RL", 28), ("RM", 32), ("R2", 32), ("ZL", 32), ("PL", 32), ("IC", 32),
                ("UL", 16), ("NL", 28)):
     _sb(_n, _w, "uint16")
 _mx("qu", "su", 128)
@@ -47,36 +48,27 @@ _mx("qB", "sB", 256)
 _mx("qv", "pv", 128)
 _mx("wq", "wp", 512)
 _mx("q6", "s6", 130)
-_mx("q7", "s7", 194)
+_mx("q7", "s7", 134)
 _mx("qe", "se", 512)
 _mx("qa", "sa", 272)
 for _t in range(ROUNDS + 1):
     _mx("qx%d" % _t, "sx%d" % _t, C)
-for _n in ("p0", "f0", "f1", "f2"):
-    _mx("q" + _n, "s" + _n, C)
+_mx("qp0", "sp0", C)
 for _t in range(ROUNDS):
-    _mx("zc%d" % _t, "zs%d" % _t, HALF)
+    _mx("zc%d" % _t, "zs%d" % _t, 256)
     _mx("lc%d" % _t, "ls%d" % _t, HALF)
-    _sb("hc%d" % _t, QS, "float8_e4m3fn_x4")
-    _sb("hs%d" % _t, HALF, "uint8")
+    _mx("hc%d" % _t, "hs%d" % _t, HALF)
 SCRATCH["ps"] = ("psum", [128, 4096], "float32")
 
 SEMAPHORES = (["sv", "st", "ss", "sg", "snd", "dx", "dx2", "dp", "du", "dw", "dv", "dy0", "dy1", "dc0", "dc1", "dd", "dq"]
-              + ["%s%d" % (_a, _t) for _a in ("rc", "lz") for _t in range(ROUNDS)])
+              + ["%s%d" % (_a, _t) for _a in ("ra", "rb", "la", "lb") for _t in range(ROUNDS)])
 
 
 def _relays(topo, src, dst):
     ok = [c for c in topo.cores_of(src) if c != src and topo.may_write(c, dst)]
     near = [c for c in ok if topo.die(c) == topo.die(src)]
     far = [c for c in ok if topo.die(c) != topo.die(src)]
-    return [near[0], far[0], near[1]]
-
-
-def _bits(engines):
-    m = 0
-    for e in engines:
-        m |= 1 << e
-    return m
+    return [far[0], near[0], far[1], near[1]]
 
 
 def _relay_program(g, core, T, topo):
@@ -90,13 +82,15 @@ def _relay_program(g, core, T, topo):
         rid, pid = topo.addr(dst, core)
         m = topo.mask(core, dst)
         k = len(topo.engines(core, dst))
-        came = len(topo.engines(T.cores[r], core)) // (2 if h < 2 else 1)
+        came = len(topo.engines(T.cores[r], core))
+        a, b = PIECES[h % 2]
         for t in range(ROUNDS):
-            g.wait_ge(T.sem["rc%d" % t], came)
+            g.wait_ge(T.sem["r%s%d" % ("ab"[h % 2], t)], came)
+            sem = T.sem["l%s%d" % ("ab"[h % 2], t)]
             if h < 2:
-                g.remote_dma(T["lc%d" % t][:, h * QS:(h + 1) * QS].bitcast(dt.uint8), T["hc%d" % t][:, :].bitcast(dt.uint8), T.sem["lz%d" % t], T.sem.snd, pid, rid, m)
+                g.remote_dma(T["lc%d" % t][:, a:b].bitcast(dt.uint8), T["hc%d" % t][:, a:b].bitcast(dt.uint8), sem, T.sem.snd, pid, rid, m)
             else:
-                g.remote_dma(T["ls%d" % t][:, :], T["hs%d" % t][:, :], T.sem["lz%d" % t], T.sem.snd, pid, rid, m)
+                g.remote_dma(T["ls%d" % t][:, a:b], T["hs%d" % t][:, a:b], sem, T.sem.snd, pid, rid, m)
         g.wait_ge(T.sem.snd, k * ROUNDS)
 
 
@@ -125,6 +119,8 @@ def rank_program(g, core, T, topo):
         return A(name, c0, c1, st, 32 * a, 32 * (a + n))
 
     def back(name, c0, c1):
+        if name in PARTS:
+            name, c0, c1 = PARTS[name][0], c0 + PARTS[name][1], c1 + PARTS[name][1]
         return (T[name][:, c1 - 1:c0 - 1:-1] if c0 else T[name][:, c1 - 1::-1], [(name, 0, 128, c0, c1, 1)])
 
     def ps(bank, c0, c1, st=1, p0=0, p1=128):
@@ -162,8 +158,6 @@ def rank_program(g, core, T, topo):
                     if bank and eq == q and (q == "t" or not ew):
                         continue
                     if not bank and not w and not ew:
-                        continue
-                    if eq == q and w and SAME:
                         continue
                     need[sem] = max(need.get(sem, 0), val)
         for sem in sorted(need, key=lambda s: -len(known.get((s, need[s]), ()))):
@@ -213,21 +207,21 @@ def rank_program(g, core, T, topo):
     def cp(out, a):
         do("v", lambda: g.vector.tensor_copy(out[0], a[0]), [out], [a])
 
-    def act(out, a, scale=1.0, bias=None, func=None):
-        if bias is not None:
-            do("s", lambda: g.scalar.activation(out[0], a[0], func or AF.Identity, bias=bias[0]), [out], [a, bias])
-        elif scale == 1.0:
-            do("s", lambda: g.scalar.activation(out[0], a[0], func or AF.Copy), [out], [a])
+    def act(out, a, scale=1.0, bias=0.0, func=None):
+        cols = [x for x in (scale, bias) if isinstance(x, tuple)]
+        sc, bi = [x[0] if isinstance(x, tuple) else x for x in (scale, bias)]
+        if not cols and bi == 0.0:
+            if sc == 1.0:
+                do("s", lambda: g.scalar.activation(out[0], a[0], func or AF.Copy), [out], [a])
+            else:
+                do("s", lambda: g.scalar.activation(out[0], a[0], AF.Copy, scale=sc), [out], [a])
         else:
-            do("s", lambda: g.scalar.activation(out[0], a[0], AF.Copy, scale=scale), [out], [a])
-
-    def codes(qo, o, qi, w, off):
-        src = A(qi, 0, w)
-        do("v", lambda: g.vector.tensor_copy(u32(A(qo, *o))[0], u32(src)[0].indirect(off[0])), [A(qo, *o)], [src, off])
+            do("s", lambda: g.scalar.activation(out[0], a[0], func or AF.Identity, bias=bi, scale=sc), [out], [a] + cols)
 
     def pick(qo, so, o, qi, si, w, off):
         act(A(so, *o), ind(A(si, 0, w), off))
-        codes(qo, o, qi, w, off)
+        src = A(qi, 0, w)
+        do("v", lambda: g.vector.tensor_copy(u32(A(qo, *o))[0], u32(src)[0].indirect(off[0])), [A(qo, *o)], [src, off])
 
     def scatter(win, off, vals):
         do("v", lambda: g.vector.tensor_copy(win[0].indirect(off[0]), vals[0]), [win], [vals, off])
@@ -256,10 +250,10 @@ def rank_program(g, core, T, topo):
     def never(name, a, b, val):
         aff(A(name, a, b), A("ZF", 0, b - a), [[0, b - a]], OP.is_equal, val, 1, 0)
 
-    def const(name, a, b, val, st=1, p0=0, p1=128):
+    def const(name, a, b, val, st=1):
         for c0 in range(a, b, 512 * st):
             c1 = min(c0 + 512 * st, b)
-            act(A(name, c0, c1, st, p0, p1), A("one", 0, len(range(c0, c1, st)), 1, p0, p1), val)
+            act(A(name, c0, c1, st), A("one", 0, len(range(c0, c1, st))), val)
 
     def ext(ap):
         return (ap, [])
@@ -278,8 +272,8 @@ def rank_program(g, core, T, topo):
             "h16": (3, [([[16, 2], [0, 16]], 0)]),
             "one": (4, [([[0, 2], [32, 4], [34, 2]], 0), ([[0, 2], [32, 4], [-2, 2]], 2)]),
             "h224": (5, [([[0, 32]], HALF)]),
-            "upper": (6, [([[0, 16]], 1), ([[0, 2], [32, 4], [-2, 2]], 2)]),
-            "none": (7, [([[0, 32]], 0)]),
+            "all": (6, [([[0, 16]], 8), ([[32, 4], [-2, 2]], 2), ([[32, 3], [-2, 2]], 6), ([[-2, 2]], 3)]),
+            "all2": (7, [([[0, 16]], 8), ([[32, 3], [-2, 2]], 35), ([[32, 3], [-2, 2]], 7), ([[0, 4]], 8)]),
             "pairs": (8, [([[16, 2], [32, 2], [1, 8]], 64 * k) for k in range(2)]),
             "own": (10, [([[16, 2], [32, 8], [256, 2]], 0)]),
             "gap": (11, [([[0, 32]], 0)]),
@@ -306,8 +300,9 @@ def rank_program(g, core, T, topo):
         j = 32 * ROWS[k][0]
         return A("CL", j, j + 1, 1, p0, p1)
 
-    MASKS = {"b0": (0, 7, 14, 1.0), "b1": (1, 0, 7, -1.0), "b2": (2, 21, 28, 1.0), "b3": (3, 14, 21, -1.0), "c0": (4, 14, 28, 1.0), "c1": (5, 0, 14, -1.0),
-             "p28": (6, 0, 28, 1.0), "n28": (7, 0, 28, -1.0), "p24": (8, 0, 24, 1.0), "n24": (9, 8, 32, -1.0)}
+    MASKS = {"b0": (0, (7, 14, 0.0), (0, 7, -BIG)), "b1": (1, (0, 7, -TINY)), "b2": (2, (21, 28, 0.0), (14, 21, -BIG)), "b3": (3, (14, 21, -TINY)),
+             "c0": (4, (14, 28, 0.0), (0, 14, -BIG)), "c1": (5, (0, 14, -TINY)),
+             "p28": (6, (0, 28, 1.0)), "n28": (7, (0, 28, -1.0)), "p24": (8, (0, 24, 1.0)), "n24": (9, (8, 32, -1.0))}
 
     def mask(k):
         j = MASKS[k][0]
@@ -316,49 +311,53 @@ def rank_program(g, core, T, topo):
     def zero(name, a, b):
         iota(A(name, a, b), [[0, b - a]], 0)
 
-    for a, b in ((0, 16), (128, 160), (272, 304), (416, 448), (560, 592), (704, 736), (848, 1120)):
-        fill(A("Z", a, b), 0.0)
+    for a, b, val in ((0, 16, 0.0), (128, 192, 0.0), (528, 576, 255.0), (576, 592, 0.0), (704, 736, 0.0), (848, 1136, 0.0)):
+        fill(A("Z", a, b), val)
+    fill(A("R3", 0, 336), 1.0)
     iota(A("ii", 0, 16), [[16, 8], [0, 2]], 0)
     iota(A("one", 0, 516), [[0, 516]], 1)
     rows(("two", "drop", "end", "h16"))
-    iota(A("PH", 0, QS), [[32, 4], [1, 28]], 0)
     for b in range(4):
-        iota(A("LC", 32 * b, 32 * b + 28), [[14, 2], [135, 2], [1, 7]], 32 * b)
-    for name in ("T1", "TX", "TL", "CS", "DT"):
-        zero(name, 256, 288)
-    zero("MC", 0, 256)
-    iota(A("DKR", 16, 128), [[-4, 4], [0, 28]], LIFT)
-    zero("XH", 0, 128)
-    aff(A("eb", 0, 516), A("one", 0, 516), [[1, 516]], OP.is_equal, 0.0, -3, -4)
-    rows(("one", "h224", "upper", "none", "pairs", "own", "gap", "last", "gap2", "mine", "gap3", "wide"))
-    for name, a, b in (("QC", 0, 8), ("CU5", 0, 128), ("C5", 512, 576), ("wt6", 0, 520), ("TW", 128, 160), ("ZF", 0, 260)):
+        iota(A("PH", 28 * b, 28 * b + 28), [[4, 7], [0, 2], [1, 2]], 32 * b)
+    zero("BQ", QS, 2 * QS)
+    for name, a, b in (("T1", 256, 288), ("CS", 256, 288), ("MC", 128, 144), ("DT", 256, 288), ("KEY", 128, 144), ("QC", 0, 8)):
         zero(name, a, b)
-    never("W6", 0, 129, -BIG)
-    never("W6", 129, 256, BIG)
-    never("K6", 0, 128, -BIG)
-    zero("wt7", 0, 776)
+    iota(A("DKR", 16, 128), [[-4, 4], [0, 28]], LIFT)
+    zero("MR", 192, 320)
+    for k in ("p28", "n28", "p24", "n24"):
+        j, (a, b, val) = MASKS[k]
+        iota(A("MR", 32 * j + a, 32 * j + b), [[0, b - a]], int(val))
+    for a, n, val in ((6, 1, -LIFT), (7, 1, -LIFT), (8, 2, -QS)):
+        iota(A("MR", 32 * a + 31, 32 * a + 31 + n), [[0, n]], val)
+    aff(A("eb", 0, 516), A("one", 0, 516), [[1, 516]], OP.is_equal, 0.0, -3, -4)
+    rows(("one", "h224", "all", "all2", "pairs", "own", "gap", "last", "gap2", "mine", "gap3", "wide"))
+    for name, a, b in (("CU5", 0, 128), ("C5", 512, 576), ("XH", 96, 128), ("wt6", 0, 520), ("TW", 128, 160), ("ZF", 0, 260), ("W6", QS, 128), ("T6", 0, 256)):
+        zero(name, a, b)
+    zero("wt7", 0, 536)
     zero("G", 576, 1088)
-    never("W7", 0, 257, -BIG)
-    never("W7", 257, 512, BIG)
-    zero("K7", HALF, 256)
+    never("W7", 0, HALF, -BIG)
+    zero("T7", 0, HALF)
+    zero("X7", 0, 32)
     iota(A("IOB", 0, C), [[1, C]], -HALF)
-    for name, a, b in (("SIG", 0, 16), ("SIG", C, 480), ("TT", 480, 512), ("TT", 992, 1024), ("RN", 0, 16), ("RN", 464, 480),
-                       ("COL", 960, 976), ("COL", 1424, 1440), ("UW", 0, 896)):
+    for name, a, b in (("SIG", 0, 16), ("SIG", C, 480), ("TT", 480, 512), ("TT", 992, 1024), ("UW", 0, 896), ("ZT", 896, 1024), ("RN", 0, 16), ("RN", 464, 480),
+                       ("RI", 0, 16), ("RI", 464, 480), ("COL", 960, 976), ("COL", 1424, 1440)):
         zero(name, a, b)
 
-    fill(A("MR", 0, 320), 0.0)
+    fill(A("MR", 0, 192), BIG)
+    fill(A("R3", 0, 336, 3), 0.0)
     cp(A("UL", 0, 16), A("ii", 0, 16))
-    for k in MASKS:
-        j, a, b, val = MASKS[k]
-        fill(A("MR", 32 * j + a, 32 * j + b), val)
-    fill(A("MR", 32 * 6 + 31, 32 * 8, 32), -float(LIFT))
-    fill(A("MR", 32 * 8 + 31, 32 * 9 + 1), -float(QS))
-    tr(A("MT", 0, 320), A("MR", 0, 320))
+    for k in ("b0", "b1", "b2", "b3", "c0", "c1"):
+        for a, b, val in MASKS[k][1:]:
+            fill(A("MR", 32 * MASKS[k][0] + a, 32 * MASKS[k][0] + b), val)
     fill(A("DB", 0, 256), -BIG)
-    cp(A("MK", 0, 10), A("MT", 0, 320, 32))
+    tr(A("MT", 0, 192), A("MR", 0, 192))
+    fill(A("D3", 0, 256), BIG)
+    cp(A("MK", 0, 6), A("MT", 0, 192, 32))
     const("DR", 0, 512, BIG)
-    const("CUR", 0, 128, 0.0)
     const("PR", 0, 2 * QS, -BIG)
+    const("CUR", 0, 416, 0.0)
+    for a, b in ((0, 384), (7, 128), (14, 256), (21, 128)):
+        const("DR", a, b, -BIG, 32)
 
     todo = []
 
@@ -370,27 +369,34 @@ def rank_program(g, core, T, topo):
             ns -= max(todo[0][0], 1)
             todo.pop(0)[1]()
 
-    for a, b, st in ((0, 128, 32), (7, 128, 32), (14, 256, 32), (21, 128, 32)):
-        later(60, fill, A("DR", a, b, st), -BIG)
+    def until(mark):
+        while any(x[0] == mark for x in todo):
+            todo.pop(0)[1]()
+
+    for j in range(2):
+        later(60, ts, A("MP3", 7 + 14 * j, 21 + 14 * j), A("one", 0, 14), mask("c%d" % j), OP.mult)
+    later(60, cp, A("MP3", 39, 67), A("MP3", 7, 35))
     later(60, tr, A("DT", 0, 128), A("DKR", 16, 144))
     later(60, tr, A("DT", 128, 256), A("DKR", 0, 128))
-    later(60, fill, A("CUR", 31, 128, 64), BIG)
-    later(60, fill, A("CUR", 63, 128, 64), -BIG)
-    later(60, fill, A("DR", 128, 384, 32), -BIG)
-    later(60, fill, A("DR", 256 + 63, 384, 64), -BIG)
-    later(60, fill, A("DR", 384, 496, 56), -BIG)
-    later(60, fill, A("K5", 0, 8), BIG)
-    later(60, fill, A("K5", 120, 128), -BIG)
+    later(60, cp, A("MP3", 71, 131), A("MP3", 7, 67))
+    later(-3, lambda: None)
+    later(60, tr, A("MT", 192, 320), A("MR", 192, 320))
+    later(60, ts, A("CK", 0, 8), A("DT", 0, 256, 32), -14.0, OP.add)
+    later(60, cp, A("MK", 6, 10), A("MT", 192, 320, 32))
+    for name, a, b, val, st in (("CUR", 286 + 31, 416, BIG, 64), ("CUR", 286 + 63, 416, -BIG, 64), ("DR", 256 + 63, 384, -BIG, 64),
+                                ("DR", 384, 496, -BIG, 56), ("K5", 0, 8, BIG, 1), ("K5", 120, 128, -BIG, 1)):
+        later(60, fill, A(name, a, b, st), val)
+    later(60, fill, AQ("QC", 2, 0, 1, 1, 2), float(QS))
+    for h in range(2):
+        later(60, fill, AQ("QC", 2 * h, 2, 3, 1, 2), -1.0 if h else 1.0)
+        later(60, fill, AQ("K6", 2 * h, QS, 128, 1, 2), BIG if h else -BIG)
     for b in range(4):
         later(140, quant, A("qe", 128 * b, 128 * b + 128), A("se", 128 * b, 128 * b + 128), A("eb", 3 - b, 515 - b))
     for c0 in range(128, 544, 128):
         later(120, tr, A("CL", c0, min(c0 + 128, 544)), A("RW", c0, min(c0 + 128, 544)))
-    later(60, fill, AQ("QC", 2, 0, 1, 1, 2), float(QS))
-    later(60, fill, AQ("QC", 2, 2, 3, 1, 2), 128.0)
     later(60, cp, A("LS", 4, 17), A("CL", 128, 544, 32))
     for a in (1, 3):
         later(60, fill, AQ("QC", a, 4, 5), float(HALF))
-        later(60, fill, AQ("QC", a, 6, 7), 256.0)
 
     def weights(lev):
         if lev == 6:
@@ -401,17 +407,21 @@ def rank_program(g, core, T, topo):
             later(140, quant, A("qv", 0, 128), A("pv", 0, 128), A("vt", 0, 512))
             return
         for a in range(4):
-            later(60, fill, AQ("wt7", a, 264 + 128 * (a % 2), 268 + 128 * (a % 2) - a // 2), -1.0 if a % 2 else 1.0)
-        later(200, quant, A("q7", 0, 194), A("s7", 0, 194), A("wt7", 0, 776))
+            later(60, fill, AQ("QC", a, 6, 7), -1.0 if a % 2 else 1.0)
+        for a in range(2):
+            later(60, fill, AQ("QC", a, 7, 8), 1.0 if a else -1.0)
+        for a in range(4):
+            later(60, fill, AQ("wt7", a, 408 + 4 * (a % 2), 412 + 4 * (a % 2) - a // 2), -1.0 if a % 2 else 1.0)
+        later(140, quant, A("q7", 0, 134), A("s7", 0, 134), A("wt7", 0, 536))
 
+    quant(A("qu", 0, 128), A("su", 0, 128), A("ut", 0, 512))
     for j in range(4):
         ts(A("MP", 7 * j, 7 * j + 7), A("one", 0, 7), mask("b%d" % j), OP.mult)
-    quant(A("qu", 0, 128), A("su", 0, 128), A("ut", 0, 512))
-    for a in range(4):
-        cp(AQ("PL", a, 0, 28), AQ("pi", 0, 0, 28))
-    pick("qB", "sB", (0, 256), "qu", "su", 128, A("UL", 0, 16))
+    pick("qB", "sB", (0, 128), "qu", "su", 128, A("UL", 0, 8))
 
     LB = 4
+    DBANK = [6, 7, 3, 2]
+    BLK = [1, 2, 7, 14, 28, 56, 112, 224]
 
     def turn2(out, row):
         tr(A(out, 0, 128), A(row, 16, 144))
@@ -423,38 +433,39 @@ def rank_program(g, core, T, topo):
             turn2("TB", "MB")
             first()
             for c0 in (0, 128):
-                scan(A("CS", c0, c0 + 128), A("DB", c0, c0 + 128), A("TB", c0, c0 + 128), -BIG, OP.max, OP.add)
-            new = ind(A("CS", 0, 288), lst("end"))
+                if lev == 3:
+                    scan(back("CS", c0, c0 + 128), back("D3", c0, c0 + 128), back("TB", c0, c0 + 128), BIG, OP.min, OP.add)
+                else:
+                    scan(A("CS", c0, c0 + 128), A("DB", c0, c0 + 128), A("TB", c0, c0 + 128), -BIG, OP.max, OP.add)
+            new = ind(A("CS", 0, 288), lst("two" if lev == 3 else "end"))
             first()
             cp(A("LL", 0, 16), new)
         else:
-            for c0, r0 in ((0, 16), (256, 0)):
-                for i, row in enumerate(("MB", "MB1")):
+            for i, row in enumerate(("MB", "MB1")):
+                for c0, r0 in ((0, 16), (256, 0)):
                     tr(A("TB", c0 + i, c0 + 256, 2), A(row, r0, r0 + 128))
             for c0 in (0, 256):
                 scan(A("C5", c0, c0 + 256), A("D5", c0, c0 + 256), A("TB", c0, c0 + 256), -BIG, OP.max, OP.add)
             new = ind(A("C5", 0, 576), lst("wide"))
             first()
-            ts(A("LL", 0, 16), new, A("QC", 2, 3), OP.add)
-            cp(A("LG", 0, 16), new)
+            cp(A("LL", 0, 16), new)
             act(A("XB", 16, 32), new, bias=A("QC", 0, 1))
         if lev == 2:
-            cp(A("DB", 0, 256, 32), A("CS", 31, 256, 32))
+            until(-3)
+            act(A("MKL", 0, QS), ind(A("MP3", 0, 144), A("LL", 0, 7)))
+            ts(A("D3", 31, 256, 32), A("CS", 31, 256, 32), -7.0, OP.add)
         if lev == 3:
-            tt(A("DB", 0, 256, 32), A("CS", 31, 256, 32), A("DT", 0, 256, 32), OP.add)
+            tt(A("DB", 0, 256, 32), A("CS", 0, 256, 32), A("CK", 0, 8), OP.add)
         if lev == 4:
             ts(A("D5", 0, 512, 64), A("CS", 31, 256, 32), float(QS), OP.add)
-        act(A("XH", 16 * lev, 16 * lev + 16), new)
+        act(A("XH", 16 * lev, 16 * lev + 16), new, bias=-float(BLK[lev]) if lev < 4 else 0.0)
 
     def counts(lev):
         for c0 in (16, 144) if lev == 7 else (16,):
             quant(A("qa", c0, c0 + 128), A("sa", c0, c0 + 128), A("G", 4 * c0, 4 * c0 + 512))
-        views = (("q7", "s7", 66, 16), ("q7", "s7", 64, 0), ("q7", "s7", 2, 128), ("q7", "s7", 0, QS)) if lev == 7 else (("q6", "s6", 2, 16), ("q6", "s6", 0, 0))
+        views = (("q7", "s7", 6, 16), ("q7", "s7", 4, 0), ("q7", "s7", 2, 144), ("q7", "s7", 0, 128)) if lev == 7 else (("q6", "s6", 2, 16), ("q6", "s6", 0, 0))
         for i, (w, ws, a, b) in enumerate(views):
             mm(ps(LB, 0, 128), A(w, a, a + 128), A(ws, a, a + 128), A("qa", b, b + 128), A("sa", b, b + 128), i == 0, i == len(views) - 1)
-
-    def places(lev, base):
-        tt(A("XH", 16 * lev, 16 * lev + 16), ind(A("TW", 0, 160), lst("upper" if lev == 7 else "one")), base, OP.add)
 
     def turn(row, c0, halves=(0, 1)):
         for i in halves:
@@ -465,20 +476,22 @@ def rank_program(g, core, T, topo):
         for i in halves:
             ts(A(dst, step * i, step * i + 16), ind(A("TT", 512 * i, 512 * i + 512), lst(k)), float(add), OP.add)
 
+    def turn_fetch(row, dst, k, step=14):
+        turn(row, 0, (0,))
+        tr(A("TT", 512, 768), A(row, HALF, HALF + 256))
+        fetch(dst, k, HALF, (0,), step)
+        tr(A("TT", 768, 992), A(row, HALF + 16, HALF + 240))
+
     def slots(c0, c1):
-        scatter(A("RN", 0, 480), A("R2", c0, c1), A("IOB", 16 * c0, 16 * c1))
+        scatter(A("RI", 0, 480), A("R2", c0, c1), A("IOB", 16 * c0, 16 * c1))
 
     def lane(t, a, b):
         return A("G", 64 + 4 * a + t, 64 + 4 * b, 4)
 
-    DBANK = [2, 3, 6, 7]
-    PBANK = [0, 1, 4, 5]
-    BLK = [1, 2, 7, 14, 28, 56, 112, 224]
     dst = T.cores[(rank + 1) % len(T.cores)]
     rel = _relays(topo, core, dst)
     eng = topo.engines(core, rel[0])
-    cut = [eng[:len(eng) // 2], eng[len(eng) // 2:]]
-    landed = sum(len(topo.engines(r, core)) for r in _relays(topo, T.cores[rank - 1], core))
+    landed = 2 * len(topo.engines(_relays(topo, T.cores[rank - 1], core)[0], core))
 
     for t in range(ROUNDS):
         last = t == ROUNDS - 1
@@ -487,41 +500,60 @@ def rank_program(g, core, T, topo):
         for i in range(2):
             quant(A(qx, HALF * i, HALF * i + HALF), A(sx, HALF * i, HALF * i + HALF), A("xn" if t else "xt", 896 * i, 896 * i + 896))
         if t == 0:
+            for a in range(4):
+                cp(AQ("PL", a, 0, 28), AQ("pi", 0, 0, 28))
             tr(A("CL", 0, 128), A("RW", 0, 128))
             cp(A("MP", 32, 64), A("MP", 0, 32))
         for i in range(2):
             o = (HALF * i, HALF * i + HALF)
             if t == 0:
                 pick(qp, sp, o, qx, sx, C, A("PL", 14 * i, 14 * i + 14))
-            mm(ps(i, 0, HALF), A("qB", 0, 128), A("sB", 0, 128), A(qp, *o), A(sp, *o))
+            for k in range(2):
+                c0 = HALF * i + 96 * k
+                mm(ps(2 * i + k, 0, 128), A("qB", 0, 128), A("sB", 0, 128), A(qp, c0, c0 + 128), A(sp, c0, c0 + 128))
+        if t == 0:
+            pick("qB", "sB", (128, 256), "qu", "su", 128, A("UL", 8, 16))
         mm(ps(5, 0, C), A("qB", 128, 256), A("sB", 128, 256), A(qp, 0, C), A(sp, 0, C))
 
         def scores(h, blocks=range(4), by=act):
             p = (32 * (h % 4), 32 * (h % 4) + 32)
             for k in blocks:
                 a = BLOCK[k]
-                if h < 4:
-                    by(AQ("BQ", a, QS * h, QS * h + QS), ps(k // 2, QS * (k % 2), QS * (k % 2) + QS, 1, *p))
-                elif h < 7:
-                    by(AQ("BQ", a, QS * h, QS * h + QS), ps(5, QS * k, QS * k + QS, 1, *p), -1.0 if h == 6 and a > 1 else 1.0)
+                bank, c0 = k, 16 * (k % 2)
+                if h == 1:
+                    by(A("BQ", QS, 2 * QS, 1, 32 * a, 32 * a + 16), ps(bank, c0, c0 + QS, 1, 32, 48))
+                elif h < 4:
+                    by(AQ("BQ", a, QS * h, QS * h + QS), ps(bank, c0, c0 + QS, 1, *p))
                 else:
-                    by(AQ("B7", k, 0, HALF), ps(5, HALF * (k % 2), HALF * (k % 2) + HALF, 1, *p), -1.0 if k % 2 else 1.0)
-
-        def unpack(b, q, s):
-            mm(ps(DBANK[b], 0, C), A("qe", 128 * b, 128 * b + 128), A("se", 128 * b, 128 * b + 128), A(q, 0, C), A(s, 0, C))
+                    by(AQ("BQ", a, QS * h, QS * h + QS), ps(5, QS * k, QS * k + QS, 1, *p))
 
         def halves(b):
-            unpack(b, qp, sp)
+            mm(ps(DBANK[b], 0, C), A("qe", 128 * b, 128 * b + 128), A("se", 128 * b, 128 * b + 128), A(qp, 0, C), A(sp, 0, C))
             act(A("HB", C * b, C * b + C), ps(DBANK[b], 0, C), 0.5)
 
-        scores(0, (0, 1), cp)
+        if last:
+            for i in range(2):
+                for c0, c1, r0 in ((0, 256, 0), (256, 480, 16)):
+                    r0 += 480 * t + HALF * i
+                    later(110, tr, A("TT", 512 * i + c0, 512 * i + c1), A("COL", r0, r0 + c1 - c0))
+            for i in range(2):
+                later(130, fetch, "R2", "last", HALF + 16, (i,))
+        done = [0 if last else 28]
+
+        def spare(n):
+            if done[0] < 28:
+                first(1000)
+                slots(done[0], min(28, done[0] + n))
+                done[0] += n
+
+        first(250 if t else 0)
         if t == 0:
             cp(A("LS", 0, 4), A("CL", 0, 128, 32))
             cp(A("MP", 64, 128), A("MP", 0, 64))
-            first(120)
-        scores(0, (2, 3), cp)
-        scores(1, (0, 1))
-        scores(1, (2,), cp)
+        scores(0, (0, 2), cp)
+        scores(0, (1, 3))
+        scores(1, (1, 3))
+        scores(1, (0,), cp)
         now = A("COL", 480 * t + 16, 480 * t + 16 + C)
 
         def background(lev):
@@ -533,10 +565,10 @@ def rank_program(g, core, T, topo):
                 if t == 0:
                     const("D5", 0, 512, -BIG)
                     const("G", 0, 576, 0.0)
-                else:
-                    act(now, ind(A("COL", 480 * t - 464, 480 * t - 16), A("PL", 0, 28)))
             if lev == 4:
                 scores(6)
+                if t:
+                    const("W7", 0, HALF, -BIG)
             if lev == 5:
                 if t == 0:
                     act(A("QC", 1, 2), col("h16"), bias=A("QC", 0, 1))
@@ -562,76 +594,63 @@ def rank_program(g, core, T, topo):
                     act(now, ind(A("IOB", 0, C), A("PL", 0, 28)))
 
         V = lambda n: A("TMP", 56 * n, 56 * n + 56)
-        H = lambda n: A("TMP", 28 * n, 28 * n + 28)
-        four = lambda name, i: A(name, 16 + i, 128, 4)
-        s0, s1 = [[A("BQ", QS * h + i, QS * h + QS, 2) for i in range(2)] for h in range(2)]
+        s0 = [A("BQ", i, QS, 2) for i in range(2)]
         tt(V(0), s0[1], s0[0], OP.is_lt)
-        scores(1, (3,), cp)
+        scores(1, (2,), cp)
         scores(2)
         ts(A("PR", 0, QS, 2), V(0), 2 * BIG, OP.mult, -BIG, OP.add)
         ts(A("PR", QS + 1, 2 * QS, 2), V(0), -2 * BIG, OP.mult, BIG, OP.add)
-        tt(A("G0", 16, 128, 2), A("PH", 0, QS, 2), V(0), OP.add)
+        tt(A("G3", 0, 336, 6), A("PH", 0, QS, 2), V(0), OP.add)
+        tt(A("G3", 3, 336, 6), A("PH", 1, QS, 2), V(0), OP.subtract)
         scan(back("TMP", QS, 2 * QS), back("PR", 0, QS), back("BQ", QS, 2 * QS))
         scan(A("TMP", 2 * QS, 3 * QS), A("PR", QS, 2 * QS), A("BQ", QS, 2 * QS))
-        tt(A("G0", 17, 128, 2), A("PH", 1, QS, 2), V(0), OP.subtract)
+        first()
         key = lambda i: A("TMP", QS * (1 + i % 2) + i, QS * (2 + i % 2), 4)
-        tt(H(14), key(0), key(2), OP.is_gt)
-        tt(H(15), key(0), key(3), OP.is_gt)
-        tt(H(16), key(1), key(2), OP.is_gt)
-        tt(H(17), key(1), key(3), OP.is_gt)
-        tt(H(18), four("G0", 0), H(14), OP.add)
-        tt(H(19), four("G0", 3), H(15), OP.subtract)
-        tt(H(20), four("G0", 1), H(16), OP.add)
-        tt(H(21), four("G0", 2), H(14), OP.subtract)
-        tt(four("GR", 0), H(18), H(15), OP.add)
-        tt(four("GR", 3), H(19), H(17), OP.subtract)
-        tt(four("GR", 1), H(20), H(17), OP.add)
-        tt(four("GR", 2), H(21), H(16), OP.subtract)
-        tr(A("TX", 0, 128), A("G0", 16, 144))
-        turn2("T1", "GR")
-        tr(A("TX", 128, 256), A("G0", 0, 128))
-        first(60)
+        for i, j in ((0, 2), (2, 0), (0, 3), (2, 1), (1, 2), (3, 0), (1, 3), (3, 1)):
+            tt(A("G3", 3 * i + 1 + j % 2, 336, 12), key(i), key(j), OP.is_gt if i < 2 else OP.is_ge)
+        first()
+        scan(A("GR", 48, 384), A("R3", 0, 336), A("G3", 0, 336), 0.0, OP.mult, OP.add)
+        first()
+        tr(A("T1", 0, 128), A("GR", 50, 432, 3))
+        tr(A("T1", 128, 256), A("GR", 2, 384, 3))
+        first(120)
         cp(A("LL", 0, 16), ind(A("T1", 0, 288), lst("two")))
         cp(A("DB", 0, 256, 32), A("T1", 0, 256, 32))
         first(60)
-        act(A("LR", 16, 128), ind(A("LC", 0, 128), A("LL", 0, 7)))
         act(A("MKL", 0, QS), ind(A("MP", 0, 128), A("LL", 0, 7)))
         act(A("XH", 16, 32), ind(A("T1", 0, 288), lst("two")))
-        act(A("XH", 0, 16), ind(A("TX", 0, 288), lst("two")))
+        act(A("XH", 0, 16), ind(A("T1", 16, 288), lst("two")))
 
         for lev in range(2, 6):
             w = BLK[lev]
             if t == 0 and lev == 5:
                 weights(6)
-            n, cur, key = (QS, "CU5", A("K5", 8, 120)) if lev == 5 else (128, "CUR", A("KEY", 0, 128))
-            scatter(A(cur, 0, 128), A("LL", 0, 7), A("BQ", QS * lev, QS * lev + QS))
+            n, cur, c0, up = ((128, "CUR", 0, 0), (128, "CUR", 128, 7), (128, "CUR", 272, 14), (QS, "CU5", 0, 0))[lev - 2]
+            key = A("K5", 8, 120) if lev == 5 else A("KEY", up * (lev == 4), 128 + up * (lev == 4))
+            scatter(A(cur, c0, c0 + (128 if lev in (2, 5) else 144)), A("LL", 0, 7), A("BQ", QS * lev, QS * lev + QS))
             first()
-            scan(key, A("DR", 128 * (lev - 2), 128 * (lev - 2) + n), A(cur, 0, n))
+            if lev > 2:
+                spare(2)
             one = lambda b: A("TQ", 32 * b, 32 * b + 1)
             if lev > 3:
-                act(A("KS", 0, QS), ind(key, A("LL", 0, 7)))
-            if lev == 2:
-                turn2("TL", "LR")
-            else:
+                scan(key, A("DR", 128 * (lev - 2), 128 * (lev - 2) + n), A(cur, c0 + up, c0 + up + n))
+                act(A("KS", 0, QS), ind(key if lev == 5 else A("KEY", 0, 144), A("LL", 0, 7)))
                 first()
-            tr(A("TQ", 0, 128), A("K5" if lev == 5 else "KEY", 0, 128))
-            if lev > 2:
-                first(260 if lev > 3 else 150)
-            if last and lev > 3:
-                turn("COL", 480 * t, (lev - 4,))
-                later(100, fetch, "R2", "last", HALF + 16, (lev - 4,))
-            if lev == 2:
-                cp(A("L2", 0, 16), ind(A("TL", 0, 288), lst("two")))
-                for b in range(4):
-                    for j in range(2):
-                        ts(A("MC", 128 * j + 32 * b, 128 * j + 32 * b + 28), A("KEY", 32 * b, 32 * b + 28), one(b), OP.is_lt if j else OP.is_gt)
-                tt(A("MB", 16, 128), ind(A("MC", 0, 256), A("L2", 0, 7)), A("MKL", 0, QS), OP.mult)
-            elif lev == 3:
-                for b in range(4):
-                    for j in range(2):
-                        a = 32 * b + w * j
-                        ts(A("MC", a, a + w), A("KEY", a, a + w), one(b), OP.is_lt if j else OP.is_gt, mask("c%d" % j), OP.mult)
-                cp(A("MB", 16, 128), ind(A("MC", 0, 128), A("LL", 0, 7)))
+                tr(A("TQ", 0, 128), A("K5", 0, 128) if lev == 5 else key)
+                first(260)
+                spare(4)
+            if lev < 4:
+                for a in (0, 64):
+                    scan(A("KEY", a, a + 64), A("DR", 128 * (lev - 2) + a, 128 * (lev - 2) + a + 64), A(cur, c0 + up + a, c0 + up + a + 64))
+                first(100)
+                for a in (0, 64):
+                    tr(A("TQ", a, a + 64), A("KEY", a, a + 64))
+                first(100)
+                for a in (0, 64):
+                    tt(A("MC", up + a, up + a + 64), A("KEY", a, a + 64), A("TQ", a, a + 64), OP.subtract)
+                first()
+                tt(A("MB", 16, 128), ind(A("MC", 0, 144), A("LL", 0, 7)), A("MKL", 0, QS), OP.is_gt)
+                spare(2)
             elif lev == 4:
                 for b in range(4):
                     ts(A("MB", 16 + w * b, 16 + w * b + w), A("KS", w * b, w * b + w), one(b ^ 1), OP.is_lt if b % 2 else OP.is_gt, mask("n28" if b % 2 else "p28"), OP.mult)
@@ -643,152 +662,168 @@ def rank_program(g, core, T, topo):
             background(lev)
             sums(lev)
 
-        scatter(A("W6", 0, 256), A("LL", 0, 7), A("BQ", QS * 6, QS * 7))
+        scatter(A("W6", 0, 128), A("LL", 0, 7), A("BQ", QS * 6, QS * 7))
         if t == 0:
             weights(7)
         first()
-        scan(A("K6", 0, QS), A("W6", 128, 128 + QS), A("W6", 0, QS))
-        act(A("KS", 0, QS), ind(A("K6", 0, 128), A("LG", 0, 7)))
+        spare(2)
+        scan(A("K6", 0, QS), A("W6", 0, QS), A("W6", 0, QS), -BIG, OP.max, OP.max)
+        act(A("KS", 0, QS), ind(A("K6", 0, 128), A("LL", 0, 7)), A("QC", 2, 3))
         tt(A("Y", 0, 32), ind(A("XH", 0, 128), lst("pairs", 2)), A("OFS", 0, 32), OP.add)
         for h in range(2):
-            tr(AQ("TQ", 2 * h, 0, 128, 1, 2), AQ("K6", 2 - 2 * h, 0, 128, 1, 2))
+            tr(AQ("T6", 2 * h, 128 * h, 128 * h + 128, 1, 2), AQ("K6", 2 - 2 * h, 0, 128, 1, 2))
         background(6)
         first()
         for b in range(4):
-            ts(lane(b, 0, QS), A("KS", 0, QS), A("TQ", 32 * b, 32 * b + 1), OP.add, 0.0, OP.is_gt)
+            ts(lane(b, 0, QS), A("KS", 0, QS), A("T6", 128 + 32 * b, 129 + 32 * b), OP.add, A("T6", 32 * b, 32 * b + 1), OP.is_gt)
         first()
         counts(6)
         if last:
-            slots(0, 6)
+            slots(done[0], 28)
         else:
             first(400)
         tr(A("TW", 0, 128), ps(LB, 0, 128))
         first()
-        places(6, A("XB", 16, 32))
+        tt(A("XH", 96, 112), ind(A("TW", 0, 160), lst("one")), A("XB", 16, 32), OP.add)
         first()
 
-        for h in range(2):
-            for d in range(2):
-                ts(AQ("LH", 2 * d, 7 * h, 7 * h + 7, 1, 2), AQ("XH", 2 * h, 96, 103, 1, 2), AQ("QC", 2 * d, 6, 7, 1, 2), OP.add)
+        cp(A("LL", 0, 8), A("XH", 96, 104))
+        for k in range(4):
+            if k == 3:
+                scatter(A("W7", 0, HALF), A("LL", 0, 7), A("BQ", QS * 7, QS * 8))
+            cp(AQ("LG", 2 * (k % 2), 7 * (k // 2), 7 * (k // 2) + 7, 1, 2), AQ("XH", 2 * (k // 2), 96, 103, 1, 2))
+        first(100)
+        for d in range(2):
+            scan(AQ("K7", 2 * d, 0, HALF, 1, 2), AQ("W7", 0, 0, HALF, 1, 2), AQ("W7", 2, 0, HALF, 1, 2), -BIG, OP.max, OP.max)
+        parts = ((0, 128), (128, HALF))
+        for a, b in parts:
+            act(A("KS", a, b), ind(A("K7", 0, HALF), A("LG", a // 16, b // 16)), A("QC", 6, 7))
+        for a, c0, k0, n in ((0, 0, 0, 128), (1, 96, 0, 128), (2, 0, 128, 96), (3, 128, 128, 96)):
+            tr(AQ("T7", a, c0, c0 + n), AQ("K7", 1 - a % 2, k0, k0 + n))
         first()
-        scatter(A("W7", 0, 512), A("LH", 0, 14), A("B7", 0, HALF))
-        ts(A("LG", 0, 14), A("LH", 0, 14), A("QC", 6, 7), OP.subtract)
-        ts(A("XB", 32, 48), A("XH", 96, 112), A("QC", 4, 5), OP.add)
-        scan(A("K7", 0, HALF), A("W7", 256, 256 + HALF), A("W7", 0, HALF))
-        act(A("KS", 0, HALF), ind(A("K7", 0, 256), A("LG", 0, 14)))
+        flip = AQ("QC", 0, 7, 8, 1, 2)
+        for a, b in parts:
+            act(AQ("SG", 0, a, b, 1, 2), AQ("KS", 0, a, b, 1, 2), flip, AQ("T7", 0, 96, 97, 1, 2), AF.Sign)
+        for a, b in parts:
+            act(AQ("G", 0, 67 + 4 * a, 64 + 4 * b, 4, 2), AQ("SG", 0, a, b, 1, 2), flip, func=AF.Relu)
+        for a, b in parts:
+            for k in range(3):
+                ts(lane(k, a, b), A("KS", a, b), A("T7", 128 + 32 * k, 129 + 32 * k), OP.add, A("T7", 32 * k, 32 * k + 1), OP.is_gt)
         first()
-        for a in range(4):
-            n = 128 if a < 2 else 96
-            tr(AQ("TQ", a, 0, n), AQ("K7", a ^ 1, 128 * (a // 2), 128 * (a // 2) + n))
-        first()
-        act(AQ("RG", 0, 0, HALF, 1, 2), AQ("KS", 0, 0, HALF, 1, 2), bias=AQ("TQ", 0, 96, 97, 1, 2), func=AF.Sign)
-        act(AQ("G", 0, 67, 64 + 4 * HALF, 4, 2), AQ("RG", 0, 0, HALF, 1, 2), func=AF.Relu)
-        for b in range(3):
-            ts(lane(b, 0, HALF), A("KS", 0, HALF), A("TQ", 32 * b, 32 * b + 1), OP.add, 0.0, OP.is_gt)
         counts(7)
+        for a in range(4):
+            ts(AQ("X7", 3, 7 * BLOCK[a], 7 * BLOCK[a] + 7), AQ("XH", a, 96, 103), col("h16", 96, 128), OP.add, float(HALF * (a % 2)), OP.add)
         if last:
-            slots(6, 16)
+            turn("RI", 0)
         first(10000)
         background(7)
-        tr(A("TW", 0, 128), ps(LB, 0, 128))
-        places(7, A("XB", 32, 48))
-        for a in range(4):
-            ts(AQ("RL", 3, 7 * BLOCK[a], 7 * BLOCK[a] + 7), AQ("XH", a, 112, 119), col("h16", 32 * a, 32 * a + 32), OP.add)
+        tr(AQ("TW", 3, 0, 128), ps(LB, 0, 128, 1, 96, 128))
+        if last:
+            fetch("IC", "last", HALF, (0,))
+        tt(A("XF", 0, 32), ind(A("TW", 0, 160), lst("all", 2)), A("X7", 0, 32), OP.add)
+        if last:
+            fetch("IC", "last", HALF, (1,))
+        cp(AQ("RL", 3, 0, 28), AQ("XF", 3, 0, 28))
 
         scatter(A("SIG", 0, 480), A("RL", 0, 28), A("IOB", 0, C))
-        ts(A("CA", 0, 28), A("RL", 0, 28), col("h16"), OP.subtract)
-        turn("SIG", 0, (0,))
-        ts(A("CT", 0, 28), A("CA", 0, 28), float(HALF), OP.is_ge, -float(HALF), OP.mult)
-        fetch("ZL", "own", HALF, (0,), 16)
-        turn("SIG", 0, (1,))
+        for i in (0, 16):
+            ts(A("UW", i, 896, 32), A("RL", 0, 28), col("h16"), OP.subtract, float(HALF), OP.subtract)
+        turn_fetch("SIG", "ZL", "own", 16)
         if not last:
             fetch("PL", "last", HALF, (0,))
         fetch("ZL", "own", HALF, (1,), 16)
-
-        for b in range(4):
-            act(A("GZ", HALF * b, HALF * b + HALF), ind(A("HB", C * b, C * b + C), A("ZL", 0, 14)))
-        qf, sf = "qf%d" % t, "sf%d" % t
         if not last:
             fetch("PL", "last", HALF, (1,))
-            for i in (0, 16):
-                tt(A("UW", i, 896, 32), A("CA", 0, 28), A("CT", 0, 28), OP.add)
-        else:
-            tt(A("CA", 0, 28), A("CA", 0, 28), A("CT", 0, 28), OP.add)
-            for b in range(2):
-                act(A("FB", C * b, C * b + C), ps(DBANK[b], 0, C))
-        for b in range(4):
-            tt(A("ZT", b, 896, 4), ind(A("HB", C * b, C * b + C), A("ZL", 16, 30)), A("GZ", HALF * b, HALF * b + HALF), OP.add)
-        if not last:
-            for a in range(3):
-                cp(AQ("PL", a, 0, 28), AQ("PL", 3, 0, 28))
-            act(A("FB", 0, C), ind(A("HB", 0, C), A("PL", 0, 28)), 2.0)
-            act(A(sf, 0, C), ind(A(sp, 0, C), A("PL", 0, 28)))
+
         zc, zs = "zc%d" % t, "zs%d" % t
-        quant(A(zc, 0, HALF), A(zs, 0, HALF), A("ZT", 0, 896))
+        for a, b in PIECES:
+            for k in range(4):
+                act(A("GZ", HALF * k + a, HALF * k + b), ind(A("HB", C * k, C * k + C), A("ZL", a // 16, b // 16)))
 
-        hazards("g", [(zc, 0, 128, 0, HALF, 1), (zs, 0, 128, 0, HALF, 1)], [])
-        tf = []
-        for i in range(2):
+        def pair(i, k):
+            a, b = PIECES[i]
+            tt(A("ZT", 4 * a + k, 4 * b, 4), ind(A("HB", C * k, C * k + C), A("ZL", 16 + a // 16, 16 + b // 16)), A("GZ", HALF * k + a, HALF * k + b), OP.add)
+
+        def send(i):
+            a, b = PIECES[i]
+            quant(A(zc, a, a + 128), A(zs, a, a + 128), A("ZT", 4 * a, 4 * a + 512))
+            hazards("g", A(zc, a, b)[1], [])
+            sem = T.sem["r%s%d" % ("ab"[i], t)]
             rid, pid = topo.addr(rel[i], core)
-            s_, d_ = T[zc][:, i * QS:(i + 1) * QS].bitcast(dt.uint8), T["hc%d" % t][:, :].bitcast(dt.uint8)
-            tf.append(RemoteDMATransfer(dst_ids=[DstId(rid=rid, pnc=pid)], dma_engine_mask=_bits(cut[i]), remote_sem=T.sem["rc%d" % t], src=s_, dst=d_))
-        g.remote_dma_fused(tf, local_sem=T.sem.snd)
-        rid, pid = topo.addr(rel[2], core)
-        g.remote_dma(T["hs%d" % t][:, :], T[zs][:, :], T.sem["rc%d" % t], T.sem.snd, pid, rid, _bits(eng))
+            g.remote_dma(T["hc%d" % t][:, a:b].bitcast(dt.uint8), T[zc][:, a:b].bitcast(dt.uint8), sem, T.sem.snd, pid, rid, topo.mask(core, rel[i]))
+            rid, pid = topo.addr(rel[2 + i], core)
+            g.remote_dma(T["hs%d" % t][:, a:b], T[zs][:, a:b], sem, T.sem.snd, pid, rid, topo.mask(core, rel[2 + i]))
 
+        nxt = "IC" if last else "PL"
+        pair(0, 0)
         if not last:
-            cp(A("NI", 0, 28), A("PL", 0, 28))
-            tr(A("UT", 0, C), A("UW", 0, C))
-            ts(A("NA", 0, 28), A("NI", 0, 28), 496, OP.bitwise_and)
-            tr(A("UT", C, 896), A("UW", C, 896))
-            tt(A("NS", 0, 28), A("NI", 0, 28), A("NA", 0, 28), OP.add)
-            ts(A("NL", 0, 28), A("NS", 0, 28), col("h16"), OP.add)
-            codes(qf, (0, C), qp, C, A("PL", 0, 28))
-            for a, b in ((0, 16), (16, 28)):
-                act(A("RN", 16 + 16 * a, 16 + 16 * b), ind(A("UT", 0, 896), A("NL", a, b)))
-            act(A("FB", C, 2 * C), ind(A("HB", C, 2 * C), A("PL", 0, 28)), 2.0)
-            turn("RN", 0)
-            fetch("RM", "mine", 0)
-        else:
-            cp(A("RM", 0, 28), A("CA", 0, 28))
-            slots(16, 28)
-            for i in range(2):
-                act(A("OD", HALF * i, HALF * i + HALF), ind(now, A("ZL", 16 * i, 16 * i + 14)), bias=col("h224"))
-            dmas("y", [(ext(T.od[:, :]), (T.OD[0:128:16, :], A("OD", 0, C)[1]))], "dd")
-            turn("RN", 0)
-            fetch("IC", "last", HALF)
+            for k in range(3):
+                cp(AQ("PL", k, 0, 28), AQ("PL", 3, 0, 28))
+        pair(0, 1)
+        pair(0, 2)
+        cp(A("NI", 0, 28), A(nxt, 0, 28))
+        pair(0, 3)
+        pair(1, 0)
+        ts(A("NA", 0, 28), A("NI", 0, 28), 496, OP.bitwise_and)
+        send(0)
+        pair(1, 1)
+        tt(A("NS", 0, 28), A("NI", 0, 28), A("NA", 0, 28), OP.add)
+        pair(1, 2)
+        pair(1, 3)
+        ts(A("NL", 0, 28), A("NS", 0, 28), col("h16"), OP.add)
+        tr(A("UT", 0, C), A("UW", 0, C))
+        send(1)
+
+        act(A("FB", 0, C), ind(A("HB", 0, C), A(nxt, 0, 28)), 2.0)
+        tr(A("UT", C, 896), A("UW", C, 896))
+        for a, b in ((0, 16), (16, 28)):
+            act(A("RN", 16 + 16 * a, 16 + 16 * b), ind(A("UT", 0, 896), A("NL", a, b)))
+        for b in (2, 3):
+            ts(A("FK", C * (b - 2), C * (b - 2) + HALF), A("GZ", HALF * b, HALF * b + HALF), 64.0, OP.mult)
+        ts(A("FK", HALF, C), ind(A("HB", 2 * C, 3 * C), A("ZL", 16, 30)), 64.0, OP.mult)
+        act(A("FK", C + HALF, 2 * C), ind(A("HB", 3 * C, 4 * C), A("ZL", 16, 30)), 64.0)
+        act(A("FB", C, 2 * C), ind(A("HB", C, 2 * C), A(nxt, 0, 28)), 2.0)
+        if not last:
+            act(A("COL", 480 * t + 496, 480 * t + 496 + C), ind(now, A("PL", 0, 28)))
+        turn_fetch("RN", "CA", "mine")
+        fetch("CA", "mine", HALF, (1,))
+        ts(A("CT", 0, 28), A("CA", 0, 28), float(HALF), OP.is_ge, -float(HALF), OP.mult)
+        cp(A("RK", 0, 28), A("CA", 0, 28))
 
         lc, ls = "lc%d" % t, "ls%d" % t
-        wait("t", "lz%d" % t, landed)
-        for b in (0, 2, 1, 3):
-            mm(ps(PBANK[b], 0, HALF), A("wq", 128 * b, 128 * b + 128), A("wp", 128 * b, 128 * b + 128), A(lc, 0, HALF), A(ls, 0, HALF))
-            if b > 1:
-                act(A("PB", HALF * b, HALF * b + HALF), ps(PBANK[b], 0, HALF), 0.03125)
-            else:
-                ts(A("PB", HALF * b, HALF * b + HALF), ps(PBANK[b], 0, HALF), 0.03125, OP.mult)
-        if not last:
-            for b in (2, 3):
-                unpack(b, qf, sf)
-        act(A("RG", 0, C), ind(A("PB", 2 * HALF, 3 * HALF), A("RM", 0, 28)))
+        for i, (a, b) in enumerate(PIECES):
+            wait("t", "l%s%d" % ("ab"[i], t), landed)
+            for k in (2, 0, 3, 1):
+                bank = 4 * i + k
+                mm(ps(bank, 0, 128), A("wq", 128 * k, 128 * k + 128), A("wp", 128 * k, 128 * k + 128), A(lc, b - 128, b), A(ls, b - 128, b))
+                got = ps(bank, 128 - (b - a), 128)
+                if k < 2:
+                    act(A("PB", HALF * k + a, HALF * k + b), got, 0.03125)
+                else:
+                    for c0 in (C * (k - 2), C * (k - 2) + HALF):
+                        tt(A("PK", c0 + a, c0 + b), got, A("FK", c0 + a, c0 + b), OP.add)
+                    if i == 0 and k == 2:
+                        tt(A("NS", 0, 28), A("CA", 0, 28), A("CT", 0, 28), OP.add)
+                    if i == 0 and k == 3:
+                        cp(A("RM", 0, 28), A("NS", 0, 28))
+        act(A("xn", 2, 1792, 4), ind(A("PK", 0, C), A("RK", 0, 28)), 0.03125)
         for i in range(2):
-            act(A("RG", C + HALF * i, C + HALF * i + HALF), ind(A("PB", 3 * HALF, 4 * HALF), A("RM", 14 * i, 14 * i + 14)))
-        for b in (0, 1):
-            tt(A("xn", b, 1792, 4), ind(A("PB", HALF * b, HALF * b + HALF), A("RM", 0, 28)), A("FB", C * b, C * b + C), OP.add)
-        tt(A("xn", 2, 1792, 4), A("RG", 0, C), ps(DBANK[2], 0, C), OP.add)
+            act(A("xn", 896 * i + 3, 896 * i + 896, 4), ind(A("PK", C, 2 * C), A("RK", 14 * i, 14 * i + 14)), 0.03125)
+        tt(A("xn", 0, 1792, 4), ind(A("PB", 0, HALF), A("RM", 0, 28)), A("FB", 0, C), OP.add)
         for i in range(2):
-            tt(A("xn", 896 * i + 3, 896 * i + 896, 4), A("RG", C + HALF * i, C + HALF * i + HALF), ps(DBANK[3], HALF * i, HALF * i + HALF), OP.add)
+            tt(A("xn", 896 * i + 1, 896 * i + 896, 4), ind(A("PB", HALF, C), A("RM", 14 * i, 14 * i + 14)), A("FB", C + HALF * i, C + HALF * i + HALF), OP.add)
 
     for i in range(2):
-        quant(A("qx3", HALF * i, HALF * i + HALF), A("sx3", HALF * i, HALF * i + HALF), A("xn", 896 * i, 896 * i + 896))
-    for i in range(2):
         o = (HALF * i, HALF * i + HALF)
-        pick("qf2", "sf2", o, "qx3", "sx3", C, A("IC", 14 * i, 14 * i + 14))
-        mm(ps(i, 0, HALF), A("qv", 0, 128), A("pv", 0, 128), A("qf2", *o), A("sf2", *o))
-        dmas("y", [(ext(T.oc[:, 896 * i:896 * i + 896]), bc(A("qf2", *o)))], "dc%d" % i)
-    dmas("s", [(ext(T.osc[4 * k:4 * k + 4, :]), A("sf2", 0, C, 1, 32 * k, 32 * k + 4)) for k in range(4)], "dq")
+        quant(A("qx3", *o), A("sx3", *o), A("xn", 896 * i, 896 * i + 896))
+        mm(ps(i, 0, HALF), A("qv", 0, 128), A("pv", 0, 128), A("qx3", *o), A("sx3", *o))
+        dmas("y", [(ext(T.oc[:, 896 * i:896 * i + 896]), bc(A("qx3", *o)))], "dc%d" % i)
     for i in range(2):
+        act(A("OD", HALF * i, HALF * i + HALF), ind(now, A("ZL", 16 * i, 16 * i + 14)), bias=col("h224"))
         cp(A("yb", HALF * i, HALF * i + HALF), ps(i, 0, HALF))
         dmas("y", [(ext(T.y[:, HALF * i:HALF * i + HALF]), A("yb", HALF * i, HALF * i + HALF))], "dy%d" % i)
+    dmas("s", [(ext(T.od[:, :]), (T.OD[0:128:16, :], A("OD", 0, C)[1]))], "dd")
+    dmas("s", [(ext(T.osc[4 * k:4 * k + 4, :]), A("sx3", 0, C, 1, 32 * k, 32 * k + 4)) for k in range(4)], "dq")
     for sem in count:
         wait("g", sem, count[sem])
-    wait("g", "snd", 2 * len(eng) * ROUNDS)
+    wait("g", "snd", 4 * len(eng) * ROUNDS)

from concourse.mybir import dt, AluOpType, ActivationFunctionType

OP = AluOpType
AF = ActivationFunctionType
ROUNDS, C, HALF, QS = 3, 448, 224, 112
BIG = 1e29
LIFT = 64
TINY = 2.0 ** -120
BLOCK = (0, 2, 1, 3)
PIECES = ((0, 128), (128, HALF))

SCRATCH = {}


def _sb(name, n, ty="float32"):
    SCRATCH[name] = ("sbuf", [128, n], ty)


def _mx(c, s, n):
    _sb(c, n, "float8_e4m3fn_x4")
    _sb(s, n, "uint8")


PARTS = {}
_z = 0
for _n, _w in (("MB", 144), ("GR", 432), ("DKR", 144), ("MB1", 144), ("MP", 128), ("MP3", 144), ("T1", 288), ("CS", 288)):
    PARTS[_n] = ("Z", _z)
    _z += _w
for _k, _n in enumerate(("MK", "QC", "OFS", "Y", "CK", "CA", "CT", "NS", "XF", "X7")):
    PARTS[_n] = ("S", 32 * _k)
for _n, _w in (("Z", _z), ("xt", 1792), ("xn", 1792), ("ut", 512), ("vt", 512), ("one", 516), ("eb", 516), ("wt6", 520), ("wt7", 536), ("G", 1088),
               ("FB", 896), ("FK", 896), ("HB", 1792), ("ZT", 1024), ("IOB", C), ("SIG", 480), ("TT", 1024), ("COL", 3 * 480), ("MR", 320), ("MT", 320),
               ("PH", QS), ("MKL", QS), ("TB", 512), ("DB", 256), ("D3", 256), ("D5", 512), ("C5", 576), ("DT", 288), ("UW", 896), ("UT", 896),
               ("RN", 480), ("RI", 480), ("G3", 336), ("R3", 336)):
    _sb(_n, _w, "bfloat16")
for _n, _w in (("RW", 544), ("CL", 544), ("K5", 128), ("S", 320), ("PR", 2 * QS), ("BQ", 8 * QS),
               ("CUR", 416), ("CU5", 128), ("KEY", 144), ("KS", HALF), ("TQ", 128), ("T7", HALF), ("MC", 144), ("T6", 256), ("TMP", 336), ("DR", 512),
               ("TW", 160), ("XH", 128), ("XB", 32), ("W6", 128), ("K6", 128), ("W7", HALF), ("K7", HALF), ("SG", HALF),
               ("ZF", 260), ("OD", C), ("GZ", 896), ("PB", C), ("PK", 2 * C), ("yb", C)):
    _sb(_n, _w)
for _n, _w in (("pi", 28), ("ii", 16), ("NI", 28), ("NA", 28)):
    _sb(_n, _w, "int32")
for _n, _w in (("LS", 20), ("LL", 16), ("LG", 16), ("RK", 28), ("RL", 28), ("RM", 32), ("R2", 32), ("ZL", 32), ("PL", 32), ("IC", 32),
               ("UL", 16), ("NL", 28)):
    _sb(_n, _w, "uint16")
_mx("qu", "su", 128)
_mx("qB", "sB", 256)
_mx("qv", "pv", 128)
_mx("wq", "wp", 512)
_mx("q6", "s6", 130)
_mx("q7", "s7", 134)
_mx("qe", "se", 512)
_mx("qa", "sa", 272)
for _t in range(ROUNDS + 1):
    _mx("qx%d" % _t, "sx%d" % _t, C)
_mx("qp0", "sp0", C)
for _t in range(ROUNDS):
    _mx("zc%d" % _t, "zs%d" % _t, 256)
    _mx("lc%d" % _t, "ls%d" % _t, HALF)
    _mx("hc%d" % _t, "hs%d" % _t, HALF)
SCRATCH["ps"] = ("psum", [128, 4096], "float32")

SEMAPHORES = (["sv", "st", "ss", "sg", "snd", "dx", "dx2", "dp", "du", "dw", "dv", "dy0", "dy1", "dc0", "dc1", "dd", "dq"]
              + ["%s%d" % (_a, _t) for _a in ("ra", "rb", "la", "lb") for _t in range(ROUNDS)])


def _relays(topo, src, dst):
    ok = [c for c in topo.cores_of(src) if c != src and topo.may_write(c, dst)]
    near = [c for c in ok if topo.die(c) == topo.die(src)]
    far = [c for c in ok if topo.die(c) != topo.die(src)]
    return [far[0], near[0], far[1], near[1]]


def _relay_program(g, core, T, topo):
    n = len(T.cores)
    for r in range(n):
        dst = T.cores[(r + 1) % n]
        rel = _relays(topo, T.cores[r], dst)
        if core not in rel:
            continue
        h = rel.index(core)
        rid, pid = topo.addr(dst, core)
        m = topo.mask(core, dst)
        k = len(topo.engines(core, dst))
        came = len(topo.engines(T.cores[r], core))
        a, b = PIECES[h % 2]
        for t in range(ROUNDS):
            g.wait_ge(T.sem["r%s%d" % ("ab"[h % 2], t)], came)
            sem = T.sem["l%s%d" % ("ab"[h % 2], t)]
            if h < 2:
                g.remote_dma(T["lc%d" % t][:, a:b].bitcast(dt.uint8), T["hc%d" % t][:, a:b].bitcast(dt.uint8), sem, T.sem.snd, pid, rid, m)
            else:
                g.remote_dma(T["ls%d" % t][:, a:b], T["hs%d" % t][:, a:b], sem, T.sem.snd, pid, rid, m)
        g.wait_ge(T.sem.snd, k * ROUNDS)


def rank_program(g, core, T, topo):
    rank = T.rank_of(core)
    if rank is None:
        _relay_program(g, core, T, topo)
        return
    Q = {"v": g.vector, "t": g.tensor, "s": g.scalar, "g": g, "y": g.sync}
    ESEM = {"v": "sv", "t": "st", "s": "ss", "g": "sg"}
    count = {"sv": 0, "st": 0, "ss": 0, "sg": 0}
    seen = {}
    hist = {}

    def A(name, c0, c1, st=1, p0=0, p1=128):
        if name in PARTS:
            name, c0, c1 = PARTS[name][0], c0 + PARTS[name][1], c1 + PARTS[name][1]
        t = T[name]
        if st == 1:
            ap = t[:, c0:c1] if (p0, p1) == (0, 128) else t[p0:p1, c0:c1]
        else:
            ap = t[:, c0:c1:st] if (p0, p1) == (0, 128) else t[p0:p1, c0:c1:st]
        return (ap, [(name, p0, p1, c0, c1, st)])

    def AQ(name, a, c0, c1, st=1, n=1):
        return A(name, c0, c1, st, 32 * a, 32 * (a + n))

    def back(name, c0, c1):
        if name in PARTS:
            name, c0, c1 = PARTS[name][0], c0 + PARTS[name][1], c1 + PARTS[name][1]
        return (T[name][:, c1 - 1:c0 - 1:-1] if c0 else T[name][:, c1 - 1::-1], [(name, 0, 128, c0, c1, 1)])

    def ps(bank, c0, c1, st=1, p0=0, p1=128):
        x = A("ps", 512 * bank + c0, 512 * bank + c1, st, p0, p1)
        return (x[0], [("ps%d" % bank, 0, 128, 0, 512, 1)])

    def ind(win, off):
        return (win[0].indirect(off[0]), win[1] + off[1])

    def bc(x):
        return (x[0].bitcast(dt.uint8), x[1])

    def u32(x):
        return (x[0].bitcast(dt.uint32), x[1])

    known = {}

    def wait(q, sem, val):
        if seen.get((q, sem), 0) < val:
            Q[q].wait_ge(T.sem[sem], val)
            seen[(q, sem)] = val
            for s, v in known.get((sem, val), ()):
                seen[(q, s)] = max(seen.get((q, s), 0), v)

    def hazards(q, reads, writes):
        need = {}
        for regs, w in ((reads, False), (writes, True)):
            for (n, p0, p1, c0, c1, st) in regs:
                bank = n[:2] == "ps"
                for (eq, sem, val, ew, a0, a1, b0, b1, bs) in hist.get(n, ()):
                    if a0 >= p1 or p0 >= a1 or b0 >= c1 or c0 >= b1:
                        continue
                    if st == bs and (c0 - b0) % st:
                        continue
                    if bank and eq == q and (q == "t" or not ew):
                        continue
                    if not bank and not w and not ew:
                        continue
                    need[sem] = max(need.get(sem, 0), val)
        for sem in sorted(need, key=lambda s: -len(known.get((s, need[s]), ()))):
            wait(q, sem, need[sem])

    def note(q, sem, val, reads, writes):
        for regs, w in ((reads, False), (writes, True)):
            for (n, p0, p1, c0, c1, st) in regs:
                h = hist.setdefault(n, [])
                if w:
                    h[:] = [e for e in h if not (p0 <= e[4] and e[5] <= p1 and c0 <= e[6] and e[7] <= c1 and e[0] == q
                                                 and (st == 1 or (st == e[8] and (c0 - e[6]) % st == 0)))]
                h[:] = [e for e in h if not (e[0] == q and e[1] == sem and e[3] == w and e[4:] == (p0, p1, c0, c1, st))]
                h.append((q, sem, val, w, p0, p1, c0, c1, st))

    def do(q, call, outs, ins):
        reads = [r for x in ins for r in x[1]]
        writes = [r for x in outs for r in x[1]]
        hazards(q, reads, writes)
        sem = ESEM[q]
        count[sem] += 1
        call().then_inc(T.sem[sem], 1)
        known[(sem, count[sem])] = [(k[1], seen[k]) for k in seen if k[0] == q]
        note(q, sem, count[sem], reads, writes)

    def dmas(q, pairs, sem):
        for out, in_ in pairs:
            hazards(q, in_[1], out[1])
        for out, in_ in pairs:
            Q[q].dma_start(out[0], in_[0]).then_inc(T.sem[sem], 16)
        count[sem] = count.get(sem, 0) + 16 * len(pairs)
        for out, in_ in pairs:
            note("d" + sem, sem, count[sem], in_[1], out[1])

    def tt(out, a, b, op):
        do("v", lambda: g.vector.tensor_tensor(out[0], a[0], b[0], op), [out], [a, b])

    def ts(out, a, s1, op0, s2=None, op1=None):
        ins = [a] + [x for x in (s1, s2) if isinstance(x, tuple)]
        v1 = s1[0] if isinstance(s1, tuple) else s1
        v2 = s2[0] if isinstance(s2, tuple) else s2
        if op1 is None:
            do("v", lambda: g.vector.tensor_scalar(out[0], a[0], v1, None, op0), [out], ins)
        else:
            do("v", lambda: g.vector.tensor_scalar(out[0], a[0], v1, v2, op0, op1), [out], ins)

    def cp(out, a):
        do("v", lambda: g.vector.tensor_copy(out[0], a[0]), [out], [a])

    def act(out, a, scale=1.0, bias=0.0, func=None):
        cols = [x for x in (scale, bias) if isinstance(x, tuple)]
        sc, bi = [x[0] if isinstance(x, tuple) else x for x in (scale, bias)]
        if not cols and bi == 0.0:
            if sc == 1.0:
                do("s", lambda: g.scalar.activation(out[0], a[0], func or AF.Copy), [out], [a])
            else:
                do("s", lambda: g.scalar.activation(out[0], a[0], AF.Copy, scale=sc), [out], [a])
        else:
            do("s", lambda: g.scalar.activation(out[0], a[0], func or AF.Identity, bias=bi, scale=sc), [out], [a] + cols)

    def pick(qo, so, o, qi, si, w, off):
        act(A(so, *o), ind(A(si, 0, w), off))
        src = A(qi, 0, w)
        do("v", lambda: g.vector.tensor_copy(u32(A(qo, *o))[0], u32(src)[0].indirect(off[0])), [A(qo, *o)], [src, off])

    def scatter(win, off, vals):
        do("v", lambda: g.vector.tensor_copy(win[0].indirect(off[0]), vals[0]), [win], [vals, off])

    def scan(out, d0, d1, first=BIG, op0=OP.min, op1=OP.max):
        do("v", lambda: g.vector.tensor_tensor_scan(out[0], d0[0], d1[0], first, op0, op1), [out], [d0, d1])

    def tr(out, a):
        do("v", lambda: g.vector.transpose(out[0], a[0]), [out], [a])

    def fill(x, val):
        do("v", lambda: g.vector.memset(x[0], val), [x], [])

    def quant(c, s, a):
        do("v", lambda: g.vector.quantize_mx(c[0], s[0], a[0]), [c, s], [a])

    def mm(out, w, ws, x, xs, start=True, stop=True):
        do("t", lambda: g.tensor.matmul_mx(out[0], w[0], ws[0], x[0], xs[0], start, stop), [out], [w, ws, x, xs])

    def aff(out, in_, pattern, op, val, base, cm):
        do("g", lambda: g.affine_select(out[0], in_[0], pattern, op, val, base, cm), [out], [in_])

    def iota(out, pattern, base, cm=0):
        do("g", lambda: g.iota(out[0], pattern, base, cm, allow_small_or_imprecise_dtypes=True), [out], [])

    def never(name, a, b, val):
        aff(A(name, a, b), A("ZF", 0, b - a), [[0, b - a]], OP.is_equal, val, 1, 0)

    def const(name, a, b, val, st=1):
        for c0 in range(a, b, 512 * st):
            c1 = min(c0 + 512 * st, b)
            act(A(name, c0, c1, st), A("one", 0, len(range(c0, c1, st))), val)

    def ext(ap):
        return (ap, [])

    dmas("s", [(A("ut", 0, 512), ext(T.u[:, :]))], "du")
    dmas("y", [(A("xt", 0, 896), ext(T.x[:, 0:896]))], "dx")
    dmas("s", [(A("xt", 896, 1792), ext(T.x[:, 896:1792]))], "dx2")
    dmas("y", [(A("pi", 0, 28, 1, 16 * h, 16 * h + 16), ext(T.p[:, :])) for h in range(2)], "dp")
    wait("y", "dx", 16)
    dmas("y", [(bc(A("wq", 0, 512)), ext(T.wc[:, :])), (A("wp", 0, 512), ext(T.ws[:, :]))], "dw")
    dmas("y", [(A("vt", 0, 512), ext(T.v[:, :]))], "dv")

    ROWS = {"two": (0, [([[0, 2], [32, 4], [160, 2]], 0), ([[0, 2], [32, 4], [-128, 2]], 128)]),
            "drop": (1, [([[0, 32]], -LIFT)]),
            "end": (2, [([[0, 2], [32, 4], [160, 2]], 31), ([[0, 2], [32, 4], [-128, 2]], 159)]),
            "h16": (3, [([[16, 2], [0, 16]], 0)]),
            "one": (4, [([[0, 2], [32, 4], [34, 2]], 0), ([[0, 2], [32, 4], [-2, 2]], 2)]),
            "h224": (5, [([[0, 32]], HALF)]),
            "all": (6, [([[0, 16]], 8), ([[32, 4], [-2, 2]], 2), ([[32, 3], [-2, 2]], 6), ([[-2, 2]], 3)]),
            "all2": (7, [([[0, 16]], 8), ([[32, 3], [-2, 2]], 35), ([[32, 3], [-2, 2]], 7), ([[0, 4]], 8)]),
            "pairs": (8, [([[16, 2], [32, 2], [1, 8]], 64 * k) for k in range(2)]),
            "own": (10, [([[16, 2], [32, 8], [256, 2]], 0)]),
            "gap": (11, [([[0, 32]], 0)]),
            "last": (12, [([[32, 8], [-224, 2]], 272), ([[32, 8], [256, 2]], 16)]),
            "gap2": (13, [([[0, 32]], 0)]),
            "mine": (14, [([[32, 8], [-224, 2]], 256), ([[32, 8], [256, 2]], 16)]),
            "gap3": (15, [([[0, 32]], 0)]),
            "wide": (16, [([[0, 2], [64, 4], [320, 2]], 63), ([[0, 2], [64, 4], [-256, 2]], 319)])}

    def rows(names):
        for k in names:
            c0 = 32 * ROWS[k][0]
            for pattern, base in ROWS[k][1]:
                n = 1
                for step, cnt in pattern:
                    n *= cnt
                iota(A("RW", c0, c0 + n), pattern, base)
                c0 += n

    def lst(k, n=1):
        return A("LS", ROWS[k][0], ROWS[k][0] + n)

    def col(k, p0=0, p1=128):
        j = 32 * ROWS[k][0]
        return A("CL", j, j + 1, 1, p0, p1)

    MASKS = {"b0": (0, (7, 14, 0.0), (0, 7, -BIG)), "b1": (1, (0, 7, -TINY)), "b2": (2, (21, 28, 0.0), (14, 21, -BIG)), "b3": (3, (14, 21, -TINY)),
             "c0": (4, (14, 28, 0.0), (0, 14, -BIG)), "c1": (5, (0, 14, -TINY)),
             "p28": (6, (0, 28, 1.0)), "n28": (7, (0, 28, -1.0)), "p24": (8, (0, 24, 1.0)), "n24": (9, (8, 32, -1.0))}

    def mask(k):
        j = MASKS[k][0]
        return A("MK", j, j + 1)

    def zero(name, a, b):
        iota(A(name, a, b), [[0, b - a]], 0)

    for a, b, val in ((0, 16, 0.0), (128, 192, 0.0), (528, 576, 255.0), (576, 592, 0.0), (704, 736, 0.0), (848, 1136, 0.0)):
        fill(A("Z", a, b), val)
    fill(A("R3", 0, 336), 1.0)
    iota(A("ii", 0, 16), [[16, 8], [0, 2]], 0)
    iota(A("one", 0, 516), [[0, 516]], 1)
    rows(("two", "drop", "end", "h16"))
    for b in range(4):
        iota(A("PH", 28 * b, 28 * b + 28), [[4, 7], [0, 2], [1, 2]], 32 * b)
    zero("BQ", QS, 2 * QS)
    for name, a, b in (("T1", 256, 288), ("CS", 256, 288), ("MC", 128, 144), ("DT", 256, 288), ("KEY", 128, 144), ("QC", 0, 8)):
        zero(name, a, b)
    iota(A("DKR", 16, 128), [[-4, 4], [0, 28]], LIFT)
    zero("MR", 192, 320)
    for k in ("p28", "n28", "p24", "n24"):
        j, (a, b, val) = MASKS[k]
        iota(A("MR", 32 * j + a, 32 * j + b), [[0, b - a]], int(val))
    for a, n, val in ((6, 1, -LIFT), (7, 1, -LIFT), (8, 2, -QS)):
        iota(A("MR", 32 * a + 31, 32 * a + 31 + n), [[0, n]], val)
    aff(A("eb", 0, 516), A("one", 0, 516), [[1, 516]], OP.is_equal, 0.0, -3, -4)
    rows(("one", "h224", "all", "all2", "pairs", "own", "gap", "last", "gap2", "mine", "gap3", "wide"))
    for name, a, b in (("CU5", 0, 128), ("C5", 512, 576), ("XH", 96, 128), ("wt6", 0, 520), ("TW", 128, 160), ("ZF", 0, 260), ("W6", QS, 128), ("T6", 0, 256)):
        zero(name, a, b)
    zero("wt7", 0, 536)
    zero("G", 576, 1088)
    never("W7", 0, HALF, -BIG)
    zero("T7", 0, HALF)
    zero("X7", 0, 32)
    iota(A("IOB", 0, C), [[1, C]], -HALF)
    for name, a, b in (("SIG", 0, 16), ("SIG", C, 480), ("TT", 480, 512), ("TT", 992, 1024), ("UW", 0, 896), ("ZT", 896, 1024), ("RN", 0, 16), ("RN", 464, 480),
                       ("RI", 0, 16), ("RI", 464, 480), ("COL", 960, 976), ("COL", 1424, 1440)):
        zero(name, a, b)

    fill(A("MR", 0, 192), BIG)
    fill(A("R3", 0, 336, 3), 0.0)
    cp(A("UL", 0, 16), A("ii", 0, 16))
    for k in ("b0", "b1", "b2", "b3", "c0", "c1"):
        for a, b, val in MASKS[k][1:]:
            fill(A("MR", 32 * MASKS[k][0] + a, 32 * MASKS[k][0] + b), val)
    fill(A("DB", 0, 256), -BIG)
    tr(A("MT", 0, 192), A("MR", 0, 192))
    fill(A("D3", 0, 256), BIG)
    cp(A("MK", 0, 6), A("MT", 0, 192, 32))
    const("DR", 0, 512, BIG)
    const("PR", 0, 2 * QS, -BIG)
    const("CUR", 0, 416, 0.0)
    for a, b in ((0, 384), (7, 128), (14, 256), (21, 128)):
        const("DR", a, b, -BIG, 32)

    todo = []

    def later(ns, f, *args):
        todo.append((ns, lambda: f(*args)))

    def first(ns=150):
        while todo and todo[0][0] <= ns:
            ns -= max(todo[0][0], 1)
            todo.pop(0)[1]()

    def until(mark):
        while any(x[0] == mark for x in todo):
            todo.pop(0)[1]()

    for j in range(2):
        later(60, ts, A("MP3", 7 + 14 * j, 21 + 14 * j), A("one", 0, 14), mask("c%d" % j), OP.mult)
    later(60, cp, A("MP3", 39, 67), A("MP3", 7, 35))
    later(60, tr, A("DT", 0, 128), A("DKR", 16, 144))
    later(60, tr, A("DT", 128, 256), A("DKR", 0, 128))
    later(60, cp, A("MP3", 71, 131), A("MP3", 7, 67))
    later(-3, lambda: None)
    later(60, tr, A("MT", 192, 320), A("MR", 192, 320))
    later(60, ts, A("CK", 0, 8), A("DT", 0, 256, 32), -14.0, OP.add)
    later(60, cp, A("MK", 6, 10), A("MT", 192, 320, 32))
    for name, a, b, val, st in (("CUR", 286 + 31, 416, BIG, 64), ("CUR", 286 + 63, 416, -BIG, 64), ("DR", 256 + 63, 384, -BIG, 64),
                                ("DR", 384, 496, -BIG, 56), ("K5", 0, 8, BIG, 1), ("K5", 120, 128, -BIG, 1)):
        later(60, fill, A(name, a, b, st), val)
    later(60, fill, AQ("QC", 2, 0, 1, 1, 2), float(QS))
    for h in range(2):
        later(60, fill, AQ("QC", 2 * h, 2, 3, 1, 2), -1.0 if h else 1.0)
        later(60, fill, AQ("K6", 2 * h, QS, 128, 1, 2), BIG if h else -BIG)
    for b in range(4):
        later(140, quant, A("qe", 128 * b, 128 * b + 128), A("se", 128 * b, 128 * b + 128), A("eb", 3 - b, 515 - b))
    for c0 in range(128, 544, 128):
        later(120, tr, A("CL", c0, min(c0 + 128, 544)), A("RW", c0, min(c0 + 128, 544)))
    later(60, cp, A("LS", 4, 17), A("CL", 128, 544, 32))
    for a in (1, 3):
        later(60, fill, AQ("QC", a, 4, 5), float(HALF))

    def weights(lev):
        if lev == 6:
            for a in range(4):
                later(60, fill, AQ("wt6", a, 8 + 128 * a, 12 + 128 * a), 1.0 if a < 2 else -1.0)
            later(140, quant, A("qa", 0, 128), A("sa", 0, 128), A("G", 0, 512))
            later(140, quant, A("q6", 0, 130), A("s6", 0, 130), A("wt6", 0, 520))
            later(140, quant, A("qv", 0, 128), A("pv", 0, 128), A("vt", 0, 512))
            return
        for a in range(4):
            later(60, fill, AQ("QC", a, 6, 7), -1.0 if a % 2 else 1.0)
        for a in range(2):
            later(60, fill, AQ("QC", a, 7, 8), 1.0 if a else -1.0)
        for a in range(4):
            later(60, fill, AQ("wt7", a, 408 + 4 * (a % 2), 412 + 4 * (a % 2) - a // 2), -1.0 if a % 2 else 1.0)
        later(140, quant, A("q7", 0, 134), A("s7", 0, 134), A("wt7", 0, 536))

    quant(A("qu", 0, 128), A("su", 0, 128), A("ut", 0, 512))
    for j in range(4):
        ts(A("MP", 7 * j, 7 * j + 7), A("one", 0, 7), mask("b%d" % j), OP.mult)
    pick("qB", "sB", (0, 128), "qu", "su", 128, A("UL", 0, 8))

    LB = 4
    DBANK = [6, 7, 3, 2]
    BLK = [1, 2, 7, 14, 28, 56, 112, 224]

    def turn2(out, row):
        tr(A(out, 0, 128), A(row, 16, 144))
        tr(A(out, 128, 256), A(row, 0, 128))

    def sums(lev):
        first()
        if lev < 5:
            turn2("TB", "MB")
            first()
            for c0 in (0, 128):
                if lev == 3:
                    scan(back("CS", c0, c0 + 128), back("D3", c0, c0 + 128), back("TB", c0, c0 + 128), BIG, OP.min, OP.add)
                else:
                    scan(A("CS", c0, c0 + 128), A("DB", c0, c0 + 128), A("TB", c0, c0 + 128), -BIG, OP.max, OP.add)
            new = ind(A("CS", 0, 288), lst("two" if lev == 3 else "end"))
            first()
            cp(A("LL", 0, 16), new)
        else:
            for i, row in enumerate(("MB", "MB1")):
                for c0, r0 in ((0, 16), (256, 0)):
                    tr(A("TB", c0 + i, c0 + 256, 2), A(row, r0, r0 + 128))
            for c0 in (0, 256):
                scan(A("C5", c0, c0 + 256), A("D5", c0, c0 + 256), A("TB", c0, c0 + 256), -BIG, OP.max, OP.add)
            new = ind(A("C5", 0, 576), lst("wide"))
            first()
            cp(A("LL", 0, 16), new)
            act(A("XB", 16, 32), new, bias=A("QC", 0, 1))
        if lev == 2:
            until(-3)
            act(A("MKL", 0, QS), ind(A("MP3", 0, 144), A("LL", 0, 7)))
            ts(A("D3", 31, 256, 32), A("CS", 31, 256, 32), -7.0, OP.add)
        if lev == 3:
            tt(A("DB", 0, 256, 32), A("CS", 0, 256, 32), A("CK", 0, 8), OP.add)
        if lev == 4:
            ts(A("D5", 0, 512, 64), A("CS", 31, 256, 32), float(QS), OP.add)
        act(A("XH", 16 * lev, 16 * lev + 16), new, bias=-float(BLK[lev]) if lev < 4 else 0.0)

    def counts(lev):
        for c0 in (16, 144) if lev == 7 else (16,):
            quant(A("qa", c0, c0 + 128), A("sa", c0, c0 + 128), A("G", 4 * c0, 4 * c0 + 512))
        views = (("q7", "s7", 6, 16), ("q7", "s7", 4, 0), ("q7", "s7", 2, 144), ("q7", "s7", 0, 128)) if lev == 7 else (("q6", "s6", 2, 16), ("q6", "s6", 0, 0))
        for i, (w, ws, a, b) in enumerate(views):
            mm(ps(LB, 0, 128), A(w, a, a + 128), A(ws, a, a + 128), A("qa", b, b + 128), A("sa", b, b + 128), i == 0, i == len(views) - 1)

    def turn(row, c0, halves=(0, 1)):
        for i in halves:
            tr(A("TT", 512 * i, 512 * i + 256), A(row, c0 + HALF * i, c0 + HALF * i + 256))
            tr(A("TT", 512 * i + 256, 512 * i + 480), A(row, c0 + HALF * i + 16, c0 + HALF * i + 240))

    def fetch(dst, k, add, halves=(0, 1), step=14):
        for i in halves:
            ts(A(dst, step * i, step * i + 16), ind(A("TT", 512 * i, 512 * i + 512), lst(k)), float(add), OP.add)

    def turn_fetch(row, dst, k, step=14):
        turn(row, 0, (0,))
        tr(A("TT", 512, 768), A(row, HALF, HALF + 256))
        fetch(dst, k, HALF, (0,), step)
        tr(A("TT", 768, 992), A(row, HALF + 16, HALF + 240))

    def slots(c0, c1):
        scatter(A("RI", 0, 480), A("R2", c0, c1), A("IOB", 16 * c0, 16 * c1))

    def lane(t, a, b):
        return A("G", 64 + 4 * a + t, 64 + 4 * b, 4)

    dst = T.cores[(rank + 1) % len(T.cores)]
    rel = _relays(topo, core, dst)
    eng = topo.engines(core, rel[0])
    landed = 2 * len(topo.engines(_relays(topo, T.cores[rank - 1], core)[0], core))

    for t in range(ROUNDS):
        last = t == ROUNDS - 1
        qx, sx = "qx%d" % t, "sx%d" % t
        qp, sp = (qx, sx) if t else ("qp0", "sp0")
        for i in range(2):
            quant(A(qx, HALF * i, HALF * i + HALF), A(sx, HALF * i, HALF * i + HALF), A("xn" if t else "xt", 896 * i, 896 * i + 896))
        if t == 0:
            for a in range(4):
                cp(AQ("PL", a, 0, 28), AQ("pi", 0, 0, 28))
            tr(A("CL", 0, 128), A("RW", 0, 128))
            cp(A("MP", 32, 64), A("MP", 0, 32))
        for i in range(2):
            o = (HALF * i, HALF * i + HALF)
            if t == 0:
                pick(qp, sp, o, qx, sx, C, A("PL", 14 * i, 14 * i + 14))
            for k in range(2):
                c0 = HALF * i + 96 * k
                mm(ps(2 * i + k, 0, 128), A("qB", 0, 128), A("sB", 0, 128), A(qp, c0, c0 + 128), A(sp, c0, c0 + 128))
        if t == 0:
            pick("qB", "sB", (128, 256), "qu", "su", 128, A("UL", 8, 16))
        mm(ps(5, 0, C), A("qB", 128, 256), A("sB", 128, 256), A(qp, 0, C), A(sp, 0, C))

        def scores(h, blocks=range(4), by=act):
            p = (32 * (h % 4), 32 * (h % 4) + 32)
            for k in blocks:
                a = BLOCK[k]
                bank, c0 = k, 16 * (k % 2)
                if h == 1:
                    by(A("BQ", QS, 2 * QS, 1, 32 * a, 32 * a + 16), ps(bank, c0, c0 + QS, 1, 32, 48))
                elif h < 4:
                    by(AQ("BQ", a, QS * h, QS * h + QS), ps(bank, c0, c0 + QS, 1, *p))
                else:
                    by(AQ("BQ", a, QS * h, QS * h + QS), ps(5, QS * k, QS * k + QS, 1, *p))

        def halves(b):
            mm(ps(DBANK[b], 0, C), A("qe", 128 * b, 128 * b + 128), A("se", 128 * b, 128 * b + 128), A(qp, 0, C), A(sp, 0, C))
            act(A("HB", C * b, C * b + C), ps(DBANK[b], 0, C), 0.5)

        if last:
            for i in range(2):
                for c0, c1, r0 in ((0, 256, 0), (256, 480, 16)):
                    r0 += 480 * t + HALF * i
                    later(110, tr, A("TT", 512 * i + c0, 512 * i + c1), A("COL", r0, r0 + c1 - c0))
            for i in range(2):
                later(130, fetch, "R2", "last", HALF + 16, (i,))
        done = [0 if last else 28]

        def spare(n):
            if done[0] < 28:
                first(1000)
                slots(done[0], min(28, done[0] + n))
                done[0] += n

        first(250 if t else 0)
        if t == 0:
            cp(A("LS", 0, 4), A("CL", 0, 128, 32))
            cp(A("MP", 64, 128), A("MP", 0, 64))
        scores(0, (0, 2), cp)
        scores(0, (1, 3))
        scores(1, (1, 3))
        scores(1, (0,), cp)
        now = A("COL", 480 * t + 16, 480 * t + 16 + C)

        def background(lev):
            if lev == 2:
                scores(3)
                scores(4)
            if lev == 3:
                scores(5)
                if t == 0:
                    const("D5", 0, 512, -BIG)
                    const("G", 0, 576, 0.0)
            if lev == 4:
                scores(6)
                if t:
                    const("W7", 0, HALF, -BIG)
            if lev == 5:
                if t == 0:
                    act(A("QC", 1, 2), col("h16"), bias=A("QC", 0, 1))
                    act(A("QC", 3, 4), A("QC", 1, 2), bias=A("QC", 4, 5))
                    act(A("QC", 5, 6), A("QC", 3, 4), bias=col("drop"))
                    for m in range(2):
                        act(A("OFS", 8 * m, 8 * m + 16), ind(A("DT", 0, 288), lst("two")), bias=A("QC", 5, 6))
                    act(A("OFS", 16, 32), A("ZF", 0, 16), bias=A("QC", 3, 4))
                else:
                    scores(7)
            if lev == 6:
                if t == 0:
                    scores(7)
                for b in range(2 if t == 0 else 3):
                    halves(b)
                for m in range(3):
                    for a in range(4):
                        later(60, cp, AQ("RL", m, 7 * BLOCK[a], 7 * BLOCK[a] + 7), AQ("Y", a, 8 * m, 8 * m + 7))
            if lev == 7:
                for b in range(2 if t == 0 else 3, 4):
                    halves(b)
                if t == 0:
                    act(now, ind(A("IOB", 0, C), A("PL", 0, 28)))

        V = lambda n: A("TMP", 56 * n, 56 * n + 56)
        s0 = [A("BQ", i, QS, 2) for i in range(2)]
        tt(V(0), s0[1], s0[0], OP.is_lt)
        scores(1, (2,), cp)
        scores(2)
        ts(A("PR", 0, QS, 2), V(0), 2 * BIG, OP.mult, -BIG, OP.add)
        ts(A("PR", QS + 1, 2 * QS, 2), V(0), -2 * BIG, OP.mult, BIG, OP.add)
        tt(A("G3", 0, 336, 6), A("PH", 0, QS, 2), V(0), OP.add)
        tt(A("G3", 3, 336, 6), A("PH", 1, QS, 2), V(0), OP.subtract)
        scan(back("TMP", QS, 2 * QS), back("PR", 0, QS), back("BQ", QS, 2 * QS))
        scan(A("TMP", 2 * QS, 3 * QS), A("PR", QS, 2 * QS), A("BQ", QS, 2 * QS))
        first()
        key = lambda i: A("TMP", QS * (1 + i % 2) + i, QS * (2 + i % 2), 4)
        for i, j in ((0, 2), (2, 0), (0, 3), (2, 1), (1, 2), (3, 0), (1, 3), (3, 1)):
            tt(A("G3", 3 * i + 1 + j % 2, 336, 12), key(i), key(j), OP.is_gt if i < 2 else OP.is_ge)
        first()
        scan(A("GR", 48, 384), A("R3", 0, 336), A("G3", 0, 336), 0.0, OP.mult, OP.add)
        first()
        tr(A("T1", 0, 128), A("GR", 50, 432, 3))
        tr(A("T1", 128, 256), A("GR", 2, 384, 3))
        first(120)
        cp(A("LL", 0, 16), ind(A("T1", 0, 288), lst("two")))
        cp(A("DB", 0, 256, 32), A("T1", 0, 256, 32))
        first(60)
        act(A("MKL", 0, QS), ind(A("MP", 0, 128), A("LL", 0, 7)))
        act(A("XH", 16, 32), ind(A("T1", 0, 288), lst("two")))
        act(A("XH", 0, 16), ind(A("T1", 16, 288), lst("two")))

        for lev in range(2, 6):
            w = BLK[lev]
            if t == 0 and lev == 5:
                weights(6)
            n, cur, c0, up = ((128, "CUR", 0, 0), (128, "CUR", 128, 7), (128, "CUR", 272, 14), (QS, "CU5", 0, 0))[lev - 2]
            key = A("K5", 8, 120) if lev == 5 else A("KEY", up * (lev == 4), 128 + up * (lev == 4))
            scatter(A(cur, c0, c0 + (128 if lev in (2, 5) else 144)), A("LL", 0, 7), A("BQ", QS * lev, QS * lev + QS))
            first()
            if lev > 2:
                spare(2)
            one = lambda b: A("TQ", 32 * b, 32 * b + 1)
            if lev > 3:
                scan(key, A("DR", 128 * (lev - 2), 128 * (lev - 2) + n), A(cur, c0 + up, c0 + up + n))
                act(A("KS", 0, QS), ind(key if lev == 5 else A("KEY", 0, 144), A("LL", 0, 7)))
                first()
                tr(A("TQ", 0, 128), A("K5", 0, 128) if lev == 5 else key)
                first(260)
                spare(4)
            if lev < 4:
                for a in (0, 64):
                    scan(A("KEY", a, a + 64), A("DR", 128 * (lev - 2) + a, 128 * (lev - 2) + a + 64), A(cur, c0 + up + a, c0 + up + a + 64))
                first(100)
                for a in (0, 64):
                    tr(A("TQ", a, a + 64), A("KEY", a, a + 64))
                first(100)
                for a in (0, 64):
                    tt(A("MC", up + a, up + a + 64), A("KEY", a, a + 64), A("TQ", a, a + 64), OP.subtract)
                first()
                tt(A("MB", 16, 128), ind(A("MC", 0, 144), A("LL", 0, 7)), A("MKL", 0, QS), OP.is_gt)
                spare(2)
            elif lev == 4:
                for b in range(4):
                    ts(A("MB", 16 + w * b, 16 + w * b + w), A("KS", w * b, w * b + w), one(b ^ 1), OP.is_lt if b % 2 else OP.is_gt, mask("n28" if b % 2 else "p28"), OP.mult)
            else:
                ts(A("MB", 16, 16 + w), A("KS", 0, w), one(2), OP.is_gt)
                ts(A("MB", 16 + w, 128), A("KS", w, QS), one(0), OP.is_lt, mask("n24"), OP.mult)
                ts(A("MB1", 16, 16 + w), A("KS", 0, w), one(3), OP.is_gt, mask("p24"), OP.mult)
                ts(A("MB1", 16 + w, 128), A("KS", w, QS), one(1), OP.is_lt, -1.0, OP.mult)
            background(lev)
            sums(lev)

        scatter(A("W6", 0, 128), A("LL", 0, 7), A("BQ", QS * 6, QS * 7))
        if t == 0:
            weights(7)
        first()
        spare(2)
        scan(A("K6", 0, QS), A("W6", 0, QS), A("W6", 0, QS), -BIG, OP.max, OP.max)
        act(A("KS", 0, QS), ind(A("K6", 0, 128), A("LL", 0, 7)), A("QC", 2, 3))
        tt(A("Y", 0, 32), ind(A("XH", 0, 128), lst("pairs", 2)), A("OFS", 0, 32), OP.add)
        for h in range(2):
            tr(AQ("T6", 2 * h, 128 * h, 128 * h + 128, 1, 2), AQ("K6", 2 - 2 * h, 0, 128, 1, 2))
        background(6)
        first()
        for b in range(4):
            ts(lane(b, 0, QS), A("KS", 0, QS), A("T6", 128 + 32 * b, 129 + 32 * b), OP.add, A("T6", 32 * b, 32 * b + 1), OP.is_gt)
        first()
        counts(6)
        if last:
            slots(done[0], 28)
        else:
            first(400)
        tr(A("TW", 0, 128), ps(LB, 0, 128))
        first()
        tt(A("XH", 96, 112), ind(A("TW", 0, 160), lst("one")), A("XB", 16, 32), OP.add)
        first()

        cp(A("LL", 0, 8), A("XH", 96, 104))
        for k in range(4):
            if k == 3:
                scatter(A("W7", 0, HALF), A("LL", 0, 7), A("BQ", QS * 7, QS * 8))
            cp(AQ("LG", 2 * (k % 2), 7 * (k // 2), 7 * (k // 2) + 7, 1, 2), AQ("XH", 2 * (k // 2), 96, 103, 1, 2))
        first(100)
        for d in range(2):
            scan(AQ("K7", 2 * d, 0, HALF, 1, 2), AQ("W7", 0, 0, HALF, 1, 2), AQ("W7", 2, 0, HALF, 1, 2), -BIG, OP.max, OP.max)
        parts = ((0, 128), (128, HALF))
        for a, b in parts:
            act(A("KS", a, b), ind(A("K7", 0, HALF), A("LG", a // 16, b // 16)), A("QC", 6, 7))
        for a, c0, k0, n in ((0, 0, 0, 128), (1, 96, 0, 128), (2, 0, 128, 96), (3, 128, 128, 96)):
            tr(AQ("T7", a, c0, c0 + n), AQ("K7", 1 - a % 2, k0, k0 + n))
        first()
        flip = AQ("QC", 0, 7, 8, 1, 2)
        for a, b in parts:
            act(AQ("SG", 0, a, b, 1, 2), AQ("KS", 0, a, b, 1, 2), flip, AQ("T7", 0, 96, 97, 1, 2), AF.Sign)
        for a, b in parts:
            act(AQ("G", 0, 67 + 4 * a, 64 + 4 * b, 4, 2), AQ("SG", 0, a, b, 1, 2), flip, func=AF.Relu)
        for a, b in parts:
            for k in range(3):
                ts(lane(k, a, b), A("KS", a, b), A("T7", 128 + 32 * k, 129 + 32 * k), OP.add, A("T7", 32 * k, 32 * k + 1), OP.is_gt)
        first()
        counts(7)
        for a in range(4):
            ts(AQ("X7", 3, 7 * BLOCK[a], 7 * BLOCK[a] + 7), AQ("XH", a, 96, 103), col("h16", 96, 128), OP.add, float(HALF * (a % 2)), OP.add)
        if last:
            turn("RI", 0)
        first(10000)
        background(7)
        tr(AQ("TW", 3, 0, 128), ps(LB, 0, 128, 1, 96, 128))
        if last:
            fetch("IC", "last", HALF, (0,))
        tt(A("XF", 0, 32), ind(A("TW", 0, 160), lst("all", 2)), A("X7", 0, 32), OP.add)
        if last:
            fetch("IC", "last", HALF, (1,))
        cp(AQ("RL", 3, 0, 28), AQ("XF", 3, 0, 28))

        scatter(A("SIG", 0, 480), A("RL", 0, 28), A("IOB", 0, C))
        for i in (0, 16):
            ts(A("UW", i, 896, 32), A("RL", 0, 28), col("h16"), OP.subtract, float(HALF), OP.subtract)
        turn_fetch("SIG", "ZL", "own", 16)
        if not last:
            fetch("PL", "last", HALF, (0,))
        fetch("ZL", "own", HALF, (1,), 16)
        if not last:
            fetch("PL", "last", HALF, (1,))

        zc, zs = "zc%d" % t, "zs%d" % t
        for a, b in PIECES:
            for k in range(4):
                act(A("GZ", HALF * k + a, HALF * k + b), ind(A("HB", C * k, C * k + C), A("ZL", a // 16, b // 16)))

        def pair(i, k):
            a, b = PIECES[i]
            tt(A("ZT", 4 * a + k, 4 * b, 4), ind(A("HB", C * k, C * k + C), A("ZL", 16 + a // 16, 16 + b // 16)), A("GZ", HALF * k + a, HALF * k + b), OP.add)

        def send(i):
            a, b = PIECES[i]
            quant(A(zc, a, a + 128), A(zs, a, a + 128), A("ZT", 4 * a, 4 * a + 512))
            hazards("g", A(zc, a, b)[1], [])
            sem = T.sem["r%s%d" % ("ab"[i], t)]
            rid, pid = topo.addr(rel[i], core)
            g.remote_dma(T["hc%d" % t][:, a:b].bitcast(dt.uint8), T[zc][:, a:b].bitcast(dt.uint8), sem, T.sem.snd, pid, rid, topo.mask(core, rel[i]))
            rid, pid = topo.addr(rel[2 + i], core)
            g.remote_dma(T["hs%d" % t][:, a:b], T[zs][:, a:b], sem, T.sem.snd, pid, rid, topo.mask(core, rel[2 + i]))

        nxt = "IC" if last else "PL"
        pair(0, 0)
        if not last:
            for k in range(3):
                cp(AQ("PL", k, 0, 28), AQ("PL", 3, 0, 28))
        pair(0, 1)
        pair(0, 2)
        cp(A("NI", 0, 28), A(nxt, 0, 28))
        pair(0, 3)
        pair(1, 0)
        ts(A("NA", 0, 28), A("NI", 0, 28), 496, OP.bitwise_and)
        send(0)
        pair(1, 1)
        tt(A("NS", 0, 28), A("NI", 0, 28), A("NA", 0, 28), OP.add)
        pair(1, 2)
        pair(1, 3)
        ts(A("NL", 0, 28), A("NS", 0, 28), col("h16"), OP.add)
        tr(A("UT", 0, C), A("UW", 0, C))
        send(1)

        act(A("FB", 0, C), ind(A("HB", 0, C), A(nxt, 0, 28)), 2.0)
        tr(A("UT", C, 896), A("UW", C, 896))
        for a, b in ((0, 16), (16, 28)):
            act(A("RN", 16 + 16 * a, 16 + 16 * b), ind(A("UT", 0, 896), A("NL", a, b)))
        for b in (2, 3):
            ts(A("FK", C * (b - 2), C * (b - 2) + HALF), A("GZ", HALF * b, HALF * b + HALF), 64.0, OP.mult)
        ts(A("FK", HALF, C), ind(A("HB", 2 * C, 3 * C), A("ZL", 16, 30)), 64.0, OP.mult)
        act(A("FK", C + HALF, 2 * C), ind(A("HB", 3 * C, 4 * C), A("ZL", 16, 30)), 64.0)
        act(A("FB", C, 2 * C), ind(A("HB", C, 2 * C), A(nxt, 0, 28)), 2.0)
        if not last:
            act(A("COL", 480 * t + 496, 480 * t + 496 + C), ind(now, A("PL", 0, 28)))
        turn_fetch("RN", "CA", "mine")
        fetch("CA", "mine", HALF, (1,))
        ts(A("CT", 0, 28), A("CA", 0, 28), float(HALF), OP.is_ge, -float(HALF), OP.mult)
        cp(A("RK", 0, 28), A("CA", 0, 28))

        lc, ls = "lc%d" % t, "ls%d" % t
        for i, (a, b) in enumerate(PIECES):
            wait("t", "l%s%d" % ("ab"[i], t), landed)
            for k in (2, 0, 3, 1):
                bank = 4 * i + k
                mm(ps(bank, 0, 128), A("wq", 128 * k, 128 * k + 128), A("wp", 128 * k, 128 * k + 128), A(lc, b - 128, b), A(ls, b - 128, b))
                got = ps(bank, 128 - (b - a), 128)
                if k < 2:
                    act(A("PB", HALF * k + a, HALF * k + b), got, 0.03125)
                else:
                    for c0 in (C * (k - 2), C * (k - 2) + HALF):
                        tt(A("PK", c0 + a, c0 + b), got, A("FK", c0 + a, c0 + b), OP.add)
                    if i == 0 and k == 2:
                        tt(A("NS", 0, 28), A("CA", 0, 28), A("CT", 0, 28), OP.add)
                    if i == 0 and k == 3:
                        cp(A("RM", 0, 28), A("NS", 0, 28))
        act(A("xn", 2, 1792, 4), ind(A("PK", 0, C), A("RK", 0, 28)), 0.03125)
        for i in range(2):
            act(A("xn", 896 * i + 3, 896 * i + 896, 4), ind(A("PK", C, 2 * C), A("RK", 14 * i, 14 * i + 14)), 0.03125)
        tt(A("xn", 0, 1792, 4), ind(A("PB", 0, HALF), A("RM", 0, 28)), A("FB", 0, C), OP.add)
        for i in range(2):
            tt(A("xn", 896 * i + 1, 896 * i + 896, 4), ind(A("PB", HALF, C), A("RM", 14 * i, 14 * i + 14)), A("FB", C + HALF * i, C + HALF * i + HALF), OP.add)

    for i in range(2):
        o = (HALF * i, HALF * i + HALF)
        quant(A("qx3", *o), A("sx3", *o), A("xn", 896 * i, 896 * i + 896))
        mm(ps(i, 0, HALF), A("qv", 0, 128), A("pv", 0, 128), A("qx3", *o), A("sx3", *o))
        dmas("y", [(ext(T.oc[:, 896 * i:896 * i + 896]), bc(A("qx3", *o)))], "dc%d" % i)
    for i in range(2):
        act(A("OD", HALF * i, HALF * i + HALF), ind(now, A("ZL", 16 * i, 16 * i + 14)), bias=col("h224"))
        cp(A("yb", HALF * i, HALF * i + HALF), ps(i, 0, HALF))
        dmas("y", [(ext(T.y[:, HALF * i:HALF * i + HALF]), A("yb", HALF * i, HALF * i + HALF))], "dy%d" % i)
    dmas("s", [(ext(T.od[:, :]), (T.OD[0:128:16, :], A("OD", 0, C)[1]))], "dd")
    dmas("s", [(ext(T.osc[4 * k:4 * k + 4, :]), A("sx3", 0, C, 1, 32 * k, 32 * k + 4)) for k in range(4)], "dq")
    for sem in count:
        wait("g", sem, count[sem])
    wait("g", "snd", 4 * len(eng) * ROUNDS)
